import numpy as np, ml_dtypes
CORES = [3,11,19,27,35,43]
N = 6
BF = ml_dtypes.bfloat16
def gentries(a):
    return np.ascontiguousarray(a.reshape(8, 16, -1).transpose(0, 2, 1)).reshape(8, -1)
def gtable(e):
    e = np.asarray(e); return np.ascontiguousarray(e.reshape(8, -1, 16).transpose(0, 2, 1)).reshape(128, -1).astype(np.int32)
K, C, NS, RO = 160, 4, 1024, 6
V, W = C * K, N * C * K
def parts(rng):
    lev = rng.integers(0, 160, (N, 8, 1, W)); b = lev + ((256 - lev) * rng.random((N, 8, 16, W))).astype(np.int64)
    L = rng.integers(0, W, (N, 8, 16, NS)); S = rng.integers(0, W, (N, 8, 16, V))
    P = np.argsort(rng.random((N, 8, C, NS)), axis=-1)[..., :K].reshape(N, 8, V); Q = rng.integers(0, NS, (N, 8, V))
    return np.minimum(b, 255), L, S, P, Q, rng.integers(400, 2000, (N, 8, 16, 1)), rng.integers(1600, 2900, (N, 8, 1))
def pack(b, L, S, P, Q, th, mg):
    return {"base": np.ascontiguousarray(b.reshape(N, 128, W)).astype(np.float32).astype(BF), "favor": np.ascontiguousarray(L.reshape(N, 128, NS)).astype(np.int32),
            "src": np.ascontiguousarray(S.reshape(N, 128, V)).astype(np.int32), "grant": np.stack([gtable(a) for a in P]), "part": np.stack([gtable(a) for a in Q]),
            "th": np.ascontiguousarray(th.reshape(N, 128, 1)).astype(np.int32), "mg": mg.astype(np.int32)}
def setup_inputs(rng):
    return pack(*parts(rng))
def setup_inputs_spread(rng):
    b, L, S, P, Q, th, mg = parts(rng)
    b = np.minimum((256 * rng.random((N, 8, 16, W)) * np.exp2(-rng.integers(0, 8, (N, 8, 1, W)).astype(np.float64))).astype(np.int64), 255)
    L = np.minimum((W * rng.random(L.shape) ** 3).astype(np.int64), W - 1); S = np.minimum((W * rng.random(S.shape) ** 2).astype(np.int64), W - 1)
    Q = np.minimum((NS * rng.random(Q.shape) ** 3).astype(np.int64), NS - 1)
    th = np.minimum(np.exp2(12 * rng.random(th.shape)).astype(np.int64) - 1, 4079); mg = np.minimum(np.exp2(12 * rng.random(mg.shape)).astype(np.int64) - 1, 4079)
    return pack(b, L, S, P, Q, th, mg)
def setup_inputs_ends(rng):
    b, L, S, P, Q, th, mg = parts(rng)
    def tip(x, lo, hi, share):
        m = rng.random(x.shape); return np.where(m < 0.5 * share, lo, np.where(m < share, hi, x))
    sort_ = rng.integers(0, 5, (N, 8, 1, W)); el = 255 * rng.integers(0, 2, b.shape)
    b = np.where(sort_ == 0, 0, np.where(sort_ == 1, 255, np.where(sort_ < 4, el, tip(b, 0, 255, 0.5))))
    L = tip(L, 0, W - 1, 0.7); S = tip(S, 0, W - 1, 0.7); Q = tip(Q, 0, NS - 1, 0.8)
    ix = np.concatenate([np.arange(K // 2), np.arange(NS - K // 2, NS)]); P = rng.permuted(np.tile(ix, (N, 8, C, 1)), axis=-1).reshape(N, 8, V)
    th = tip(th, 0, 4079, 1.0); th[:, :, 15] = 4079; th[:, :, 0] = 0
    for r in range(N):
        last = 4079 if (N - 1 - r) % 2 == 0 else 0
        mg[r, :7, 0] = rng.permutation(np.array([0, 0, 0, 4079, 4079, 4079, 4079 - last])); mg[r, 7, 0] = last
    zero = rng.random((N, 8)) < 0.7; zero[:, 7] = True
    b[..., W - 1] = np.where(zero[:, :, None], 0, b[..., W - 1])
    hi = np.array([0, K + 1, K - 2, 2 * K - 1, V - 1, V - 2 - K]); lo = np.array([K, 1, 2 * K - 2, K - 1, V - 2, V - 1 - K])
    b[:, :, :, hi] = 255; b[:, :, :, lo] = 0; S[:, :, 15, hi] = W - 1; S[:, :, 15, lo] = 0
    np.put_along_axis(L[:, :, 15], P[:, :, hi], W - 1, 2)
    return pack(b, L, S, P, Q, th, mg)
def setup_inputs_corners(rng):
    b, L, S, P, Q, th, mg = parts(rng); e = np.arange(V); rev = (e // K ^ 1) * K + e % K
    for r in range(N):
        for g, k in enumerate(rng.permutation(8)):
            if k == 0: S[r, g] = e
            if k == 1:
                L[r, g] = rng.integers(0, W, (1, NS)); S[r, g] = rng.choice(np.array([0, V - 1, V, W - 1]), (16, V)); Q[r, g] = rng.choice(np.array([0, NS - 1]), V)
            if k == 2:
                b[r, g] = rng.integers(0, 4, (16, W)); th[r, g, :, 0] = rng.integers(0, 41, 16); mg[r, g, 0] = rng.integers(0, 21)
            if k == 3:
                Q[r, g] = P[r, g]; S[r, g] = rev; mg[r, g, 0] = rng.integers(0, 600)
                for c in range(C):
                    a = e[c * K:(c + 1) * K]; L[r, g][:, P[r, g, a]] = np.where(rng.random((16, K)) < 0.5, a, rev[a])
            if k == 4:
                L[r, g] = rng.integers(V, W, (16, NS)); S[r, g] = rng.integers(V, W, (16, V)); th[r, g] = 4079; mg[r, g] = 4079
            if k == 5: th[r, g] = 0; mg[r, g] = 0
            if k == 6:
                b[r, g] = 255 * rng.integers(0, 2, (16, W)); L[r, g, 8:] = L[r, g, :8]; th[r, g, :, 0] = 255 * rng.integers(0, 16, 16); mg[r, g, 0] = 255 * rng.integers(0, 9)
            if k == 7:
                b[r, g] = 8 * rng.integers(0, 32, (1, W)); th[r, g, :, 0] = 128 * rng.integers(1, 20, 16); mg[r, g, 0] = 128 * rng.integers(4, 14)
    return pack(b, L, S, P, Q, th, mg)
def setup_inputs_crowd(rng):
    b, L, S, P, Q, th, mg = parts(rng); z = (1 + (RO - 1) % (N - 1)) * V + ((RO - 1) % C) * K
    s = 490 + np.arange(64); low = (s // 16)[None, :] + (np.arange(16)[:, None] < (s % 16)[None, :]).astype(np.int64)
    for r in range(N):
        for g, k in enumerate(rng.permutation(8) % 4):
            if k == 3: continue
            b[r, g, :, :V] = rng.integers(200, 256, (16, V)); b[r, g, :, z:z + 64] = low; b[r, g, :, z + 64:z + K] = 0
            L[r, g] = z + K - 1 if k == 2 else rng.integers(z + 64, z + K, (16, NS))
            if k == 2: Q[r, g] = rng.integers(0, NS)
            c0 = (1, 0, C - 1)[k]; a = int(rng.integers(0, K)) + K * np.arange(c0, C)
            b[r, g][:, a] = 0; S[r, g][:, a] = z + rng.integers(0, 64, (16, C - c0))
            th[r, g, :, 0] = rng.integers(480, 521, 16); mg[r, g, 0] = rng.choice(np.array([0, 1, 3199]))
    return pack(b, L, S, P, Q, th, mg)
def check_inputs(d):
    bad = []; x = np.asarray(d["base"]).astype(np.float32)
    if not np.all((x >= 0) & (x <= 255) & (x == np.floor(x))): bad.append("range of base")
    for k, lo, hi in (("favor", 0, W - 1), ("src", 0, W - 1), ("grant", 0, NS - 1), ("part", 0, NS - 1), ("th", 0, 4079), ("mg", 0, 4079)):
        if np.min(d[k]) < lo or np.max(d[k]) > hi: bad.append("range of " + k)
    p = np.sort(np.stack([gentries(a) for a in d["grant"]]).astype(np.int64).reshape(N, 8, C, K), axis=-1)
    if np.any(p[..., 1:] == p[..., :-1]): bad.append("grantors of a class differ")
    return bad
def reference(base, favor, src, grant, part, th, mg):
    b = base.astype(np.float32).astype(np.int64).reshape(N, 8, 16, W); X = b + 0
    L = favor.astype(np.int64).reshape(N, 8, 16, NS); S = src.astype(np.int64).reshape(N, 8, 16, V)
    P = np.stack([gentries(a) for a in grant]).astype(np.int64); Q = np.stack([gentries(a) for a in part]).astype(np.int64)
    lim = th.astype(np.int64).reshape(N, 8, 16, 1); gap = mg.astype(np.int64).reshape(N, 8, 1); A = np.zeros((N, 8), np.int64); lane = np.arange(K)
    for t in range(RO):
        c = t % C; o = c * K; v = (c ^ 1) * K; e = o + lane; be = b[..., o:o + K]; old = X[..., o:o + K] + 0; s = S[..., o:o + K] + 0
        far = np.take_along_axis(X, s.reshape(N, 8, 1, 16 * K), 3).reshape(N, 8, 16, 16, K)
        dist = np.sum(np.abs(far - old[:, :, :, None, :]), axis=2)
        lapse = dist > lim + (A & 31)[:, :, None, None]
        x = np.where(lapse, be, old); s = np.where(lapse, e, s)
        pe = P[:, :, None, o:o + K]; T = np.take_along_axis(L, pe, 3)
        y = np.take_along_axis(X, T.reshape(N, 8, 1, 16 * K), 3).reshape(N, 8, 16, 16, K)
        k1 = np.argmin(y, axis=3); least = np.min(y, axis=3); less = least < x
        x = np.where(less, least, x); s = np.where(less, np.take_along_axis(T, k1, 2), s)
        den = np.sum(be - x, axis=2) - np.sum(b[..., v:v + K] - X[..., v:v + K], axis=2) > gap
        k2 = np.sum(y[:, :, :, 0, :], axis=2) & 15
        new = np.take_along_axis(np.take_along_axis(L, Q[:, :, None, o:o + K], 3), k2[:, :, None, :], 2)
        put = den[:, :, None, :] & (np.arange(16)[:, None] == ((lane + t) & 15)[None, :])
        np.put_along_axis(L, np.broadcast_to(pe, T.shape), np.where(put, new, T), 3)
        x = np.where(den[:, :, None, :], be, x); s = np.where(den[:, :, None, :], e, s); A = A + np.sum(den, axis=2)
        d = 1 + t % (N - 1)
        X[..., o:o + K] = x; S[..., o:o + K] = s; X[..., d * V + o:d * V + o + K] = np.roll(x, d, axis=0)
    return {"yx": X.reshape(N, 128, W).astype(np.float32).astype(BF), "ys": S.reshape(N, 128, V).astype(np.float32), "yl": L.reshape(N, 128, NS).astype(np.float32)}

@@ -1,0 +1,643 @@
+from concourse.bass import DstId, RemoteDMATransfer
+from concourse.mybir import dt, AluOpType, AxisListType, ActivationFunctionType
+
+K, C, NS, RO, N = 160, 4, 1024, 6, 6
+V_, W_ = C * K, N * C * K
+ALU = AluOpType
+ACT = ActivationFunctionType
+F32, BF, I32, U16 = "float32", "bfloat16", "int32", "uint16"
+
+SCRATCH = {
+    "Xb": ("sbuf", [128, W_], BF), "Xk": ("sbuf", [128, W_], F32), "Bb": ("sbuf", [128, V_], BF),
+    "Li": ("sbuf", [128, NS], I32), "Lf": ("sbuf", [128, NS], F32),
+    "Si": ("sbuf", [128, V_], I32), "S16": ("sbuf", [128, V_], U16), "Sf": ("sbuf", [128, V_], F32),
+    "Pi": ("sbuf", [128, 40], I32), "Qi": ("sbuf", [128, 40], I32),
+    "P16": ("sbuf", [128, 40], U16), "Q16": ("sbuf", [128, 40], U16),
+    "thi": ("sbuf", [128, 1], I32), "mgi": ("sbuf", [128, 1], I32), "mgf": ("sbuf", [128, 1], F32),
+    "thf": ("sbuf", [128, 2], F32), "mgr": ("sbuf", [128, K], F32),
+    "YS": ("sbuf", [128, 2 * 1280], F32), "YV": ("sbuf", [128, 1280], F32), "R": ("sbuf", [128, RO * 1280], F32),
+    "D0c": ("sbuf", [128, 1280], BF),
+    "far": ("sbuf", [128, RO * 2560], BF), "ab": ("sbuf", [128, 2 * 2560], BF),
+    "sb": ("sbuf", [128, RO * K], BF), "land": ("sbuf", [128, RO * K], BF),
+    "Tf": ("sbuf", [128, 2 * K], F32), "O16": ("sbuf", [128, 2 * K], U16), "LQ": ("sbuf", [128, K], F32),
+    "mi": ("sbuf", [128, K], I32), "xx": ("sbuf", [128, K], BF), "uu": ("sbuf", [128, K], BF),
+    "x1a": ("sbuf", [128, K], BF), "x1": ("sbuf", [128, K], BF),
+    "sg": ("sbuf", [128, RO * K], BF), "acc": ("sbuf", [128, 8], F32),
+    "Ai": ("sbuf", [128, 8], I32), "Am": ("sbuf", [128, 8], I32), "Af": ("sbuf", [128, 8], F32), "bias": ("sbuf", [128, 8], F32),
+    "hi": ("sbuf", [128, K], I32), "hr": ("sbuf", [128, K], I32), "sel": ("sbuf", [128, K], F32),
+    "dl": ("sbuf", [128, K], F32), "dv": ("sbuf", [128, K], F32),
+    "sa": ("sbuf", [128, RO * K], F32), "sa2": ("sbuf", [128, K], F32), "sz": ("sbuf", [128, RO * K], I32),
+    "one": ("sbuf", [128, 144], F32), "Iw": ("sbuf", [128, 144], F32), "W0": ("sbuf", [128, 144], F32), "W1": ("sbuf", [128, 144], F32),
+    "Ip": ("sbuf", [128, 128], BF), "In": ("sbuf", [128, 128], BF), "I12": ("sbuf", [128, 128], BF),
+    "P25": ("sbuf", [128, 128], BF), "N25": ("sbuf", [128, 128], BF), "Inf": ("sbuf", [128, 128], F32),
+    "B1": ("sbuf", [128, 128], F32), "B2": ("sbuf", [128, 128], F32), "Bp": ("sbuf", [128, 128], BF), "Bn": ("sbuf", [128, 128], BF),
+    "Bs": ("sbuf", [128, 128], F32), "Z": ("sbuf", [128, 144], BF),
+    "G1": ("sbuf", [128, 128], F32), "G2s": ("sbuf", [128, 128], F32), "Gt": ("sbuf", [128, 128], F32),
+    "rlo": ("sbuf", [128, 480], BF), "rhi": ("sbuf", [128, 128], BF), "r1": ("sbuf", [128, K], BF), "cr": ("sbuf", [128, 14 * 128], BF),
+    "Z2": ("sbuf", [128, 144], BF), "Zn": ("sbuf", [128, 144], BF), "rep": ("sbuf", [128, 2560], BF),
+    "c2": ("sbuf", [128, RO * K], F32),
+    "pi": ("sbuf", [128, 1], I32), "pm": ("sbuf", [128, 1], I32), "pc": ("sbuf", [128, 4], F32),
+    "jm": ("sbuf", [128, 176], F32), "dg": ("sbuf", [128, 176], F32),
+    "PD0": ("psum", [128, 512], F32), "PD1": ("psum", [128, 512], F32), "PDI": ("psum", [128, 512], F32), "PS": ("psum", [128, 512], F32),
+    "PE": ("psum", [128, 512], F32), "PK": ("psum", [128, 512], F32), "PL": ("psum", [128, 512], F32), "PV": ("psum", [128, 512], F32),
+}
+NDMA = 48
+SEMAPHORES = ["cV", "cS", "cT", "cG", "sent"] + ["arr%d" % t for t in range(2 * RO)] + ["d%d" % i for i in range(NDMA)]
+
+KEY0 = 61440 - (1 << 24)
+FIX, DLAT, DBW = 50.0, 2000.0, 300.0
+TIMES = [(1.0, 1.56, 3.8, 0.5, 120.0, 80.0, 3500.0), (0.87, 1.15, 2.2, 0.43, 70.0, 40.0, 4500.0), (1.2, 1.95, 5.2, 0.6, 180.0, 120.0, 2800.0)]
+YCH = [[(0, 20), (20, 60), (60, 108), (108, 160)]] * 4 + [[(0, 40), (40, 100), (100, 160)]] * 2
+FARV = [((0, 40, "S"), (40, 80, "S"), (80, 120, "S"), (120, 160, "V"))] * 4 + [((0, 40, "S"), (40, 80, "S"), (80, 120, "r"), (120, 160, "r"))] * 2
+PARTS = [[(0, 160)]] * 6
+LAG = [0, 1, 2, 4]
+PASSES, MOVES, SEED, SLACK = 6, 300, 1, 200.0
+RESET, SWAPS, PACK = 1000000, 5000, 4
+KEPT = {}
+PCH = [(0, 6), (6, 11), (11, 16)]
+BCH = [(0, 960), (960, 1920), (1920, 2880), (2880, 3360), (3360, 3840)]
+
+
+def plan(T, g, topo, core, rank):
+    ops = []
+    size = {"float32": 4, "bfloat16": 2, "int32": 4, "uint16": 2}
+
+    def A(name, a=None, b=None, step=1, parts=128, p0=0):
+        n = SCRATCH[name][1][1]
+        a = 0 if a is None else a
+        b = n if b is None else b
+        t = T[name]
+        ap = t[p0:parts, a:b] if step == 1 else t[p0:parts, a:b:step]
+        return {"ap": ap, "buf": name, "lo": a, "hi": b, "n": len(range(a, b, step)), "ps": SCRATCH[name][0] == "psum",
+                "w": size[SCRATCH[name][2]], "x": []}
+
+    def IND(win, off):
+        return {"ap": win["ap"].indirect(off["ap"]), "buf": win["buf"], "lo": win["lo"], "hi": win["hi"], "n": 16 * off["n"],
+                "ps": False, "w": win["w"], "x": [off], "ind": True}
+
+    def add(eng, fn, cost, rd, wr, kind="c", grp=None, lat=0.0):
+        r, w = [], []
+        for a in rd:
+            if isinstance(a, dict):
+                r.append(a); r.extend(a["x"])
+        for a in wr:
+            w.append(a); r.extend(a["x"])
+        ops.append({"eng": eng, "fn": fn, "cost": cost, "rd": r, "wr": w, "kind": kind, "grp": grp, "lat": lat, "id": len(ops)})
+        return ops[-1]
+
+    def val(s):
+        return s["ap"] if isinstance(s, dict) else s
+
+    def vcost(out, ins, two=False):
+        n = out["n"]
+        if out.get("ind"): return (FIX, 0, 0, n, 0)
+        if any(a.get("ind") for a in ins): return (FIX, 0, n, 0, 0)
+        if two: r = 1.0 if any(a["ps"] for a in ins) else 2.0
+        else: r = 0.5 if all(a["w"] == 2 for a in ins + [out]) else 1.0
+        return (0, max(64.0, n * r), 0, 0, 0)
+
+    def tc(out, in_):
+        return add("V", lambda: g.vector.tensor_copy(out["ap"], in_["ap"]), vcost(out, [in_]), [in_], [out])
+
+    def tt(out, a, b, op):
+        return add("V", lambda: g.vector.tensor_tensor(out["ap"], a["ap"], b["ap"], op), vcost(out, [a, b], True), [a, b], [out])
+
+    def ts(out, a, s1, op0, s2=None, op1=None):
+        if op1 is None: fn = lambda: g.vector.tensor_scalar(out["ap"], a["ap"], val(s1), None, op0)
+        else: fn = lambda: g.vector.tensor_scalar(out["ap"], a["ap"], val(s1), val(s2), op0, op1)
+        return add("V", fn, vcost(out, [a]), [a, s1, s2], [out])
+
+    def ms(out, c):
+        return add("V", lambda: g.vector.memset(out["ap"], c), (0, max(64.0, out["n"] * out["w"] / 4.0), 0, 0, 0), [], [out])
+
+    def scan(out, d0, d1):
+        return add("V", lambda: g.vector.tensor_tensor_scan(out["ap"], d0["ap"], d1["ap"], 0.0, ALU.add, ALU.min), (0, max(64, out["n"]), 0, 0, 0), [d0, d1], [out])
+
+    def act(out, in_, func, bias=0.0, scale=1.0, accum=None):
+        if accum is None: fn = lambda: g.scalar.activation(out["ap"], in_["ap"], func, bias=val(bias), scale=scale)
+        else: fn = lambda: g.scalar.activation(out["ap"], in_["ap"], func, bias=val(bias), scale=scale, accum_out=accum["ap"])
+        cost = (FIX, 0, out["n"], 0, 0) if in_.get("ind") else (FIX, out["n"], 0, 0, 0)
+        return add("S", fn, cost, [in_, bias], [out] + ([accum] if accum else []))
+
+    ng = [0]
+
+    def mm(out, terms):
+        ng[0] += 1
+        for i in range(len(terms)):
+            mm1(out, terms[i][0], terms[i][1], i == 0, i == len(terms) - 1, ng[0])
+
+    def mm1(out, l, r, st, sp, grp):
+        return add("T", lambda: g.tensor.matmul(out["ap"], l["ap"], r["ap"], st, sp), (0, 0, 0, 0, max(64, r["n"]) * (4 if r["w"] == 4 else 1)),
+                   [l, r], [out], grp=grp)
+
+    def iota(out, pat, base, cm):
+        if SCRATCH[out["buf"]][2] == I32: fn = lambda: g.iota(out["ap"], pat, base, cm)
+        else: fn = lambda: g.iota(out["ap"], pat, base, cm, allow_small_or_imprecise_dtypes=True)
+        return add("G", fn, (130, 2 * out["n"], 0, 0, 0), [], [out])
+
+    def asel(out, in_, pat, base, cm, op):
+        return add("G", lambda: g.affine_select(out["ap"], in_["ap"], pat, op, 0.0, base, cm), (170, 2 * out["n"], 0, 0, 0), [in_], [out])
+
+    def dma(q, out, in_):
+        e = g.sync if q == "Y" else g.scalar
+        sb = out if isinstance(out, dict) else in_
+        nb = sb["n"] * sb["w"] * 128
+        return add(q, lambda: e.dma_start(val(out), val(in_)), (60, 0, 0, 0, 0), [in_], [out] if isinstance(out, dict) else [], kind="d", lat=DLAT + nb / DBW)
+
+    dma("Y", A("Pi"), T.grant[:])
+    loads = [(A("Li"), T.favor[:])] + [(A("Xb", a, b), T.base[:, a:b]) for a, b in BCH]
+    loads += [(A("Bb"), T.base[:, 0:V_]), (A("Si", 0, K), T.src[:, 0:K]), (A("Si", K, V_), T.src[:, K:V_])]
+    before = 0.0
+    for out, src in ((A("mgi", parts=8), T.mg[:]), (A("Qi"), T.part[:]), (A("thi"), T.th[:])):
+        dma("S", out, src)
+    prev = ops[0]
+    for out, src in loads:
+        op = dma("Y", out, src)
+        op["after"] = prev
+        prev = op
+        op["lat"] += before
+        before += out["n"] * out["w"] * 128 / DBW
+
+    ms(A("one"), 1.0)
+    asel(A("Iw"), A("one"), [[-1, 144]], 8, 1, ALU.is_equal)
+    ms(A("rlo", parts=64), 0.0)
+    iota(A("rlo", parts=1), [[0, 3], [1, K]], 0, 0)
+    iota(A("pi"), [[0, 1]], 0, 1)
+    asel(A("B1"), A("one", 0, 128), [[-16, 8], [0, 16]], 0, 1, ALU.is_ge)
+    asel(A("B2"), A("B1"), [[16, 8], [0, 16]], 15, -1, ALU.is_ge)
+    asel(A("G1", parts=8), A("one", 0, 128, parts=8), [[1, 128]], 0, -16, ALU.is_ge)
+    asel(A("G2s", parts=8), A("G1", parts=8), [[-1, 128]], 15, 16, ALU.is_ge)
+    iota(A("jm"), [[0, 11], [1, 16]], 0, 0)
+    for j in (1, 2): ms(A("rlo", j * K, (j + 1) * K, parts=33, p0=32), float(j * K))
+    ms(A("rhi", parts=64), 2.0 ** -16)
+    ms(A("r1", parts=1), 1.0)
+    crv = [1.0, -491520.0] + [4096.0 + c * K for c in range(C)] + [16384.0, 2.0 ** -16, -255.0]
+    crv += [((1 + t % (N - 1)) * V_ + (t % C) * K - 4096) / 65536.0 for t in range(RO - 1)]
+    for j in range(len(crv)): ms(A("cr", j * 128, (j + 1) * 128, parts=1), crv[j])
+    CR = lambda j: A("cr", j * 128, (j + 1) * 128, parts=1)
+    Id = A("Iw", 8, 136)
+    for nm, s in (("Ip", 1.0), ("In", -1.0), ("I12", 4096.0), ("P25", 2.0 ** 25), ("N25", -2.0 ** 25), ("Inf", -1.0)):
+        ts(A(nm), Id, s, ALU.mult)
+    ts(A("pm"), A("pi"), 15, ALU.bitwise_and)
+    tc(A("pc", 0, 1), A("pm"))
+    ts(A("pc", 1, 2), A("pm"), 8.0, ALU.is_lt)
+    ts(A("pc", 2, 3), A("pm"), 8.0, ALU.is_ge)
+    ts(A("pc", 3, 4), A("pm"), -1.0, ALU.mult, 4112.0 - 7.47, ALU.add)
+    ts(A("W0"), A("Iw"), A("pc", 1, 2), ALU.mult)
+    ts(A("W1"), A("Iw"), A("pc", 2, 3), ALU.mult)
+    for nm, s in (("Bp", 8192.0), ("Bn", -8192.0), ("Bs", 4096.0)):
+        ts(A(nm), A("B2"), s, ALU.mult)
+    ms(A("Z"), 0.0)
+    tc(A("Z", 15, 128, 16), A("B2", 0, 128, 16))
+    ts(A("Z2"), A("Z"), 2.0, ALU.mult)
+    ts(A("Zn"), A("Z"), -1.0, ALU.mult)
+    ts(A("Gt", parts=8), A("G2s", parts=8), -8192.0, ALU.mult)
+    ts(A("dg"), A("jm"), A("pc", 0, 1), ALU.not_equal, 1e9, ALU.mult)
+    nd0 = 8 * max(b - a for ch in YCH for a, b in ch)
+    ms(A("D0c", 0, nd0), -0.0625)
+    ms(A("D0c", 0, nd0, 8), 1024.0)
+    ms(A("Af", 0, 1), 80.0)
+    LO = A("rlo", 0, K, parts=1)
+    R1 = A("r1", parts=1)
+    X1 = A("PV", 336, 336 + K)
+
+    tc(A("P16"), A("Pi"))
+
+    def lists(t):
+        c, u = t % C, (t % 2) * K
+        off = A("P16", 10 * c, 10 * c + 10)
+        if t == 0: tc(A("Tf", u, u + K), IND(A("Li"), off))
+        else: act(A("Tf", u, u + K), IND(A("Lf"), off), ACT.Identity)
+        ev, od = A("Tf", u, u + K, 2), A("Tf", u + 1, u + K, 2)
+        mm(A("PL", 320, 400), [(A("W0", 8, 136), ev), (A("W0", 0, 128), od)])
+        mm(A("PL", 400, 480), [(A("W1", 16, 144), ev), (A("W1", 8, 136), od)])
+        tc(A("O16", u, u + K), A("PL", 320, 480))
+
+    lists(0)
+    banks = ["PD0", "PD1", "PDI", "PS", "PE", "PK", "PV", "PD0", "PD1", "PDI"]
+    cuts = [0, 480, 960, 1440, 1920, 2400, 2880, 3120, 3360, 3600, 3840]
+    for j in range(10):
+        a, b = cuts[j], cuts[j + 1]
+        ps = A(banks[j], 0, b - a)
+        mm(ps, [(A("rhi", parts=33), A("rlo", 0, b - a, parts=33)), (A("Ip"), A("Xb", a, b))])
+        if j % 2 == 0: act(A("Xk", a, b), ps, ACT.Identity, bias=(KEY0 + a) / 65536.0)
+        else: ts(A("Xk", a, b), ps, (KEY0 + a) / 65536.0, ALU.add)
+    ts(A("PV", K, K + 176), A("dg"), 255.5, ALU.add)
+    tc(A("Q16"), A("Qi"))
+    for j in range(2): tc(A("Lf", 512 * j, 512 * j + 512), A("Li", 512 * j, 512 * j + 512))
+    for c in range(C): tc(A("S16", c * K, c * K + K), A("Si", c * K, c * K + K))
+    ts(A("thf", 0, 1), A("thi"), -4096.0, ALU.add)
+    tc(A("thf", 1, 2), A("thi"))
+    tc(A("mgf", parts=8), A("mgi", parts=8))
+    ts(A("mgr", 0, 128, parts=8), A("one", 0, 128, parts=8), A("mgf", parts=8), ALU.mult)
+    ts(A("mgr", 128, K, parts=8), A("one", 0, K - 128, parts=8), A("mgf", parts=8), ALU.mult)
+    ts(A("bias", 0, 1), A("thf", 0, 1), -8192.0, ALU.mult)
+    for a, b in ((960, 1440), (1600, 2240), (2400, 3040), (3360, 3840)):
+        dma("Y", T.yx[:, a:b], A("Xb", a, b))["low"] = True
+
+    last = {}
+
+    def far_gather(t):
+        o = (t % C) * K
+        for l0, l1, e in FARV[t]:
+            out, src = A("far", 2560 * t + 16 * l0, 2560 * t + 16 * l1), IND(A("Xb"), A("S16", o + l0, o + l1))
+            if e == "S": act(out, src, ACT.Identity)
+            elif e == "V": tc(out, src)
+            else:
+                r0, a0 = 1280 * (t - C) + 16 * (l0 - 80), 2560 * (t % 2) + 16 * l0
+                tt(out, src, A("rep", r0, r0 + 16 * (l1 - l0)), ALU.subtract)
+                if e == "a": act(A("ab", a0, a0 + 16 * (l1 - l0)), out, ACT.Abs)
+                else: ts(A("ab", a0, a0 + 16 * (l1 - l0)), out, 0.0, ALU.max)
+
+    nch = [0]
+
+    def distances(t, old):
+        for h in ((0, 1) if t < C else (1, 0)):
+            ng[0] += 1
+            gid, f0, a0 = ng[0], 2560 * t + 1280 * h, 2560 * (t % 2) + 1280 * h
+            di = A("PDI", 80 * h, 80 * h + 80)
+            if FARV[t][-1][2] in "ar" and h == 1:
+                for l0, l1, e in FARV[t]:
+                    if e not in "ar": continue
+                    f0, a0, n = 2560 * t + 16 * l0, 2560 * (t % 2) + 16 * l0, 16 * (l1 - l0)
+                    terms = [(A("Zn", 15 - p, 143 - p), A("far", f0 + p, f0 + n, 16)) for p in range(16)] if e == "r" else []
+                    terms += [(A("Z2" if e == "r" else "Z", 15 - p, 143 - p), A("ab", a0 + p, a0 + n, 16)) for p in range(16)]
+                    mm(A("PDI", l0, l1), terms)
+                act(di, di, ACT.Identity, bias=A("bias", t, t + 1), scale=8192.0)
+                continue
+            for p0, p1 in PCH:
+                bank = "PD%d" % (nch[0] % 2)
+                nch[0] += 1
+                for p in range(p0, p1):
+                    mm(A(bank, 80 * (p - p0), 80 * (p - p0 + 1)),
+                       [(A("In"), A(old[0], old[1] + 80 * h, old[1] + 80 * h + 80)), (A("Ip"), A("far", f0 + p, f0 + 1280, 16))])
+                act(A("ab", a0 + 80 * p0, a0 + 80 * p1), A(bank, 0, 80 * (p1 - p0)), ACT.Abs)
+                for p in range(p0, p1):
+                    mm1(di, A("Z", 15 - p, 143 - p), A("ab", a0 + 80 * p, a0 + 80 * p + 80), p == 0, p == 15 and t >= C, gid)
+            if t < C:
+                mm1(di, A("I12"), A("sg", t * K + 80 * h, t * K + 80 * h + 80), False, True, gid)
+            else:
+                act(di, di, ACT.Identity, bias=A("bias", t, t + 1), scale=8192.0)
+        if t < C: act(A("PDI", 0, K), A("PDI", 0, K), ACT.Identity, bias=A("bias", t, t + 1), scale=8192.0)
+
+    def keys(t, own, n0, told, n1):
+        ps = A("PK", 0, K)
+        mm(ps, [(CR(7), LO), (A("Ip"), own)])
+        act(A("Xk", n0, n0 + K), ps, ACT.Identity, bias=(KEY0 + n0) / 65536.0)
+        ps = A("PK", K, 2 * K)
+        mm(ps, [(CR(8), R1), (CR(9 + t), R1), (CR(7), LO)])
+        for l0, l1 in PARTS[t]:
+            tt(A("Xk", n1 + l0, n1 + l1), A("land", t * K + l0, t * K + l1), A("PK", K + l0, K + l1), ALU.add)
+
+    def sources(t):
+        c = t % C
+        o = c * K
+        be, xf, Rk = A("Bb", o, o + K), A("sb", t * K, t * K + K), A("R", 1280 * t + 7, 1280 * t + 1280, 8)
+        G2, sa, sz = A("PS", 0, K), A("sa", t * K, t * K + K), A("sz", t * K, t * K + K)
+        if t < C:
+            distances(t, ("Bb", o))
+            mm(G2, [(A("P25"), xf), (A("N25"), be), (CR(0), LO), (CR(2 + c), R1)])
+            tt(sa, A("PDI", 0, K), A("Si", o, o + K), ALU.max)
+            tt(G2, sa, G2, ALU.min)
+        else:
+            G3 = A("PS", K, 2 * K)
+            mm(G3, [(CR(0), LO), (CR(2 + c), R1)])
+            tt(A("x1"), xf, X1, ALU.subtract)
+            mm(G2, [(CR(6), R1), (A("P25"), A("x1"))])
+            tt(sa, A("PDI", 0, K), A("Si", o, o + K), ALU.max)
+            tt(A("sa2"), sa, A("PE", 0, K), ALU.max)
+            tt(sa, A("sa2"), G3, ALU.min)
+            tt(G2, sa, G2, ALU.min)
+        act(A("c2", t * K, t * K + K), Rk, ACT.Identity, scale=65536.0)
+        tt(sz, A("c2", t * K, t * K + K), G2, ALU.max)
+        ts(A("Si", o, o + K), sz, 4095, ALU.bitwise_and)
+        if t + C < RO:
+            tc(A("S16", o, o + K), A("Si", o, o + K))
+        else:
+            tc(A("Sf", o, o + K), A("Si", o, o + K))
+            dma("Y", T.ys[:, o:o + K], A("Sf", o, o + K))
+
+    for t in range(RO):
+        c = t % C
+        o, f, d, u = c * K, c ^ 1, 1 + t % (N - 1), (t % 2) * K
+        ys0, r0 = 1280 * (t % 2), 1280 * t
+        be, xf = A("Bb", o, o + K), A("sb", t * K, t * K + K)
+        bP, E, Tf = A("PV", 0, K), A("PE", 0, K), A("Tf", u, u + K)
+        Rk = A("R", r0 + 7, r0 + 1280, 8)
+        prev = None
+        for l0, l1 in YCH[t]:
+            op = act(A("YS", ys0 + 8 * l0, ys0 + 8 * l1), IND(A("Xk"), A("O16", u + l0 // 2, u + l1 // 2)), ACT.Identity, bias=-0.5)
+            op["after"] = prev
+            prev = op
+            tt(A("YV", 8 * l0, 8 * l1), IND(A("Xk"), A("O16", u + 80 + l0 // 2, u + 80 + l1 // 2)), A("YS", ys0 + 8 * l0, ys0 + 8 * l1), ALU.min)
+            scan(A("R", r0 + 8 * l0, r0 + 8 * l1), A("D0c", 0, 8 * (l1 - l0)), A("YV", 8 * l0, 8 * l1))
+        mm(bP, [(A("Ip"), be)])
+        if t >= C:
+            far_gather(t)
+            distances(t, ("sb", last[c] * K))
+        dst = T.cores[(rank + d) % N]
+        ld = A("land", t * K, t * K + K)
+        for part in range(len(PARTS[t])):
+            l0, l1 = PARTS[t][part]
+            mi, xx, uu, bl, El = A("mi", l0, l1), A("xx", l0, l1), A("uu", l0, l1), A("PV", l0, l1), A("PE", l0, l1)
+            ts(mi, A("R", r0 + 8 * l0 + 7, r0 + 8 * l1, 8), 255.502, ALU.add)
+            if t < C:
+                tt(xx, mi, bl, ALU.min)
+            else:
+                tt(A("x1a", l0, l1), A("PDI", l0, l1), A("sb", last[c] * K + l0, last[c] * K + l1), ALU.max)
+                tt(A("PV", 336 + l0, 336 + l1), A("x1a", l0, l1), bl, ALU.min)
+                tt(xx, mi, A("PV", 336 + l0, 336 + l1), ALU.min)
+            terms = [(A("Gt", parts=8), A("mgr", l0, l1, parts=8)), (A("Bp"), A("Bb", o + l0, o + l1))]
+            if f in last:
+                terms += [(A("Bn"), A("Bb", f * K + l0, f * K + l1)), (A("Bp"), A("sb", last[f] * K + l0, last[f] * K + l1))]
+            mm(El, terms + [(A("Bn"), xx)])
+            tt(uu, El, xx, ALU.max)
+            out, far_end = A("sb", t * K + l0, t * K + l1), A("land", t * K + l0, t * K + l1)
+            tt(out, uu, bl, ALU.min)
+
+            def send(k=2 * t + part, dst=dst, out=out, far_end=far_end):
+                rid, pid, _ = topo.addr(dst)
+                return g.remote_dma(far_end["ap"], out["ap"], T.sem["arr%d" % k], T.sem.sent, pid, rid, topo.mask(core, dst))
+            op = add("G", send, (900 + 3 * (l1 - l0) + (1500 if t + part == 0 else 0), 0, 0, 0, 0), [out], [far_end], kind="r", lat=-1080.0)
+            op["t"] = 2 * t + part
+            op["out"] = len(topo.engines(core, dst))
+            op["in"] = len(topo.engines(T.cores[(rank - d) % N], core))
+        act(A("LQ"), IND(A("Lf"), A("Q16", 10 * c, 10 * c + 10)), ACT.Identity, scale=2.0 ** -12)
+        mm(A("PL", 0, K), [(A("B2"), A("YS", ys0, ys0 + 1280, 8))])
+        ts(A("hi"), A("PL", 0, K), A("pc", 3, 4), ALU.add)
+        ts(A("hr"), A("hi"), 15, ALU.bitwise_and)
+        tt(A("sel"), A("LQ"), A("hr"), ALU.max)
+        mm(A("PL", K, 2 * K), [(CR(1), R1), (A("Inf"), Tf), (A("Bs"), A("sel"))])
+        tt(A("dl"), A("uu"), A("PV", K + t, 2 * K + t), ALU.is_gt)
+        tt(A("dv"), A("PL", K, 2 * K), A("dl"), ALU.mult)
+        tt(IND(A("Lf"), A("P16", 10 * c, 10 * c + 10)), Tf, A("dv"), ALU.add)
+        if t < RO - 1:
+            lists(t + 1)
+            keys(t, xf, o, ld, d * V_ + o)
+            act(A("sg", t * K, t * K + K), A("uu"), ACT.Sign, bias=-255.5, accum=A("acc", t, t + 1))
+            ts(A("Ai", t, t + 1), A("acc", t, t + 1), 0.5, ALU.mult, A("Af", t, t + 1), ALU.add)
+            if t < RO - 2: ts(A("Af", t + 1, t + 2), A("Ai", t, t + 1), 80.0, ALU.add)
+            ts(A("Am", t, t + 1), A("Ai", t, t + 1), 31, ALU.bitwise_and)
+            w = 0 if t + 1 < C else 1
+            ts(A("bias", t + 1, t + 2), A("Am", t, t + 1), A("thf", w, w + 1), ALU.add, -8192.0, ALU.mult)
+        else:
+            for j in range(2):
+                dma("YS"[j], T.yl[:, 512 * j:512 * j + 512], A("Lf", 512 * j, 512 * j + 512))
+        if t < C: far_gather(t)
+        else: sources(t)
+        if t + C < RO and FARV[t + C][-1][2] in "ar":
+            for p in range(16): tc(A("rep", 1280 * t + p, 1280 * t + 1280, 16), A("sb", t * K + 80, t * K + K))
+        for t2 in range(C):
+            if LAG[t2] == t: sources(t2)
+        if t + C >= RO: dma("Y", T.yx[:, o:o + K], xf)
+        for l0, l1 in (PARTS[t] if t == RO - 1 else [(0, K)]):
+            dma("Y", T.yx[:, d * V_ + o + l0:d * V_ + o + l1], A("land", t * K + l0, t * K + l1))
+        if t < RO - 1:
+            if t < C - 1:
+                dma("Y", A("Xb", o, o + K), xf)
+                dma("Y", A("Xb", d * V_ + o, d * V_ + o + K), ld)
+            else:
+                tc(A("Xb", o, o + K), xf)
+                for l0, l1 in PARTS[t]:
+                    tc(A("Xb", d * V_ + o + l0, d * V_ + o + l1), A("land", t * K + l0, t * K + l1))
+        last[c] = t
+    return ops
+
+
+def depend(ops):
+    seen = {}
+    for op in ops:
+        deps = {op["after"]["id"]: False} if op.get("after") else {}
+        for acc, write in [(a, False) for a in op["rd"]] + [(a, True) for a in op["wr"]]:
+            for o2, a2, w2 in seen.get(acc["buf"], []):
+                if o2 is op: continue
+                hit = (write or w2) and acc["lo"] < a2["hi"] and a2["lo"] < acc["hi"]
+                if acc["buf"] == "rep" and write and w2: hit = False
+                if acc["ps"] and (o2["eng"] != op["eng"] or op["eng"] == "T"):
+                    if not hit and op["eng"] == o2["eng"]:
+                        deps.setdefault(o2["id"], False)
+                        continue
+                    hit = True
+                if hit:
+                    soft = op["eng"] == "T" and o2["eng"] == "T" and acc["ps"]
+                    deps[o2["id"]] = deps.get(o2["id"], False) or not soft
+        op["deps"] = deps
+        for acc, write in [(a, False) for a in op["rd"]] + [(a, True) for a in op["wr"]]:
+            seen.setdefault(acc["buf"], []).append((op, acc, write))
+
+
+def tables(ops):
+    anc, red = [], []
+    for op in ops:
+        a = 0
+        for j in op["deps"]: a |= anc[j]
+        red.append([j for j in op["deps"] if not (a >> j) & 1])
+        for j in op["deps"]: a |= 1 << j
+        anc.append(a)
+    out = []
+    for cyc, ga, sc, pe, hop, own, rem in TIMES:
+        cost = [c[0] + cyc * (c[1] + ga * c[2] + sc * c[3]) + pe * c[4] for c in [op["cost"] for op in ops]]
+        lat = [op["lat"] + (rem if op["kind"] == "r" else 0.0) for op in ops]
+        pre, suc = [], [[] for op in ops]
+        for op in ops:
+            row = []
+            for j in red[op["id"]]:
+                p = ops[j]
+                w = lat[j] + (own if p["eng"] == op["eng"] and p["kind"] == "c" else hop) if op["deps"][j] else 0.0
+                row.append((j, w))
+                suc[j].append((op["id"], w))
+            pre.append(row)
+        out.append((cost, lat, pre, suc))
+    return out
+
+
+def place(eng, first, cost, edges, rank):
+    busy = {e: [] for e in "VSTGY"}
+    t1 = [0.0] * len(cost)
+    for i in rank:
+        t0, c = first[i], cost[i]
+        for j, w in edges[i]:
+            if t1[j] + w > t0: t0 = t1[j] + w
+        lst = busy[eng[i]]
+        pos = n = len(lst)
+        while pos and lst[pos - 1][1] > t0: pos -= 1
+        while pos < n and t0 + c > lst[pos][0]:
+            if lst[pos][1] > t0: t0 = lst[pos][1]
+            pos += 1
+        lst.insert(pos, (t0, t0 + c))
+        t1[i] = t0 + c
+    return t1
+
+
+def play(eng, first, tab, seq):
+    cost, lat, pre, suc = tab
+    free = {e: 0.0 for e in "VSTGY"}
+    t1 = [0.0] * len(cost)
+    end = 0.0
+    for i in seq:
+        t = free[eng[i]]
+        if first[i] > t: t = first[i]
+        for j, w in pre[i]:
+            if t1[j] + w > t: t = t1[j] + w
+        t += cost[i]
+        t1[i] = free[eng[i]] = t
+        if t + lat[i] > end: end = t + lat[i]
+    return end, t1
+
+
+def order(ops):
+    if "seq" not in KEPT:
+        n = len(ops)
+        tabs = tables(ops)
+        eng = [op["eng"] for op in ops]
+        first = [9000.0 if op.get("low") else 0.0 for op in ops]
+        cost, lat, pre, suc = tabs[0]
+
+        def judge(pr):
+            t1 = place(eng, first, cost, pre, sorted(range(n), key=lambda i: (pr[i], i)))
+            t0 = [t1[i] - cost[i] for i in range(n)]
+            seq = sorted(range(n), key=lambda i: (t0[i], i))
+            ends = [play(eng, first, tab, seq)[0] for tab in tabs]
+            return sum(ends), t0, seq, ends
+
+        bl = [cost[i] + lat[i] for i in range(n)]
+        for i in reversed(range(n)):
+            for j, w in pre[i]: bl[j] = max(bl[j], cost[j] + w + bl[i])
+        pr = [-b for b in bl]
+        best = None
+        for it in range(PASSES):
+            cur = judge(pr)
+            if best is None or cur[0] < best[0]: best = (cur[0], pr, cur[2], cur[3])
+            back = place(eng, lat, cost, suc, sorted(range(n), key=lambda i: (-cur[1][i] - cost[i], -i)))
+            pr = [-b for b in back]
+        pick = [i for i in range(n) if eng[i] in "VS"] * 3 + list(range(n))
+        z = SEED
+        now = best
+        for it in range(MOVES):
+            pr = list(now[1])
+            for rep in range(1 + it % 2):
+                z = (z * 6364136223846793005 + 1442695040888963407) % (1 << 64)
+                i = pick[(z >> 33) % len(pick)]
+                step = ((z >> 13) % 2001 - 1000) / 1000.0
+                pr[i] += step * (400.0, 1500.0, 5000.0)[(z >> 28) % 3]
+                todo = [i]
+                while todo:
+                    a = todo.pop()
+                    for j, w in (pre[a] if step < 0 else suc[a]):
+                        if step < 0 and pr[j] >= pr[a]:
+                            pr[j] = pr[a] - 1.0
+                            todo.append(j)
+                        elif step >= 0 and pr[j] <= pr[a]:
+                            pr[j] = pr[a] + 1.0
+                            todo.append(j)
+            cur = judge(pr)
+            if cur[0] <= now[0] + SLACK * (1.0 - it / MOVES):
+                now = (cur[0], cur[1] if it % RESET else pr, cur[2], cur[3])
+                if cur[0] < best[0]: best = now
+        now = best
+        for it in range(SWAPS):
+            z = (z * 6364136223846793005 + 1442695040888963407) % (1 << 64)
+            seq = now[2]
+            c, la, pr_, su_ = tabs[(z >> 50) % len(tabs)]
+            t1 = play(eng, first, (c, la, pr_, su_), seq)[1]
+            front, lastof = {}, {}
+            for i in seq:
+                front[i] = lastof.get(eng[i])
+                lastof[eng[i]] = i
+            i = max(range(n), key=lambda a: t1[a] + la[a])
+            pairs = []
+            while i is not None:
+                s0, nxt = t1[i] - c[i], None
+                for j, w in pr_[i]:
+                    if t1[j] + w >= s0 - 1e-6: nxt = j
+                if nxt is None and front[i] is not None and t1[front[i]] >= s0 - 1e-6:
+                    nxt = front[i]
+                    pairs.append((nxt, i))
+                i = nxt
+            if not pairs: continue
+            a, b = pairs[(z >> 20) % len(pairs)]
+            pr = [0.0] * n
+            for pos in range(n): pr[seq[pos]] = float(pos)
+            early = (z >> 10) & 1
+            for rep in range((z >> 12) % 3 if (z >> 16) & 1 else 0):
+                if early and front[a] is not None: a = front[a]
+            if early: pr[b] = pr[a] - 0.5
+            else: pr[a] = pr[b] + 0.5 + ((z >> 12) % 40 if (z >> 16) & 1 else 0)
+            todo = [b if early else a]
+            while todo:
+                x = todo.pop()
+                for j, w in (pre[x] if early else suc[x]):
+                    if early and pr[j] >= pr[x]:
+                        pr[j] = pr[x] - 1e-4
+                        todo.append(j)
+                    elif not early and pr[j] <= pr[x]:
+                        pr[j] = pr[x] + 1e-4
+                        todo.append(j)
+            seq = sorted(range(n), key=lambda x: (pr[x], x)) if (z >> 40) % 4 >= PACK else judge(pr)[2]
+            plays = [play(eng, first, tab, seq) for tab in tabs]
+            tot = sum(p[0] for p in plays)
+            if tot <= now[0] + SLACK * (1.0 - it / SWAPS):
+                t1 = plays[0][1]
+                seq = sorted(range(n), key=lambda x: (t1[x] - cost[x], pr[x]))
+                now = (tot, None, seq, [p[0] for p in plays])
+                if tot < best[0]: best = now
+        KEPT["seq"], KEPT["ends"] = best[2], best[3]
+    return [ops[i] for i in KEPT["seq"]]
+
+
+def emit(seq, ops, g, T):
+    q = {"V": g.vector, "S": g.scalar, "T": g.tensor, "G": g, "Y": g.sync}
+    for op in ops: op["sig"] = op["kind"] != "c"
+    rankq = {}
+    for op in seq:
+        rankq[op["eng"]] = rankq.get(op["eng"], 0) + 1
+        op["pos"] = rankq[op["eng"]]
+    for op in seq:
+        best = {}
+        op["need"] = []
+        for j, hard in op["deps"].items():
+            p = ops[j]
+            if not hard: continue
+            if p["kind"] != "c": op["need"].append(p)
+            elif p["eng"] not in best or best[p["eng"]]["pos"] < p["pos"]: best[p["eng"]] = p
+        op["need"].extend(best.values())
+    upto = {}
+    for op in seq:
+        keep = []
+        for p in op["need"]:
+            key = (op["eng"], p["eng"] if p["kind"] == "c" else p["id"])
+            if upto.get(key, 0) >= p["pos"]: continue
+            upto[key] = p["pos"]
+            p["sig"] = True
+            keep.append(p)
+        op["need"] = keep
+    cnt, nd, sent, ends = {}, 0, 0, []
+    for op in seq:
+        if op["kind"] == "c":
+            if op["sig"]: cnt[op["eng"]] = cnt.get(op["eng"], 0) + 1
+            op["sem"], op["val"] = T.sem["c" + op["eng"]], cnt.get(op["eng"], 0)
+        elif op["kind"] == "d":
+            op["sem"], op["val"] = T.sem["d%d" % nd], 16
+            nd += 1
+            ends.append(op)
+        else:
+            op["sem"], op["val"] = T.sem["arr%d" % op["t"]], op["in"]
+            sent += op["out"]
+    for op in seq:
+        e = q[op["eng"]]
+        for p in op["need"]: e.wait_ge(p["sem"], p["val"])
+        ins = op["fn"]()
+        if op["kind"] == "d": ins.then_inc(op["sem"], 16)
+        elif op["kind"] == "c" and op["sig"]: ins.then_inc(op["sem"], 1)
+    g.wait_ge(T.sem.sent, sent)
+    for op in ends:
+        if not op["wr"]: q[op["eng"]].wait_ge(op["sem"], 16)
+
+
+def rank_program(g, core, T, topo):
+    rank = T.rank_of(core)
+    if rank is None:
+        return
+    ops = plan(T, g, topo, core, rank)
+    depend(ops)
+    emit(order(ops), ops, g, T)

@@ -46,7 +46,7 @@ SEMAPHORES = ["cV", "cS", "cT", "cG", "sent"] + ["arr%d" % t for t in range(2 * 
 
 KEY0 = 61440 - (1 << 24)
 FIX, DLAT, DBW = 50.0, 2000.0, 300.0
-TIMES = [(1.0, 1.56, 3.8, 0.5, 120.0, 80.0, 3500.0), (0.87, 1.15, 2.2, 0.43, 70.0, 40.0, 4500.0), (1.2, 1.95, 5.2, 0.6, 180.0, 120.0, 2800.0)]
+TIMES = [(1.0, 1.56, 3.8, 0.5, 120.0, 80.0, 2000.0), (0.87, 1.15, 2.2, 0.43, 70.0, 40.0, 3000.0), (1.2, 1.95, 5.2, 0.6, 180.0, 120.0, 1800.0)]
 YCH = [[(0, 20), (20, 60), (60, 108), (108, 160)]] * 4 + [[(0, 40), (40, 100), (100, 160)]] * 2
 FARV = [((0, 40, "S"), (40, 80, "S"), (80, 120, "S"), (120, 160, "V"))] * 4 + [((0, 40, "S"), (40, 80, "S"), (80, 120, "r"), (120, 160, "r"))] * 2
 PARTS = [[(0, 160)]] * 6

@@ -14,12 +14,13 @@ SCRATCH = {
     "Pi": ("sbuf", [128, 40], I32), "Qi": ("sbuf", [128, 40], I32),
     "P16": ("sbuf", [128, 40], U16), "Q16": ("sbuf", [128, 40], U16),
     "thi": ("sbuf", [128, 1], I32), "mgi": ("sbuf", [128, 1], I32), "mgf": ("sbuf", [128, 1], F32),
-    "thf": ("sbuf", [128, 2], F32), "mgr": ("sbuf", [128, K], F32),
+    "thp": ("sbuf", [128, 2], I32), "Dh": ("sbuf", [128, 256], BF), "Dl": ("sbuf", [128, RO * 128], BF), "cn": ("sbuf", [128, 2 * K], BF),
+    "thf": ("sbuf", [128, 3], F32), "mgr": ("sbuf", [128, K], F32),
     "YS": ("sbuf", [128, 2 * 1280], F32), "YV": ("sbuf", [128, 1280], F32), "R": ("sbuf", [128, RO * 1280], F32),
     "D0c": ("sbuf", [128, 1280], BF),
-    "far": ("sbuf", [128, RO * 2560], BF), "ab": ("sbuf", [128, 2 * 2560], BF),
+    "far": ("sbuf", [128, RO * 2560], BF), "ab": ("sbuf", [128, 3 * 2560], BF),
     "sb": ("sbuf", [128, RO * K], BF), "land": ("sbuf", [128, RO * K], BF),
-    "Tf": ("sbuf", [128, 2 * K], F32), "O16": ("sbuf", [128, 2 * K], U16), "LQ": ("sbuf", [128, K], F32),
+    "Tf": ("sbuf", [128, 2 * K], F32), "O16": ("sbuf", [128, 2 * K], U16),
     "mi": ("sbuf", [128, K], I32), "xx": ("sbuf", [128, K], BF), "uu": ("sbuf", [128, K], BF),
     "x1a": ("sbuf", [128, K], BF), "x1": ("sbuf", [128, K], BF),
     "sg": ("sbuf", [128, RO * K], BF), "acc": ("sbuf", [128, 8], F32),
@@ -28,13 +29,13 @@ SCRATCH = {
     "dl": ("sbuf", [128, K], F32), "dv": ("sbuf", [128, K], F32),
     "sa": ("sbuf", [128, RO * K], F32), "sa2": ("sbuf", [128, K], F32), "sz": ("sbuf", [128, RO * K], I32),
     "one": ("sbuf", [128, 144], F32), "Iw": ("sbuf", [128, 144], F32), "W0": ("sbuf", [128, 144], F32), "W1": ("sbuf", [128, 144], F32),
-    "Ip": ("sbuf", [128, 128], BF), "In": ("sbuf", [128, 128], BF), "I12": ("sbuf", [128, 128], BF),
+    "Ip": ("sbuf", [128, 128], BF), "In": ("sbuf", [128, 128], BF),
     "P25": ("sbuf", [128, 128], BF), "N25": ("sbuf", [128, 128], BF), "Inf": ("sbuf", [128, 128], F32),
     "B1": ("sbuf", [128, 128], F32), "B2": ("sbuf", [128, 128], F32), "Bp": ("sbuf", [128, 128], BF), "Bn": ("sbuf", [128, 128], BF),
-    "Bs": ("sbuf", [128, 128], F32), "Z": ("sbuf", [128, 144], BF),
+    "Z": ("sbuf", [128, 144], BF),
     "G1": ("sbuf", [128, 128], F32), "G2s": ("sbuf", [128, 128], F32), "Gt": ("sbuf", [128, 128], F32),
     "rlo": ("sbuf", [128, 480], BF), "rhi": ("sbuf", [128, 128], BF), "r1": ("sbuf", [128, K], BF), "cr": ("sbuf", [128, 14 * 128], BF),
-    "Z2": ("sbuf", [128, 144], BF), "Zn": ("sbuf", [128, 144], BF), "rep": ("sbuf", [128, 2560], BF),
+    "Z2": ("sbuf", [128, 144], BF), "Zn": ("sbuf", [128, 144], BF), "rep": ("sbuf", [128, RO * 1280], BF),
     "c2": ("sbuf", [128, RO * K], F32),
     "pi": ("sbuf", [128, 1], I32), "pm": ("sbuf", [128, 1], I32), "pc": ("sbuf", [128, 4], F32),
     "jm": ("sbuf", [128, 176], F32), "dg": ("sbuf", [128, 176], F32),
@@ -42,24 +43,26 @@ SCRATCH = {
     "PE": ("psum", [128, 512], F32), "PK": ("psum", [128, 512], F32), "PL": ("psum", [128, 512], F32), "PV": ("psum", [128, 512], F32),
 }
 NDMA = 48
-SEMAPHORES = ["cV", "cS", "cT", "cG", "sent"] + ["arr%d" % t for t in range(2 * RO)] + ["d%d" % i for i in range(NDMA)]
+SEMAPHORES = ["cV", "cS", "cT", "cG", "sent"] + ["arr%d" % t for t in range(RO)] + ["d%d" % i for i in range(NDMA)]
 
 KEY0 = 61440 - (1 << 24)
-FIX, DLAT, DBW = 50.0, 2000.0, 300.0
-TIMES = [(1.0, 1.56, 3.8, 0.5, 120.0, 80.0, 2000.0), (0.87, 1.15, 2.2, 0.43, 70.0, 40.0, 3000.0), (1.2, 1.95, 5.2, 0.6, 180.0, 120.0, 1800.0)]
-YCH = [[(0, 20), (20, 60), (60, 108), (108, 160)]] * 4 + [[(0, 40), (40, 100), (100, 160)]] * 2
-FARV = [((0, 40, "S"), (40, 80, "S"), (80, 120, "S"), (120, 160, "V"))] * 4 + [((0, 40, "S"), (40, 80, "S"), (80, 120, "r"), (120, 160, "r"))] * 2
-PARTS = [[(0, 160)]] * 6
+FIX, DLAT, DBW = 60.0, 1400.0, 300.0
+TIMES = [(0.83, 1.56, 3.8, 0.42, 200.0, 120.0, 900.0), (0.9, 1.25, 2.6, 0.46, 160.0, 90.0, 1700.0), (1.15, 1.8, 4.6, 0.6, 230.0, 130.0, 1100.0)]
+YCH = [[(0, 20), (20, 60), (60, 112), (112, 160)]] * 4 + [[(0, 40), (40, 100), (100, 160)]] * 2
+SELF = [20] * 4 + [0] * 2
+FARV = [((0, 40, "S"), (40, 80, "S"), (80, 120, "S"), (120, 134, "S"), (134, 148, e), (148, 160, e)) for e in "Vrrr"] \
+    + [((0, 40, "S"), (40, 80, "S"), (80, 120, "r"), (120, 160, "r"))] * 2
+REP = ["G"] * 6
 LAG = [0, 1, 2, 4]
-PASSES, MOVES, SEED, SLACK = 6, 300, 1, 200.0
-RESET, SWAPS, PACK = 1000000, 5000, 4
-KEPT = {}
-PCH = [(0, 6), (6, 11), (11, 16)]
+KEYQ = "SVSVSVSVSV"
 BCH = [(0, 960), (960, 1920), (1920, 2880), (2880, 3360), (3360, 3840)]
+DUE, REACH = {}, (1, 8, 30, 120)
+SHIFTS, PACK, SWAPS, SEED, SLACK, RUN = 1000, 6, 5000, 1, 500.0, 256
+KEPT = {}
 
 
 def plan(T, g, topo, core, rank):
-    ops = []
+    ops, tag = [], [None]
     size = {"float32": 4, "bfloat16": 2, "int32": 4, "uint16": 2}
 
     def A(name, a=None, b=None, step=1, parts=128, p0=0):
@@ -75,14 +78,14 @@ def plan(T, g, topo, core, rank):
         return {"ap": win["ap"].indirect(off["ap"]), "buf": win["buf"], "lo": win["lo"], "hi": win["hi"], "n": 16 * off["n"],
                 "ps": False, "w": win["w"], "x": [off], "ind": True}
 
-    def add(eng, fn, cost, rd, wr, kind="c", grp=None, lat=0.0):
+    def add(eng, fn, cost, rd, wr, kind="c", lat=0.0):
         r, w = [], []
         for a in rd:
             if isinstance(a, dict):
                 r.append(a); r.extend(a["x"])
         for a in wr:
             w.append(a); r.extend(a["x"])
-        ops.append({"eng": eng, "fn": fn, "cost": cost, "rd": r, "wr": w, "kind": kind, "grp": grp, "lat": lat, "id": len(ops)})
+        ops.append({"eng": eng, "fn": fn, "cost": cost, "rd": r, "wr": w, "kind": kind, "grp": None, "lat": lat, "id": len(ops), "after": None, "tag": tag[0]})
         return ops[-1]
 
     def val(s):
@@ -90,11 +93,11 @@ def plan(T, g, topo, core, rank):
 
     def vcost(out, ins, two=False):
         n = out["n"]
-        if out.get("ind"): return (FIX, 0, 0, n, 0)
-        if any(a.get("ind") for a in ins): return (FIX, 0, n, 0, 0)
+        if out.get("ind"): return (0, FIX, 0, n, 0)
+        if any(a.get("ind") for a in ins): return (0, FIX, n, 0, 0)
         if two: r = 1.0 if any(a["ps"] for a in ins) else 2.0
         else: r = 0.5 if all(a["w"] == 2 for a in ins + [out]) else 1.0
-        return (0, max(64.0, n * r), 0, 0, 0)
+        return (0, 20 + max(64.0, n * r), 0, 0, 0)
 
     def tc(out, in_):
         return add("V", lambda: g.vector.tensor_copy(out["ap"], in_["ap"]), vcost(out, [in_]), [in_], [out])
@@ -111,32 +114,45 @@ def plan(T, g, topo, core, rank):
         return add("V", lambda: g.vector.memset(out["ap"], c), (0, max(64.0, out["n"] * out["w"] / 4.0), 0, 0, 0), [], [out])
 
     def scan(out, d0, d1):
-        return add("V", lambda: g.vector.tensor_tensor_scan(out["ap"], d0["ap"], d1["ap"], 0.0, ALU.add, ALU.min), (0, max(64, out["n"]), 0, 0, 0), [d0, d1], [out])
+        return add("V", lambda: g.vector.tensor_tensor_scan(out["ap"], d0["ap"], d1["ap"], 0.0, ALU.add, ALU.min), (0, 20 + max(64, out["n"]), 0, 0, 0), [d0, d1], [out])
 
     def act(out, in_, func, bias=0.0, scale=1.0, accum=None):
         if accum is None: fn = lambda: g.scalar.activation(out["ap"], in_["ap"], func, bias=val(bias), scale=scale)
         else: fn = lambda: g.scalar.activation(out["ap"], in_["ap"], func, bias=val(bias), scale=scale, accum_out=accum["ap"])
-        cost = (FIX, 0, out["n"], 0, 0) if in_.get("ind") else (FIX, out["n"], 0, 0, 0)
+        cost = (0, 78, out["n"], 0, 0) if in_.get("ind") else (0, 78 + out["n"], 0, 0, 0)
         return add("S", fn, cost, [in_, bias], [out] + ([accum] if accum else []))
 
-    ng = [0]
+    def run(items, grp=None):
+        def fn():
+            for out, l, r, st, sp in items: ins = g.tensor.matmul(out["ap"], l["ap"], r["ap"], st, sp)
+            return ins
+        cyc = sum(max(64, r["n"]) * (4 if r["w"] == 4 else 1) for out, l, r, st, sp in items)
+        op = add("T", fn, (0, 0, 0, 0, cyc), [a for it in items for a in it[1:3]], [it[0] for it in items])
+        op["grp"], op["shut"] = grp, items[-1][4]
+        return op
 
-    def mm(out, terms):
-        ng[0] += 1
-        for i in range(len(terms)):
-            mm1(out, terms[i][0], terms[i][1], i == 0, i == len(terms) - 1, ng[0])
+    def runs(items, grp=None):
+        part = []
+        for it in items:
+            part.append(it)
+            if sum(max(64, x[2]["n"]) for x in part) >= RUN and (grp or it[4]):
+                run(part, grp)
+                part = []
+        if part: run(part, grp)
 
-    def mm1(out, l, r, st, sp, grp):
-        return add("T", lambda: g.tensor.matmul(out["ap"], l["ap"], r["ap"], st, sp), (0, 0, 0, 0, max(64, r["n"]) * (4 if r["w"] == 4 else 1)),
-                   [l, r], [out], grp=grp)
+    def terms(out, pairs, st=True, sp=True):
+        return [(out, pairs[i][0], pairs[i][1], st and i == 0, sp and i == len(pairs) - 1) for i in range(len(pairs))]
+
+    def mm(out, pairs):
+        return run(terms(out, pairs))
 
     def iota(out, pat, base, cm):
         if SCRATCH[out["buf"]][2] == I32: fn = lambda: g.iota(out["ap"], pat, base, cm)
         else: fn = lambda: g.iota(out["ap"], pat, base, cm, allow_small_or_imprecise_dtypes=True)
-        return add("G", fn, (130, 2 * out["n"], 0, 0, 0), [], [out])
+        return add("G", fn, (0, 157 + 2 * out["n"], 0, 0, 0), [], [out])
 
     def asel(out, in_, pat, base, cm, op):
-        return add("G", lambda: g.affine_select(out["ap"], in_["ap"], pat, op, 0.0, base, cm), (170, 2 * out["n"], 0, 0, 0), [in_], [out])
+        return add("G", lambda: g.affine_select(out["ap"], in_["ap"], pat, op, 0.0, base, cm), (0, 205 + 2 * out["n"], 0, 0, 0), [in_], [out])
 
     def dma(q, out, in_):
         e = g.sync if q == "Y" else g.scalar
@@ -173,22 +189,22 @@ def plan(T, g, topo, core, rank):
     ms(A("r1", parts=1), 1.0)
     crv = [1.0, -491520.0] + [4096.0 + c * K for c in range(C)] + [16384.0, 2.0 ** -16, -255.0]
     crv += [((1 + t % (N - 1)) * V_ + (t % C) * K - 4096) / 65536.0 for t in range(RO - 1)]
-    for j in range(len(crv)): ms(A("cr", j * 128, (j + 1) * 128, parts=1), crv[j])
+    for j in range(len(crv)): act(A("cr", j * 128, (j + 1) * 128, parts=1), A("one", 0, 128, parts=1), ACT.Identity, scale=crv[j])
     CR = lambda j: A("cr", j * 128, (j + 1) * 128, parts=1)
     Id = A("Iw", 8, 136)
-    for nm, s in (("Ip", 1.0), ("In", -1.0), ("I12", 4096.0), ("P25", 2.0 ** 25), ("N25", -2.0 ** 25), ("Inf", -1.0)):
-        ts(A(nm), Id, s, ALU.mult)
+    for nm, s in (("Ip", 1.0), ("In", -1.0), ("P25", 2.0 ** 25), ("N25", -2.0 ** 25), ("Inf", -1.0)):
+        act(A(nm), Id, ACT.Identity, scale=s)
     ts(A("pm"), A("pi"), 15, ALU.bitwise_and)
     tc(A("pc", 0, 1), A("pm"))
     ts(A("pc", 1, 2), A("pm"), 8.0, ALU.is_lt)
     ts(A("pc", 2, 3), A("pm"), 8.0, ALU.is_ge)
-    ts(A("pc", 3, 4), A("pm"), -1.0, ALU.mult, 4112.0 - 7.47, ALU.add)
+    ts(A("pc", 3, 4), A("pm"), -1.0, ALU.mult, 2041.03125, ALU.add)
     ts(A("W0"), A("Iw"), A("pc", 1, 2), ALU.mult)
     ts(A("W1"), A("Iw"), A("pc", 2, 3), ALU.mult)
-    for nm, s in (("Bp", 8192.0), ("Bn", -8192.0), ("Bs", 4096.0)):
-        ts(A(nm), A("B2"), s, ALU.mult)
+    for nm, s in (("Bp", 8192.0), ("Bn", -8192.0)):
+        act(A(nm), A("B2"), ACT.Identity, scale=s)
     ms(A("Z"), 0.0)
-    tc(A("Z", 15, 128, 16), A("B2", 0, 128, 16))
+    ts(A("Z", 15, 128, 16), A("B2", 0, 128, 16), 8192.0, ALU.mult)
     ts(A("Z2"), A("Z"), 2.0, ALU.mult)
     ts(A("Zn"), A("Z"), -1.0, ALU.mult)
     ts(A("Gt", parts=8), A("G2s", parts=8), -8192.0, ALU.mult)
@@ -210,101 +226,130 @@ def plan(T, g, topo, core, rank):
         else: act(A("Tf", u, u + K), IND(A("Lf"), off), ACT.Identity)
         ev, od = A("Tf", u, u + K, 2), A("Tf", u + 1, u + K, 2)
         mm(A("PL", 320, 400), [(A("W0", 8, 136), ev), (A("W0", 0, 128), od)])
-        mm(A("PL", 400, 480), [(A("W1", 16, 144), ev), (A("W1", 8, 136), od)])
-        tc(A("O16", u, u + K), A("PL", 320, 480))
+        mm(A("PV", 176, 256), [(A("W1", 16, 144), ev), (A("W1", 8, 136), od)])
+        tc(A("O16", u, u + 80), A("PL", 320, 400))
+        tc(A("O16", u + 80, u + K), A("PV", 176, 256))
 
     lists(0)
-    banks = ["PD0", "PD1", "PDI", "PS", "PE", "PK", "PV", "PD0", "PD1", "PDI"]
+    banks = ["PD0", "PD1", "PDI", "PS", "PE", "PK", "PV", "PL", "PD0", "PD1"]
     cuts = [0, 480, 960, 1440, 1920, 2400, 2880, 3120, 3360, 3600, 3840]
     for j in range(10):
         a, b = cuts[j], cuts[j + 1]
-        ps = A(banks[j], 0, b - a)
-        mm(ps, [(A("rhi", parts=33), A("rlo", 0, b - a, parts=33)), (A("Ip"), A("Xb", a, b))])
-        if j % 2 == 0: act(A("Xk", a, b), ps, ACT.Identity, bias=(KEY0 + a) / 65536.0)
+        ps = A(banks[j], 0, 480 if banks[j] in ("PV", "PL") else b - a)
+        ps["ap"], ps["n"] = A(banks[j], 0, b - a)["ap"], b - a
+        run(terms(ps, [(A("rhi", parts=33), A("rlo", 0, b - a, parts=33))], sp=False), ("key", j))
+        run(terms(ps, [(A("Ip"), A("Xb", a, b))], st=False), ("key", j))
+        if KEYQ[j] == "S": act(A("Xk", a, b), ps, ACT.Identity, bias=(KEY0 + a) / 65536.0)
         else: ts(A("Xk", a, b), ps, (KEY0 + a) / 65536.0, ALU.add)
-    ts(A("PV", K, K + 176), A("dg"), 255.5, ALU.add)
     tc(A("Q16"), A("Qi"))
     for j in range(2): tc(A("Lf", 512 * j, 512 * j + 512), A("Li", 512 * j, 512 * j + 512))
     for c in range(C): tc(A("S16", c * K, c * K + K), A("Si", c * K, c * K + K))
-    ts(A("thf", 0, 1), A("thi"), -4096.0, ALU.add)
-    tc(A("thf", 1, 2), A("thi"))
+    ts(A("thp", 0, 1), A("thi"), 63, ALU.bitwise_and)
+    ts(A("thp", 1, 2), A("thi"), 6, ALU.arith_shift_right)
+    tc(A("thf", 0, 2), A("thp"))
+    ts(A("thf", 2, 3), A("thp", 1, 2), -64.0, ALU.add)
+    for w in range(2): ts(A("Dh", 128 * w, 128 * w + 128), A("Ip"), A("thf", 2 - w, 3 - w), ALU.mult)
+    ts(A("Dl", 0, 128), A("Ip"), A("thf", 0, 1), ALU.mult)
+    ms(A("cn", 0, K), -8192.0)
+    ms(A("cn", K, 2 * K), -8192.0 * 64)
     tc(A("mgf", parts=8), A("mgi", parts=8))
     ts(A("mgr", 0, 128, parts=8), A("one", 0, 128, parts=8), A("mgf", parts=8), ALU.mult)
     ts(A("mgr", 128, K, parts=8), A("one", 0, K - 128, parts=8), A("mgf", parts=8), ALU.mult)
-    ts(A("bias", 0, 1), A("thf", 0, 1), -8192.0, ALU.mult)
     for a, b in ((960, 1440), (1600, 2240), (2400, 3040), (3360, 3840)):
         dma("Y", T.yx[:, a:b], A("Xb", a, b))["low"] = True
 
     last = {}
 
+    def paired(t):
+        return min([l0 for l0, l1, e in FARV[t] if e in "ar"] + [K])
+
+    def repeat(t):
+        l0, tag[0] = paired(t), "rep%d" % t
+        old = A("Bb", t * K + l0, t * K + K) if t < C else A("sb", (t - C) * K + l0, (t - C) * K + K)
+        for p in range(16 if l0 < K else 0):
+            out = A("rep", 1280 * t + p, 1280 * t + 16 * (K - l0), 16)
+            if REP[t] == "G": asel(out, old, [[0, K - l0]], 0, 0, ALU.is_ge)
+            else: tc(out, old)
+
     def far_gather(t):
         o = (t % C) * K
         for l0, l1, e in FARV[t]:
+            tag[0] = "far%d%s" % (t, e)
             out, src = A("far", 2560 * t + 16 * l0, 2560 * t + 16 * l1), IND(A("Xb"), A("S16", o + l0, o + l1))
             if e == "S": act(out, src, ACT.Identity)
             elif e == "V": tc(out, src)
             else:
-                r0, a0 = 1280 * (t - C) + 16 * (l0 - 80), 2560 * (t % 2) + 16 * l0
+                r0 = 1280 * t + 16 * (l0 - paired(t))
                 tt(out, src, A("rep", r0, r0 + 16 * (l1 - l0)), ALU.subtract)
-                if e == "a": act(A("ab", a0, a0 + 16 * (l1 - l0)), out, ACT.Abs)
-                else: ts(A("ab", a0, a0 + 16 * (l1 - l0)), out, 0.0, ALU.max)
 
     nch = [0]
 
-    def distances(t, old):
-        for h in ((0, 1) if t < C else (1, 0)):
-            ng[0] += 1
-            gid, f0, a0 = ng[0], 2560 * t + 1280 * h, 2560 * (t % 2) + 1280 * h
-            di = A("PDI", 80 * h, 80 * h + 80)
-            if FARV[t][-1][2] in "ar" and h == 1:
-                for l0, l1, e in FARV[t]:
-                    if e not in "ar": continue
-                    f0, a0, n = 2560 * t + 16 * l0, 2560 * (t % 2) + 16 * l0, 16 * (l1 - l0)
-                    terms = [(A("Zn", 15 - p, 143 - p), A("far", f0 + p, f0 + n, 16)) for p in range(16)] if e == "r" else []
-                    terms += [(A("Z2" if e == "r" else "Z", 15 - p, 143 - p), A("ab", a0 + p, a0 + n, 16)) for p in range(16)]
-                    mm(A("PDI", l0, l1), terms)
-                act(di, di, ACT.Identity, bias=A("bias", t, t + 1), scale=8192.0)
-                continue
-            for p0, p1 in PCH:
-                bank = "PD%d" % (nch[0] % 2)
-                nch[0] += 1
-                for p in range(p0, p1):
-                    mm(A(bank, 80 * (p - p0), 80 * (p - p0 + 1)),
-                       [(A("In"), A(old[0], old[1] + 80 * h, old[1] + 80 * h + 80)), (A("Ip"), A("far", f0 + p, f0 + 1280, 16))])
-                act(A("ab", a0 + 80 * p0, a0 + 80 * p1), A(bank, 0, 80 * (p1 - p0)), ACT.Abs)
-                for p in range(p0, p1):
-                    mm1(di, A("Z", 15 - p, 143 - p), A("ab", a0 + 80 * p, a0 + 80 * p + 80), p == 0, p == 15 and t >= C, gid)
-            if t < C:
-                mm1(di, A("I12"), A("sg", t * K + 80 * h, t * K + 80 * h + 80), False, True, gid)
-            else:
-                act(di, di, ACT.Identity, bias=A("bias", t, t + 1), scale=8192.0)
-        if t < C: act(A("PDI", 0, K), A("PDI", 0, K), ACT.Identity, bias=A("bias", t, t + 1), scale=8192.0)
+    def lapse(t, l0=0, l1=K):
+        return A("PDI", (t % 3) * K + l0, (t % 3) * K + l1) if t < C else A("PK", 2 * K + l0, 2 * K + l1)
 
-    def keys(t, own, n0, told, n1):
+    def distances(t, old):
+        lp, w = paired(t), 128 * (t >= C)
+        cut = [0, lp] if lp <= 102 else [0, lp // 2, lp]
+        segs = [(cut[j], cut[j + 1], "p") for j in range(len(cut) - 1)]
+        rs = [(lp, K, FARV[t][-1][2])] if lp < K else []
+        for l0, l1, e in (segs + rs if t < C else rs + segs):
+            tag[0] = "dist%d%s" % (t, e)
+            gid, f0, a0, n = (t, l0), 2560 * t + 16 * l0, 2560 * (t % 3) + 16 * l0, l1 - l0
+            di = lapse(t, l0, l1)
+            den = [(A("Dh", w, w + 128), A("cn", K, K + n)), (A("Dl", 128 * t, 128 * t + 128), A("cn", 0, n))]
+            if t < C: den += [(A("P25"), A("sg", t * K + l0, t * K + l1))]
+            if e in "ar":
+                pairs = []
+                if e == "r":
+                    for m0, m1, e2 in FARV[t]:
+                        if e2 == "r": ts(A("ab", a0 + 16 * (m0 - l0), a0 + 16 * (m1 - l0)), A("far", f0 + 16 * (m0 - l0), f0 + 16 * (m1 - l0)), 0.0, ALU.max)
+                    pairs = [(A("Zn", 15 - p, 143 - p), A("far", f0 + p, f0 + 16 * n, 16)) for p in range(16)]
+                else:
+                    act(A("ab", a0, a0 + 16 * n), A("far", f0, f0 + 16 * n), ACT.Abs)
+                more = [(A("Z2" if e == "r" else "Z", 15 - p, 143 - p), A("ab", a0 + p, a0 + 16 * n, 16)) for p in range(16)]
+                runs(terms(di, pairs + more + den if t < C else pairs + den + more), gid)
+            else:
+                nb = -(-16 // (512 // n))
+                for j in range(nb):
+                    p0, p1 = 16 * j // nb, 16 * (j + 1) // nb
+                    bank = "PD%d" % (nch[0] % 2)
+                    nch[0] += 1
+                    items = []
+                    for p in range(p0, p1):
+                        items += terms(A(bank, n * (p - p0), n * (p - p0 + 1)),
+                                       [(A("In"), A(old[0], old[1] + l0, old[1] + l1)), (A("Ip"), A("far", f0 + p, f0 + 16 * n, 16))])
+                    runs(items)
+                    act(A("ab", a0 + n * p0, a0 + n * p1), A(bank, 0, n * (p1 - p0)), ACT.Abs)
+                    pairs = [(A("Z", 15 - p, 143 - p), A("ab", a0 + n * p, a0 + n * p + n)) for p in range(p0, p1)]
+                    if t >= C: runs(terms(di, (den if p0 == 0 else []) + pairs, p0 == 0, p1 == 16), gid)
+                    else: runs(terms(di, pairs + (den if p1 == 16 else []), p0 == 0, p1 == 16), gid)
+
+    def keys(t, own, n0, n1):
         ps = A("PK", 0, K)
         mm(ps, [(CR(7), LO), (A("Ip"), own)])
         act(A("Xk", n0, n0 + K), ps, ACT.Identity, bias=(KEY0 + n0) / 65536.0)
         ps = A("PK", K, 2 * K)
         mm(ps, [(CR(8), R1), (CR(9 + t), R1), (CR(7), LO)])
-        for l0, l1 in PARTS[t]:
-            tt(A("Xk", n1 + l0, n1 + l1), A("land", t * K + l0, t * K + l1), A("PK", K + l0, K + l1), ALU.add)
+        tt(A("Xk", n1, n1 + K), A("land", t * K, t * K + K), ps, ALU.add)
 
     def sources(t):
         c = t % C
-        o = c * K
+        o, q = c * K, (t % 3) * K
         be, xf, Rk = A("Bb", o, o + K), A("sb", t * K, t * K + K), A("R", 1280 * t + 7, 1280 * t + 1280, 8)
-        G2, sa, sz = A("PS", 0, K), A("sa", t * K, t * K + K), A("sz", t * K, t * K + K)
+        sa, sz, di = A("sa", t * K, t * K + K), A("sz", t * K, t * K + K), lapse(t)
         if t < C:
+            G2 = A("PS", 0, K)
             distances(t, ("Bb", o))
+            tag[0] = "src%d" % t
             mm(G2, [(A("P25"), xf), (A("N25"), be), (CR(0), LO), (CR(2 + c), R1)])
-            tt(sa, A("PDI", 0, K), A("Si", o, o + K), ALU.max)
+            tt(sa, di, A("Si", o, o + K), ALU.max)
             tt(G2, sa, G2, ALU.min)
         else:
-            G3 = A("PS", K, 2 * K)
+            G2, G3, tag[0] = A("PS", 2 * K, 3 * K), A("PS", K, 2 * K), "src%d" % t
             mm(G3, [(CR(0), LO), (CR(2 + c), R1)])
             tt(A("x1"), xf, X1, ALU.subtract)
             mm(G2, [(CR(6), R1), (A("P25"), A("x1"))])
-            tt(sa, A("PDI", 0, K), A("Si", o, o + K), ALU.max)
+            tt(sa, di, A("Si", o, o + K), ALU.max)
             tt(A("sa2"), sa, A("PE", 0, K), ALU.max)
             tt(sa, A("sa2"), G3, ALU.min)
             tt(G2, sa, G2, ALU.min)
@@ -317,112 +362,112 @@ def plan(T, g, topo, core, rank):
             tc(A("Sf", o, o + K), A("Si", o, o + K))
             dma("Y", T.ys[:, o:o + K], A("Sf", o, o + K))
 
+    for t in range(C): repeat(t)
     for t in range(RO):
         c = t % C
-        o, f, d, u = c * K, c ^ 1, 1 + t % (N - 1), (t % 2) * K
+        o, f, d, u, q = c * K, c ^ 1, 1 + t % (N - 1), (t % 2) * K, (t % 3) * K
         ys0, r0 = 1280 * (t % 2), 1280 * t
-        be, xf = A("Bb", o, o + K), A("sb", t * K, t * K + K)
-        bP, E, Tf = A("PV", 0, K), A("PE", 0, K), A("Tf", u, u + K)
-        Rk = A("R", r0 + 7, r0 + 1280, 8)
-        prev = None
+        be, xf, ld = A("Bb", o, o + K), A("sb", t * K, t * K + K), A("land", t * K, t * K + K)
+        bP, E, Tf, mi, xx, uu = A("PV", 0, K), A("PE", 0, K), A("Tf", u, u + K), A("mi"), A("xx"), A("uu")
+        prev, tag[0] = None, None
         for l0, l1 in YCH[t]:
-            op = act(A("YS", ys0 + 8 * l0, ys0 + 8 * l1), IND(A("Xk"), A("O16", u + l0 // 2, u + l1 // 2)), ACT.Identity, bias=-0.5)
-            op["after"] = prev
-            prev = op
+            low, src = A("YS", ys0 + 8 * l0, ys0 + 8 * l1), IND(A("Xk"), A("O16", u + l0 // 2, u + l1 // 2))
+            if l1 <= SELF[t]:
+                ts(low, src, -0.5, ALU.add)
+            else:
+                op = act(low, src, ACT.Identity, bias=-0.5)
+                op["after"] = prev
+                prev = op
             tt(A("YV", 8 * l0, 8 * l1), IND(A("Xk"), A("O16", u + 80 + l0 // 2, u + 80 + l1 // 2)), A("YS", ys0 + 8 * l0, ys0 + 8 * l1), ALU.min)
             scan(A("R", r0 + 8 * l0, r0 + 8 * l1), A("D0c", 0, 8 * (l1 - l0)), A("YV", 8 * l0, 8 * l1))
         mm(bP, [(A("Ip"), be)])
         if t >= C:
             far_gather(t)
             distances(t, ("sb", last[c] * K))
-        dst = T.cores[(rank + d) % N]
-        ld = A("land", t * K, t * K + K)
-        for part in range(len(PARTS[t])):
-            l0, l1 = PARTS[t][part]
-            mi, xx, uu, bl, El = A("mi", l0, l1), A("xx", l0, l1), A("uu", l0, l1), A("PV", l0, l1), A("PE", l0, l1)
-            ts(mi, A("R", r0 + 8 * l0 + 7, r0 + 8 * l1, 8), 255.502, ALU.add)
-            if t < C:
-                tt(xx, mi, bl, ALU.min)
-            else:
-                tt(A("x1a", l0, l1), A("PDI", l0, l1), A("sb", last[c] * K + l0, last[c] * K + l1), ALU.max)
-                tt(A("PV", 336 + l0, 336 + l1), A("x1a", l0, l1), bl, ALU.min)
-                tt(xx, mi, A("PV", 336 + l0, 336 + l1), ALU.min)
-            terms = [(A("Gt", parts=8), A("mgr", l0, l1, parts=8)), (A("Bp"), A("Bb", o + l0, o + l1))]
-            if f in last:
-                terms += [(A("Bn"), A("Bb", f * K + l0, f * K + l1)), (A("Bp"), A("sb", last[f] * K + l0, last[f] * K + l1))]
-            mm(El, terms + [(A("Bn"), xx)])
-            tt(uu, El, xx, ALU.max)
-            out, far_end = A("sb", t * K + l0, t * K + l1), A("land", t * K + l0, t * K + l1)
-            tt(out, uu, bl, ALU.min)
+        tag[0] = None
+        ts(mi, A("R", r0 + 7, r0 + 1280, 8), 255.502, ALU.add)
+        if t < C:
+            tt(xx, mi, bP, ALU.min)
+        else:
+            tt(A("x1a"), lapse(t), A("sb", last[c] * K, last[c] * K + K), ALU.max)
+            tt(X1, A("x1a"), bP, ALU.min)
+            tt(xx, mi, X1, ALU.min)
+        pairs = [(A("Gt", parts=8), A("mgr", parts=8)), (A("Bp"), be)]
+        if f in last:
+            pairs += [(A("Bn"), A("Bb", f * K, f * K + K)), (A("Bp"), A("sb", last[f] * K, last[f] * K + K))]
+        run(terms(E, pairs[:1], sp=False), ("E", t))
+        run(terms(E, pairs[1:], st=False, sp=False), ("E", t))
+        run(terms(E, [(A("Bn"), xx)], st=False), ("E", t))
+        tt(uu, E, xx, ALU.max)
+        tt(xf, uu, bP, ALU.min)
 
-            def send(k=2 * t + part, dst=dst, out=out, far_end=far_end):
-                rid, pid, _ = topo.addr(dst)
-                return g.remote_dma(far_end["ap"], out["ap"], T.sem["arr%d" % k], T.sem.sent, pid, rid, topo.mask(core, dst))
-            op = add("G", send, (900 + 3 * (l1 - l0) + (1500 if t + part == 0 else 0), 0, 0, 0, 0), [out], [far_end], kind="r", lat=-1080.0)
-            op["t"] = 2 * t + part
-            op["out"] = len(topo.engines(core, dst))
-            op["in"] = len(topo.engines(T.cores[(rank - d) % N], core))
-        act(A("LQ"), IND(A("Lf"), A("Q16", 10 * c, 10 * c + 10)), ACT.Identity, scale=2.0 ** -12)
+        def send(t=t, dst=T.cores[(rank + d) % N], xf=xf, ld=ld):
+            rid, pid, _ = topo.addr(dst)
+            return g.remote_dma(ld["ap"], xf["ap"], T.sem["arr%d" % t], T.sem.sent, pid, rid, topo.mask(core, dst))
+        op = add("G", send, (800 + (1300 if t == 0 else 0), 0, 0, 0, 0), [xf], [ld], kind="r")
+        op["t"] = t
+        op["out"] = len(topo.engines(core, T.cores[(rank + d) % N]))
+        op["in"] = len(topo.engines(T.cores[(rank - d) % N], core))
+        tag[0] = "sel%d" % t
         mm(A("PL", 0, K), [(A("B2"), A("YS", ys0, ys0 + 1280, 8))])
-        ts(A("hi"), A("PL", 0, K), A("pc", 3, 4), ALU.add)
-        ts(A("hr"), A("hi"), 15, ALU.bitwise_and)
-        tt(A("sel"), A("LQ"), A("hr"), ALU.max)
-        mm(A("PL", K, 2 * K), [(CR(1), R1), (A("Inf"), Tf), (A("Bs"), A("sel"))])
-        tt(A("dl"), A("uu"), A("PV", K + t, 2 * K + t), ALU.is_gt)
+        ts(A("hi"), A("PL", 0, K), A("pc", 3, 4), ALU.add, 4096.0, ALU.mult)
+        ts(A("hr"), A("hi"), 15 * 4096, ALU.bitwise_and)
+        tt(A("sel"), IND(A("Lf"), A("Q16", 10 * c, 10 * c + 10)), A("hr"), ALU.max)
+        run(terms(A("PL", K, 2 * K), [(CR(1), R1), (A("Inf"), Tf)], sp=False), ("L", t))
+        run(terms(A("PL", K, 2 * K), [(A("B2"), A("sel"))], st=False), ("L", t))
+        tag[0] = None
+        tt(A("dl"), E, A("dg", t, K + t), ALU.is_gt)
         tt(A("dv"), A("PL", K, 2 * K), A("dl"), ALU.mult)
         tt(IND(A("Lf"), A("P16", 10 * c, 10 * c + 10)), Tf, A("dv"), ALU.add)
         if t < RO - 1:
             lists(t + 1)
-            keys(t, xf, o, ld, d * V_ + o)
-            act(A("sg", t * K, t * K + K), A("uu"), ACT.Sign, bias=-255.5, accum=A("acc", t, t + 1))
+            keys(t, xf, o, d * V_ + o)
+            tag[0] = "cnt%d" % t
+            act(A("sg", t * K, t * K + K), uu, ACT.Sign, bias=-255.5, accum=A("acc", t, t + 1))
             ts(A("Ai", t, t + 1), A("acc", t, t + 1), 0.5, ALU.mult, A("Af", t, t + 1), ALU.add)
             if t < RO - 2: ts(A("Af", t + 1, t + 2), A("Ai", t, t + 1), 80.0, ALU.add)
             ts(A("Am", t, t + 1), A("Ai", t, t + 1), 31, ALU.bitwise_and)
-            w = 0 if t + 1 < C else 1
-            ts(A("bias", t + 1, t + 2), A("Am", t, t + 1), A("thf", w, w + 1), ALU.add, -8192.0, ALU.mult)
+            ts(A("bias", t + 1, t + 2), A("Am", t, t + 1), A("thf", 0, 1), ALU.add)
+            ts(A("Dl", 128 * t + 128, 128 * t + 256), A("Ip"), A("bias", t + 1, t + 2), ALU.mult)
         else:
             for j in range(2):
-                dma("YS"[j], T.yl[:, 512 * j:512 * j + 512], A("Lf", 512 * j, 512 * j + 512))
+                dma("YS"[j], T.yl[:, 512 * j:512 * j + 512], A("Lf", 512 * j, 512 * j + 512))["lat"] += 512 * 512 / DBW
+        if t + C < RO: repeat(t + C)
         if t < C: far_gather(t)
         else: sources(t)
-        if t + C < RO and FARV[t + C][-1][2] in "ar":
-            for p in range(16): tc(A("rep", 1280 * t + p, 1280 * t + 1280, 16), A("sb", t * K + 80, t * K + K))
         for t2 in range(C):
             if LAG[t2] == t: sources(t2)
+        tag[0] = None
         if t + C >= RO: dma("Y", T.yx[:, o:o + K], xf)
-        for l0, l1 in (PARTS[t] if t == RO - 1 else [(0, K)]):
-            dma("Y", T.yx[:, d * V_ + o + l0:d * V_ + o + l1], A("land", t * K + l0, t * K + l1))
+        dma("Y", T.yx[:, d * V_ + o:d * V_ + o + K], ld)
         if t < RO - 1:
             if t < C - 1:
                 dma("Y", A("Xb", o, o + K), xf)
                 dma("Y", A("Xb", d * V_ + o, d * V_ + o + K), ld)
             else:
                 tc(A("Xb", o, o + K), xf)
-                for l0, l1 in PARTS[t]:
-                    tc(A("Xb", d * V_ + o + l0, d * V_ + o + l1), A("land", t * K + l0, t * K + l1))
+                tc(A("Xb", d * V_ + o, d * V_ + o + K), ld)
         last[c] = t
     return ops
 
 
 def depend(ops):
-    seen = {}
+    seen, held = {}, {}
     for op in ops:
-        deps = {op["after"]["id"]: False} if op.get("after") else {}
-        for acc, write in [(a, False) for a in op["rd"]] + [(a, True) for a in op["wr"]]:
+        deps = {op["after"]["id"]: False} if op["after"] else {}
+        touch = [(a, False) for a in op["rd"]] + [(a, True) for a in op["wr"]]
+        if op["eng"] == "T" and op["wr"][0]["buf"] in ("PDI", "PE", "PK", "PL"):
+            if op["wr"][0]["buf"] in held: deps[held[op["wr"][0]["buf"]]] = False
+            held[op["wr"][0]["buf"]] = op["id"]
+        for acc, write in touch:
             for o2, a2, w2 in seen.get(acc["buf"], []):
-                if o2 is op: continue
-                hit = (write or w2) and acc["lo"] < a2["hi"] and a2["lo"] < acc["hi"]
-                if acc["buf"] == "rep" and write and w2: hit = False
-                if acc["ps"] and (o2["eng"] != op["eng"] or op["eng"] == "T"):
-                    if not hit and op["eng"] == o2["eng"]:
-                        deps.setdefault(o2["id"], False)
-                        continue
-                    hit = True
-                if hit:
-                    soft = op["eng"] == "T" and o2["eng"] == "T" and acc["ps"]
-                    deps[o2["id"]] = deps.get(o2["id"], False) or not soft
+                if not ((write or w2) and acc["lo"] < a2["hi"] and a2["lo"] < acc["hi"]): continue
+                if acc["buf"] == "rep" and write and w2: continue
+                soft = op["eng"] == "T" and o2["eng"] == "T" and acc["ps"]
+                deps[o2["id"]] = deps.get(o2["id"], False) or not soft
         op["deps"] = deps
-        for acc, write in [(a, False) for a in op["rd"]] + [(a, True) for a in op["wr"]]:
+        op["banks"] = sorted(set(a["buf"] for a, w in touch if a["ps"]))
+        for acc, write in touch:
             seen.setdefault(acc["buf"], []).append((op, acc, write))
 
 
@@ -438,132 +483,152 @@ def tables(ops):
     for cyc, ga, sc, pe, hop, own, rem in TIMES:
         cost = [c[0] + cyc * (c[1] + ga * c[2] + sc * c[3]) + pe * c[4] for c in [op["cost"] for op in ops]]
         lat = [op["lat"] + (rem if op["kind"] == "r" else 0.0) for op in ops]
-        pre, suc = [], [[] for op in ops]
+        pre = []
         for op in ops:
             row = []
             for j in red[op["id"]]:
                 p = ops[j]
-                w = lat[j] + (own if p["eng"] == op["eng"] and p["kind"] == "c" else hop) if op["deps"][j] else 0.0
-                row.append((j, w))
-                suc[j].append((op["id"], w))
+                row.append((j, lat[j] + (own if p["eng"] == op["eng"] and p["kind"] == "c" else hop) if op["deps"][j] else 0.0))
             pre.append(row)
-        out.append((cost, lat, pre, suc))
+        out.append((cost, lat, pre, hop))
     return out
 
 
-def place(eng, first, cost, edges, rank):
-    busy = {e: [] for e in "VSTGY"}
-    t1 = [0.0] * len(cost)
-    for i in rank:
-        t0, c = first[i], cost[i]
-        for j, w in edges[i]:
-            if t1[j] + w > t0: t0 = t1[j] + w
-        lst = busy[eng[i]]
-        pos = n = len(lst)
-        while pos and lst[pos - 1][1] > t0: pos -= 1
-        while pos < n and t0 + c > lst[pos][0]:
-            if lst[pos][1] > t0: t0 = lst[pos][1]
-            pos += 1
-        lst.insert(pos, (t0, t0 + c))
-        t1[i] = t0 + c
-    return t1
-
-
-def play(eng, first, tab, seq):
-    cost, lat, pre, suc = tab
-    free = {e: 0.0 for e in "VSTGY"}
-    t1 = [0.0] * len(cost)
+def play(ops, tab, seq):
+    cost, lat, pre, hop = tab
+    n = len(cost)
+    t1, why = [0.0] * n + [-1e9], [None] * n
+    front = {e: n for e in "VSTGY"}
+    bank = {b: {} for b in SCRATCH if SCRATCH[b][0] == "psum"}
     end = 0.0
     for i in seq:
-        t = free[eng[i]]
-        if first[i] > t: t = first[i]
+        e, t, banks = ops[i]["key"]
+        y, j = None, front[e]
+        if t1[j] > t: t, y = t1[j], j
+        for b in banks:
+            held = bank[b]
+            for e2, j in held.items():
+                if e2 != e and t1[j] + hop > t: t, y = t1[j] + hop, j
+            held[e] = i
         for j, w in pre[i]:
-            if t1[j] + w > t: t = t1[j] + w
+            if t1[j] + w >= t: t, y = t1[j] + w, -1 - j
         t += cost[i]
-        t1[i] = free[eng[i]] = t
+        t1[i], why[i], front[e] = t, y, i
         if t + lat[i] > end: end = t + lat[i]
-    return end, t1
+    return end, t1, why
+
+
+def clash(ops, seq):
+    lock = {}
+    for i in seq:
+        op = ops[i]
+        if op["eng"] != "T": continue
+        for b in op["banks"]:
+            if lock.get(b) not in (None, op["grp"]): return True
+            lock[b] = None if op["shut"] else op["grp"]
+    return False
+
+
+def place(ops, first, cost, edges, hop, rank):
+    busy = {e: [] for e in "VSTGY"}
+    bank = {b: [] for b in SCRATCH if SCRATCH[b][0] == "psum"}
+    t1 = [0.0] * len(cost)
+    for i in rank:
+        t0, c, e, banks = first[i], cost[i], ops[i]["eng"], ops[i]["banks"]
+        for j, w in edges[i]:
+            if t1[j] + w > t0: t0 = t1[j] + w
+        lst = busy[e]
+        moved = True
+        while moved:
+            pos = n = len(lst)
+            while pos and lst[pos - 1][1] > t0: pos -= 1
+            while pos < n and t0 + c > lst[pos][0]:
+                if lst[pos][1] > t0: t0 = lst[pos][1]
+                pos += 1
+            moved = False
+            for b in banks:
+                held = bank[b]
+                k = len(held)
+                while k and held[k - 1][0] > t0 - 1500.0:
+                    k -= 1
+                    s2, f2, e2 = held[k]
+                    if e2 != e and t0 < f2 + hop and s2 < t0 + c + hop: t0, moved = f2 + hop, True
+        lst.insert(pos, (t0, t0 + c))
+        for b in banks:
+            held = bank[b]
+            k = len(held)
+            while k and held[k - 1][0] > t0: k -= 1
+            held.insert(k, (t0, t0 + c, e))
+        t1[i] = t0 + c
+    return t1
 
 
 def order(ops):
     if "seq" not in KEPT:
         n = len(ops)
+        for op in ops:
+            op["first"] = 9000.0 if op.get("low") else 0.0
+            op["key"] = (op["eng"], op["first"], op["banks"])
         tabs = tables(ops)
-        eng = [op["eng"] for op in ops]
-        first = [9000.0 if op.get("low") else 0.0 for op in ops]
-        cost, lat, pre, suc = tabs[0]
+        cost, lat, pre, hop = tabs[0]
+        suc = [[] for op in ops]
+        for i in range(n):
+            for j, w in pre[i]: suc[j].append((i, w))
 
-        def judge(pr):
-            t1 = place(eng, first, cost, pre, sorted(range(n), key=lambda i: (pr[i], i)))
-            t0 = [t1[i] - cost[i] for i in range(n)]
-            seq = sorted(range(n), key=lambda i: (t0[i], i))
-            ends = [play(eng, first, tab, seq)[0] for tab in tabs]
-            return sum(ends), t0, seq, ends
+        def urge(due):
+            way = [cost[i] + max(lat[i], due.get(ops[i]["tag"], 0.0)) for i in range(n)]
+            for i in reversed(range(n)):
+                for j, w in pre[i]: way[j] = max(way[j], cost[j] + w + way[i])
+            return [-x for x in way]
 
-        bl = [cost[i] + lat[i] for i in range(n)]
-        for i in reversed(range(n)):
-            for j, w in pre[i]: bl[j] = max(bl[j], cost[j] + w + bl[i])
-        pr = [-b for b in bl]
-        best = None
-        for it in range(PASSES):
-            cur = judge(pr)
-            if best is None or cur[0] < best[0]: best = (cur[0], pr, cur[2], cur[3])
-            back = place(eng, lat, cost, suc, sorted(range(n), key=lambda i: (-cur[1][i] - cost[i], -i)))
-            pr = [-b for b in back]
-        pick = [i for i in range(n) if eng[i] in "VS"] * 3 + list(range(n))
-        z = SEED
-        now = best
-        for it in range(MOVES):
-            pr = list(now[1])
-            for rep in range(1 + it % 2):
-                z = (z * 6364136223846793005 + 1442695040888963407) % (1 << 64)
-                i = pick[(z >> 33) % len(pick)]
-                step = ((z >> 13) % 2001 - 1000) / 1000.0
-                pr[i] += step * (400.0, 1500.0, 5000.0)[(z >> 28) % 3]
-                todo = [i]
-                while todo:
-                    a = todo.pop()
-                    for j, w in (pre[a] if step < 0 else suc[a]):
-                        if step < 0 and pr[j] >= pr[a]:
-                            pr[j] = pr[a] - 1.0
-                            todo.append(j)
-                        elif step >= 0 and pr[j] <= pr[a]:
-                            pr[j] = pr[a] + 1.0
-                            todo.append(j)
-            cur = judge(pr)
-            if cur[0] <= now[0] + SLACK * (1.0 - it / MOVES):
-                now = (cur[0], cur[1] if it % RESET else pr, cur[2], cur[3])
-                if cur[0] < best[0]: best = now
+        def judge(seq, most=1e18):
+            ends = []
+            for tab in tabs:
+                ends.append(play(ops, tab, seq)[0])
+                if ends[0] > most: return 1e18, seq, ends
+            return (1e18 if clash(ops, seq) else sum(ends)), seq, ends
+
+        def pack(pr):
+            t1 = place(ops, [op["first"] for op in ops], cost, pre, hop, sorted(range(n), key=lambda x: (pr[x], x)))
+            return t1, sorted(range(n), key=lambda x: (t1[x] - cost[x], x))
+
+        def repack(pr):
+            t1 = pack(pr)[0]
+            back = place(ops, lat, cost, suc, hop, sorted(range(n), key=lambda x: (-t1[x], -x)))
+            return [-x for x in back]
+
+        due, z = dict(DUE), SEED
+        tags = sorted(set(op["tag"] for op in ops if op["tag"]))
+        best = judge(pack(urge(due))[1])
+        for it in range(SHIFTS):
+            z = (z * 6364136223846793005 + 1442695040888963407) % (1 << 64)
+            tg = tags[(z >> 33) % len(tags)]
+            pr = urge(due)
+            was = max(due.get(tg, 0.0), min(-pr[i] - cost[i] for i in range(n) if ops[i]["tag"] == tg))
+            new = dict(due)
+            new[tg] = was + ((z >> 13) % 2001 - 900) / 1000.0 * (500.0, 2000.0, 6000.0)[(z >> 28) % 3]
+            cur = judge(pack(urge(new))[1])
+            if cur[0] <= best[0]: best, due = cur, new
+        KEPT["due"], KEPT["log"] = due, [int(best[0] / 3)]
         now = best
         for it in range(SWAPS):
             z = (z * 6364136223846793005 + 1442695040888963407) % (1 << 64)
-            seq = now[2]
-            c, la, pr_, su_ = tabs[(z >> 50) % len(tabs)]
-            t1 = play(eng, first, (c, la, pr_, su_), seq)[1]
-            front, lastof = {}, {}
-            for i in seq:
-                front[i] = lastof.get(eng[i])
-                lastof[eng[i]] = i
-            i = max(range(n), key=lambda a: t1[a] + la[a])
+            seq, tab = now[1], tabs[(z >> 50) % len(tabs)]
+            end, t1, why = play(ops, tab, seq)
+            i = max(range(n), key=lambda a: t1[a] + tab[1][a])
             pairs = []
-            while i is not None:
-                s0, nxt = t1[i] - c[i], None
-                for j, w in pr_[i]:
-                    if t1[j] + w >= s0 - 1e-6: nxt = j
-                if nxt is None and front[i] is not None and t1[front[i]] >= s0 - 1e-6:
-                    nxt = front[i]
-                    pairs.append((nxt, i))
-                i = nxt
+            while why[i] is not None:
+                j = why[i]
+                if j >= 0 and t1[j] > 0: pairs.append((j, i))
+                i = j if j >= 0 else -1 - j
             if not pairs: continue
             a, b = pairs[(z >> 20) % len(pairs)]
             pr = [0.0] * n
             for pos in range(n): pr[seq[pos]] = float(pos)
-            early = (z >> 10) & 1
-            for rep in range((z >> 12) % 3 if (z >> 16) & 1 else 0):
-                if early and front[a] is not None: a = front[a]
-            if early: pr[b] = pr[a] - 0.5
-            else: pr[a] = pr[b] + 0.5 + ((z >> 12) % 40 if (z >> 16) & 1 else 0)
-            todo = [b if early else a]
+            early, far = (z >> 10) & 1, (z >> 12) % REACH[(z >> 44) % len(REACH)]
+            x = b if early else a
+            pr[x] = pr[a] - 0.5 - far if early else pr[b] + 0.5 + far
+            todo = [x]
             while todo:
                 x = todo.pop()
                 for j, w in (pre[x] if early else suc[x]):
@@ -573,25 +638,30 @@ def order(ops):
                     elif not early and pr[j] <= pr[x]:
                         pr[j] = pr[x] + 1e-4
                         todo.append(j)
-            seq = sorted(range(n), key=lambda x: (pr[x], x)) if (z >> 40) % 4 >= PACK else judge(pr)[2]
-            plays = [play(eng, first, tab, seq) for tab in tabs]
-            tot = sum(p[0] for p in plays)
-            if tot <= now[0] + SLACK * (1.0 - it / SWAPS):
-                t1 = plays[0][1]
-                seq = sorted(range(n), key=lambda x: (t1[x] - cost[x], pr[x]))
-                now = (tot, None, seq, [p[0] for p in plays])
-                if tot < best[0]: best = now
-        KEPT["seq"], KEPT["ends"] = best[2], best[3]
+            how = (z >> 40) % 8
+            if how >= PACK: cur = judge(sorted(range(n), key=lambda x: (pr[x], x)), now[2][0] + 600.0)
+            else: cur = judge(pack(repack(pr) if how == 0 else pr)[1], now[2][0] + 600.0)
+            if cur[0] <= now[0] + SLACK * (1.0 - it / SWAPS):
+                t1 = play(ops, tabs[0], cur[1])[1]
+                spot = {cur[1][pos]: pos for pos in range(n)}
+                again = judge(sorted(range(n), key=lambda x: (t1[x] - cost[x], spot[x])))
+                now = again if again[0] <= cur[0] else cur
+                if now[0] < best[0]: best = now
+        KEPT["seq"], KEPT["ends"] = best[1], best[2]
     return [ops[i] for i in KEPT["seq"]]
 
 
 def emit(seq, ops, g, T):
     q = {"V": g.vector, "S": g.scalar, "T": g.tensor, "G": g, "Y": g.sync}
-    for op in ops: op["sig"] = op["kind"] != "c"
-    rankq = {}
+    rankq, bank = {}, {}
     for op in seq:
+        op["sig"] = op["kind"] != "c"
         rankq[op["eng"]] = rankq.get(op["eng"], 0) + 1
         op["pos"] = rankq[op["eng"]]
+        for b in op["banks"]:
+            for e2, j in bank.get(b, {}).items():
+                if e2 != op["eng"]: op["deps"][j] = True
+            bank.setdefault(b, {})[op["eng"]] = op["id"]
     for op in seq:
         best = {}
         op["need"] = []

@@ -15,7 +15,7 @@ SCRATCH = {
     "P16": ("sbuf", [128, 40], U16), "Q16": ("sbuf", [128, 40], U16),
     "thi": ("sbuf", [128, 1], I32), "mgi": ("sbuf", [128, 1], I32), "mgf": ("sbuf", [128, 1], F32),
     "thp": ("sbuf", [128, 2], I32), "Dh": ("sbuf", [128, 256], BF), "Dl": ("sbuf", [128, RO * 128], BF), "cn": ("sbuf", [128, 2 * K], BF),
-    "thf": ("sbuf", [128, 3], F32), "mgr": ("sbuf", [128, K], F32),
+    "thf": ("sbuf", [128, 4], F32), "mgr": ("sbuf", [128, K], F32),
     "YS": ("sbuf", [128, 2 * 1280], F32), "YV": ("sbuf", [128, 1280], F32), "R": ("sbuf", [128, RO * 1280], F32),
     "D0c": ("sbuf", [128, 1280], BF),
     "far": ("sbuf", [128, RO * 2560], BF), "ab": ("sbuf", [128, 3 * 2560], BF),
@@ -24,7 +24,7 @@ SCRATCH = {
     "mi": ("sbuf", [128, K], I32), "xx": ("sbuf", [128, K], BF), "uu": ("sbuf", [128, K], BF),
     "x1a": ("sbuf", [128, K], BF), "x1": ("sbuf", [128, K], BF),
     "sg": ("sbuf", [128, RO * K], BF), "acc": ("sbuf", [128, 8], F32),
-    "Ai": ("sbuf", [128, 8], I32), "Am": ("sbuf", [128, 8], I32), "Af": ("sbuf", [128, 8], F32), "bias": ("sbuf", [128, 8], F32),
+    "cnt": ("sbuf", [128, 6 * RO], F32), "Lj": ("sbuf", [128, 10], I32), "L16": ("sbuf", [128, 10], U16),
     "hi": ("sbuf", [128, K], I32), "hr": ("sbuf", [128, K], I32), "sel": ("sbuf", [128, K], F32),
     "dl": ("sbuf", [128, K], F32), "dv": ("sbuf", [128, K], F32),
     "sa": ("sbuf", [128, RO * K], F32), "sa2": ("sbuf", [128, K], F32), "sz": ("sbuf", [128, RO * K], I32),
@@ -33,36 +33,63 @@ SCRATCH = {
     "P25": ("sbuf", [128, 128], BF), "N25": ("sbuf", [128, 128], BF), "Inf": ("sbuf", [128, 128], F32),
     "B1": ("sbuf", [128, 128], F32), "B2": ("sbuf", [128, 128], F32), "Bp": ("sbuf", [128, 128], BF), "Bn": ("sbuf", [128, 128], BF),
     "Z": ("sbuf", [128, 144], BF),
-    "G1": ("sbuf", [128, 128], F32), "G2s": ("sbuf", [128, 128], F32), "Gt": ("sbuf", [128, 128], F32),
-    "rlo": ("sbuf", [128, 480], BF), "rhi": ("sbuf", [128, 128], BF), "r1": ("sbuf", [128, K], BF), "cr": ("sbuf", [128, 14 * 128], BF),
-    "Z2": ("sbuf", [128, 144], BF), "Zn": ("sbuf", [128, 144], BF), "rep": ("sbuf", [128, RO * 1280], BF),
+    "Gt": ("sbuf", [128, 128], F32), "ef": ("sbuf", [128, 2 * K], F32), "X4": ("sbuf", [128, W_], BF), "X5": ("sbuf", [128, W_], BF),
+    "rlo": ("sbuf", [128, 512], BF), "rhi": ("sbuf", [128, 128], BF), "r1": ("sbuf", [128, 416], BF), "cr": ("sbuf", [128, 16 * 128], BF),
+    "Z2": ("sbuf", [128, 144], BF), "Zn": ("sbuf", [128, 144], BF), "rep": ("sbuf", [128, 16 * 800], BF),
     "c2": ("sbuf", [128, RO * K], F32),
     "pi": ("sbuf", [128, 1], I32), "pm": ("sbuf", [128, 1], I32), "pc": ("sbuf", [128, 4], F32),
     "jm": ("sbuf", [128, 176], F32), "dg": ("sbuf", [128, 176], F32),
     "PD0": ("psum", [128, 512], F32), "PD1": ("psum", [128, 512], F32), "PDI": ("psum", [128, 512], F32), "PS": ("psum", [128, 512], F32),
     "PE": ("psum", [128, 512], F32), "PK": ("psum", [128, 512], F32), "PL": ("psum", [128, 512], F32), "PV": ("psum", [128, 512], F32),
 }
-NDMA = 48
-SEMAPHORES = ["cV", "cS", "cT", "cG", "sent"] + ["arr%d" % t for t in range(RO)] + ["d%d" % i for i in range(NDMA)]
+NDMA = 56
+SEMAPHORES = ["cV", "cS", "cT", "cG", "sent"] + ["arr%d" % t for t in range(RO)] + [w + str(k) for w in ("fa", "fb") for k in range(8)] + ["d%d" % i for i in range(NDMA)]
 
 KEY0 = 61440 - (1 << 24)
-FIX, DLAT, DBW = 60.0, 1400.0, 300.0
-TIMES = [(0.83, 1.56, 3.8, 0.42, 200.0, 120.0, 900.0), (0.9, 1.25, 2.6, 0.46, 160.0, 90.0, 1700.0), (1.15, 1.8, 4.6, 0.6, 230.0, 130.0, 1100.0)]
-YCH = [[(0, 20), (20, 60), (60, 112), (112, 160)]] * 4 + [[(0, 40), (40, 100), (100, 160)]] * 2
-SELF = [20] * 4 + [0] * 2
-FARV = [((0, 40, "S"), (40, 80, "S"), (80, 120, "S"), (120, 134, "S"), (134, 148, e), (148, 160, e)) for e in "Vrrr"] \
-    + [((0, 40, "S"), (40, 80, "S"), (80, 120, "r"), (120, 160, "r"))] * 2
-REP = ["G"] * 6
+FIX, DLAT, DBW, CALL, MARGIN = 60.0, 1400.0, 300.0, 1100.0, 1.25
+TIMES = [(0.83, 1.56, 3.8, 0.42, 210.0, 160.0, 800.0), (1.18, 1.98, 4.6, 0.6, 220.0, 150.0, 900.0), (1.15, 1.55, 4.2, 0.7, 200.0, 120.0, 2500.0)]
+YCH = [[(0, 24), (24, 52), (52, 104), (104, 160)]] * 4 + [[(0, 40), (40, 100), (100, 160)]] * 2
+SELF = [24] * 4 + [0] * 2
+FARV = [((0, 36, "S"), (36, 74, "S"), (74, 112, "S"), (112, 136, "V"), (136, 160, "F")),
+        ((0, 48, "S"), (48, 96, "S"), (96, 144, "F"), (144, 160, "W")),
+        ((0, 16, "W"), (16, 64, "F"), (64, 112, "S"), (112, 160, "S")),
+        ((0, 32, "S"), (32, 64, "S"), (64, 112, "F"), (112, 160, "F")),
+        ((0, 44, "S"), (44, 88, "S"), (88, 124, "r"), (124, 160, "r")),
+        ((0, 36, "r"), (36, 72, "r"), (72, 116, "S"), (116, 160, "S"))]
+FOLDS = [(0, 136, 160, -1), (1, 96, 160, 1), (2, 0, 64, 2), (3, 64, 160, 3)]
+TURN = ()
+ROWS, MEAN, FREE, GAP, TRIP, BUSY, EARLY = 8, 0, 0, -400.0, 2500.0, 0.0, 0.0
+REPS = [(0,), (1, 2), (3,), (4, 5)]
+CUTS = {}
 LAG = [0, 1, 2, 4]
-KEYQ = "SVSVSVSVSV"
-BCH = [(0, 960), (960, 1920), (1920, 2880), (2880, 3360), (3360, 3840)]
-DUE, REACH = {}, (1, 8, 30, 120)
-SHIFTS, PACK, SWAPS, SEED, SLACK, RUN = 1000, 6, 5000, 1, 500.0, 256
+KEYQ = "SVSVSSDD"
+BCH = [(0, 1024), (1024, 2048), (2048, 2560), (2560, 3072), (3072, 3488), (3488, 3840)]
+LEFT = [50000.0, 42500.0, 35000.0, 28000.0, 21000.0, 11000.0, 1500.0, 0.0]
+DUE = {"far%d%s" % (t, e): LEFT[t + 1] for t in range(C) for e in "SVrFW"}
+DUE.update({"dist%d%s" % (t, e): LEFT[t + 2] for t in range(C) for e in "prFW"})
+DUE.update({"src%d" % t: LEFT[t + 3] for t in range(C)})
+DUE.update({"rep%d" % t: LEFT[min(t, C - 1)] for t in (0, 1, 3, 4)})
+DUE.update({"far3" + e: 19000.0 for e in "SVFW"})
+DUE.update({"dist2" + e: 19000.0 for e in "pFW"})
+DUE.update({"dist3" + e: 10000.0 for e in "pFW"})
+DUE["src2"] = 1500.0
+REACH, WEIGHT = (1, 8, 30, 120), (1.2, 1.0, 1.0)
+SHIFTS, PACK, SWAPS, SEED, SLACK, RUN = 800, 1, 15000, 2, 100.0, 256
 KEPT = {}
+
+
+def neighbour(core, T, topo):
+    return [c for c in topo.cores_of(core) if c not in T.cores and topo.die(c) == topo.die(core)][0]
+
+
+def folded(k, A):
+    t, l0, l1, at = FOLDS[k]
+    return A("far", 2560 * t + 16 * l0, 2560 * t + 16 * l1), A("ab", 2560 * (t % 3) + 16 * l0, 2560 * (t % 3) + 16 * l1)
 
 
 def plan(T, g, topo, core, rank):
     ops, tag = [], [None]
+    mate = neighbour(core, T, topo)
     size = {"float32": 4, "bfloat16": 2, "int32": 4, "uint16": 2}
 
     def A(name, a=None, b=None, step=1, parts=128, p0=0):
@@ -117,10 +144,10 @@ def plan(T, g, topo, core, rank):
         return add("V", lambda: g.vector.tensor_tensor_scan(out["ap"], d0["ap"], d1["ap"], 0.0, ALU.add, ALU.min), (0, 20 + max(64, out["n"]), 0, 0, 0), [d0, d1], [out])
 
     def act(out, in_, func, bias=0.0, scale=1.0, accum=None):
-        if accum is None: fn = lambda: g.scalar.activation(out["ap"], in_["ap"], func, bias=val(bias), scale=scale)
+        if accum is None: fn = lambda: g.scalar.activation(out["ap"], in_["ap"], func, bias=val(bias), scale=val(scale))
         else: fn = lambda: g.scalar.activation(out["ap"], in_["ap"], func, bias=val(bias), scale=scale, accum_out=accum["ap"])
         cost = (0, 78, out["n"], 0, 0) if in_.get("ind") else (0, 78 + out["n"], 0, 0, 0)
-        return add("S", fn, cost, [in_, bias], [out] + ([accum] if accum else []))
+        return add("S", fn, cost, [in_, bias, scale], [out] + ([accum] if accum else []))
 
     def run(items, grp=None):
         def fn():
@@ -152,7 +179,7 @@ def plan(T, g, topo, core, rank):
         return add("G", fn, (0, 157 + 2 * out["n"], 0, 0, 0), [], [out])
 
     def asel(out, in_, pat, base, cm, op):
-        return add("G", lambda: g.affine_select(out["ap"], in_["ap"], pat, op, 0.0, base, cm), (0, 205 + 2 * out["n"], 0, 0, 0), [in_], [out])
+        return add("G", lambda: g.affine_select(out["ap"], in_["ap"], pat, op, 0.0, base, cm), (0, MARGIN * (205 + 2 * out["n"]), 0, 0, 0), [in_], [out])
 
     def dma(q, out, in_):
         e = g.sync if q == "Y" else g.scalar
@@ -162,7 +189,7 @@ def plan(T, g, topo, core, rank):
 
     dma("Y", A("Pi"), T.grant[:])
     loads = [(A("Li"), T.favor[:])] + [(A("Xb", a, b), T.base[:, a:b]) for a, b in BCH]
-    loads += [(A("Bb"), T.base[:, 0:V_]), (A("Si", 0, K), T.src[:, 0:K]), (A("Si", K, V_), T.src[:, K:V_])]
+    loads += [(A("Si", 0, K), T.src[:, 0:K]), (A("Bb"), T.base[:, 0:V_]), (A("Si", K, V_), T.src[:, K:V_])]
     before = 0.0
     for out, src in ((A("mgi", parts=8), T.mg[:]), (A("Qi"), T.part[:]), (A("thi"), T.th[:])):
         dma("S", out, src)
@@ -177,25 +204,32 @@ def plan(T, g, topo, core, rank):
     ms(A("one"), 1.0)
     asel(A("Iw"), A("one"), [[-1, 144]], 8, 1, ALU.is_equal)
     ms(A("rlo", parts=64), 0.0)
-    iota(A("rlo", parts=1), [[0, 3], [1, K]], 0, 0)
+    iota(A("rlo", 0, K, parts=1), [[1, K]], 0, 0)
     iota(A("pi"), [[0, 1]], 0, 1)
     asel(A("B1"), A("one", 0, 128), [[-16, 8], [0, 16]], 0, 1, ALU.is_ge)
     asel(A("B2"), A("B1"), [[16, 8], [0, 16]], 15, -1, ALU.is_ge)
-    asel(A("G1", parts=8), A("one", 0, 128, parts=8), [[1, 128]], 0, -16, ALU.is_ge)
-    asel(A("G2s", parts=8), A("G1", parts=8), [[-1, 128]], 15, 16, ALU.is_ge)
     iota(A("jm"), [[0, 11], [1, 16]], 0, 0)
-    for j in (1, 2): ms(A("rlo", j * K, (j + 1) * K, parts=33, p0=32), float(j * K))
+    for c in range(RO - C): iota(A("ef", c * K, c * K + K), [[1, K]], 4096 + c * K, 0)
+    for a in range(K, 512, K):
+        b = min(a + K, 512)
+        ms(A("rlo", a, b, parts=33, p0=32), float(a))
+        tc(A("rlo", a, b, parts=1), A("rlo", 0, b - a, parts=1))
     ms(A("rhi", parts=64), 2.0 ** -16)
     ms(A("r1", parts=1), 1.0)
-    crv = [1.0, -491520.0] + [4096.0 + c * K for c in range(C)] + [16384.0, 2.0 ** -16, -255.0]
-    crv += [((1 + t % (N - 1)) * V_ + (t % C) * K - 4096) / 65536.0 for t in range(RO - 1)]
-    for j in range(len(crv)): act(A("cr", j * 128, (j + 1) * 128, parts=1), A("one", 0, 128, parts=1), ACT.Identity, scale=crv[j])
+    crv = [1.0, -491520.0] + [4096.0 + c * K for c in range(C)] + [-2.0 ** 33, 2.0 ** -16, -255.0]
+    crv += [((1 + t % (N - 1)) * V_ + (t % C) * K - 4096) / 65536.0 for t in range(RO - 1)] + [(a - 4096) / 65536.0 for a, b in BCH[-2:]]
+    for j in range(len(crv)):
+        if j < ROWS: act(A("cr", j * 128, (j + 1) * 128, parts=1), A("one", 0, 128, parts=1), ACT.Identity, scale=crv[j])
+        else: ms(A("cr", j * 128, (j + 1) * 128, parts=1), crv[j])
     CR = lambda j: A("cr", j * 128, (j + 1) * 128, parts=1)
     Id = A("Iw", 8, 136)
     for nm, s in (("Ip", 1.0), ("In", -1.0), ("P25", 2.0 ** 25), ("N25", -2.0 ** 25), ("Inf", -1.0)):
         act(A(nm), Id, ACT.Identity, scale=s)
     ts(A("pm"), A("pi"), 15, ALU.bitwise_and)
     tc(A("pc", 0, 1), A("pm"))
+    if TURN:
+        iota(A("Lj"), [[16, 10]], 0, 0)
+        ts(A("L16"), A("Lj"), A("pc", 0, 1), ALU.add)
     ts(A("pc", 1, 2), A("pm"), 8.0, ALU.is_lt)
     ts(A("pc", 2, 3), A("pm"), 8.0, ALU.is_ge)
     ts(A("pc", 3, 4), A("pm"), -1.0, ALU.mult, 2041.03125, ALU.add)
@@ -205,17 +239,17 @@ def plan(T, g, topo, core, rank):
         act(A(nm), A("B2"), ACT.Identity, scale=s)
     ms(A("Z"), 0.0)
     ts(A("Z", 15, 128, 16), A("B2", 0, 128, 16), 8192.0, ALU.mult)
-    ts(A("Z2"), A("Z"), 2.0, ALU.mult)
-    ts(A("Zn"), A("Z"), -1.0, ALU.mult)
-    ts(A("Gt", parts=8), A("G2s", parts=8), -8192.0, ALU.mult)
+    act(A("Z2"), A("Z"), ACT.Identity, scale=2.0)
+    act(A("Zn"), A("Z"), ACT.Identity, scale=-1.0)
+    mm(A("PS", 0, 128, parts=8), [(A("Iw", 8, 136, 16), A("B2"))])
+    act(A("Gt", parts=8), A("PS", 0, 128, parts=8), ACT.Identity, scale=-8192.0)
     ts(A("dg"), A("jm"), A("pc", 0, 1), ALU.not_equal, 1e9, ALU.mult)
     nd0 = 8 * max(b - a for ch in YCH for a, b in ch)
     ms(A("D0c", 0, nd0), -0.0625)
     ms(A("D0c", 0, nd0, 8), 1024.0)
-    ms(A("Af", 0, 1), 80.0)
+    ms(A("cnt", 0, 1), 80.0 - 15.5)
     LO = A("rlo", 0, K, parts=1)
-    R1 = A("r1", parts=1)
-    X1 = A("PV", 336, 336 + K)
+    R1 = A("r1", 0, K, parts=1)
 
     tc(A("P16"), A("Pi"))
 
@@ -225,22 +259,35 @@ def plan(T, g, topo, core, rank):
         if t == 0: tc(A("Tf", u, u + K), IND(A("Li"), off))
         else: act(A("Tf", u, u + K), IND(A("Lf"), off), ACT.Identity)
         ev, od = A("Tf", u, u + K, 2), A("Tf", u + 1, u + K, 2)
-        mm(A("PL", 320, 400), [(A("W0", 8, 136), ev), (A("W0", 0, 128), od)])
-        mm(A("PV", 176, 256), [(A("W1", 16, 144), ev), (A("W1", 8, 136), od)])
-        tc(A("O16", u, u + 80), A("PL", 320, 400))
-        tc(A("O16", u + 80, u + K), A("PV", 176, 256))
+        low, high = A("PL", 352, 432), A("PV", 176, 256) if t else A("PL", 432, 512)
+        mm(low, [(A("W0", 8, 136), ev), (A("W0", 0, 128), od)])
+        mm(high, [(A("W1", 16, 144), ev), (A("W1", 8, 136), od)])
+        tc(A("O16", u, u + 80), low)
+        tc(A("O16", u + 80, u + K), high)
 
-    lists(0)
-    banks = ["PD0", "PD1", "PDI", "PS", "PE", "PK", "PV", "PL", "PD0", "PD1"]
-    cuts = [0, 480, 960, 1440, 1920, 2400, 2880, 3120, 3360, 3600, 3840]
-    for j in range(10):
+    banks = ["PD0", "PD1", "PDI", "PE", "PK", "PV", "PS", "PL"]
+    cuts = list(range(0, BCH[-1][0], 512)) + list(BCH[-1])
+    step = {}
+
+    def chain(name, op):
+        op["after"], step[name] = step.get(name), op
+
+    for j in range(8):
         a, b = cuts[j], cuts[j + 1]
-        ps = A(banks[j], 0, 480 if banks[j] in ("PV", "PL") else b - a)
-        ps["ap"], ps["n"] = A(banks[j], 0, b - a)["ap"], b - a
-        run(terms(ps, [(A("rhi", parts=33), A("rlo", 0, b - a, parts=33))], sp=False), ("key", j))
-        run(terms(ps, [(A("Ip"), A("Xb", a, b))], st=False), ("key", j))
-        if KEYQ[j] == "S": act(A("Xk", a, b), ps, ACT.Identity, bias=(KEY0 + a) / 65536.0)
-        else: ts(A("Xk", a, b), ps, (KEY0 + a) / 65536.0, ALU.add)
+        ramp, ones = [(A("rhi", parts=33), A("rlo", 0, b - a, parts=33))], A("r1", 0, b - a, parts=1) if KEYQ[j] == "D" else None
+        if ones: chain("T", mm(A(banks[j], 0, b - a), ramp + [(CR(8), ones), (CR(8 + j), ones)]))
+        else: chain("T", run(terms(A(banks[j], 0, b - a), ramp, sp=False), ("key", j)))
+    lists(0)
+    for op in ops[-5:]: chain(op["eng"], op)
+    for j in range(8):
+        a, b = cuts[j], cuts[j + 1]
+        ps = A(banks[j], 0, b - a)
+        if KEYQ[j] == "D":
+            chain("V", tt(A("Xk", a, b), A("Xb", a, b), ps, ALU.add))
+            continue
+        chain("T", run(terms(ps, [(A("Ip"), A("Xb", a, b))], st=False), ("key", j)))
+        if KEYQ[j] == "S": chain("S", act(A("Xk", a, b), ps, ACT.Identity, bias=(KEY0 + a) / 65536.0))
+        else: chain("V", ts(A("Xk", a, b), ps, (KEY0 + a) / 65536.0, ALU.add))
     tc(A("Q16"), A("Qi"))
     for j in range(2): tc(A("Lf", 512 * j, 512 * j + 512), A("Li", 512 * j, 512 * j + 512))
     for c in range(C): tc(A("S16", c * K, c * K + K), A("Si", c * K, c * K + K))
@@ -248,39 +295,77 @@ def plan(T, g, topo, core, rank):
     ts(A("thp", 1, 2), A("thi"), 6, ALU.arith_shift_right)
     tc(A("thf", 0, 2), A("thp"))
     ts(A("thf", 2, 3), A("thp", 1, 2), -64.0, ALU.add)
+    ts(A("thf", 3, 4), A("thp", 0, 1), 15.5, ALU.add)
     for w in range(2): ts(A("Dh", 128 * w, 128 * w + 128), A("Ip"), A("thf", 2 - w, 3 - w), ALU.mult)
     ts(A("Dl", 0, 128), A("Ip"), A("thf", 0, 1), ALU.mult)
     ms(A("cn", 0, K), -8192.0)
     ms(A("cn", K, 2 * K), -8192.0 * 64)
     tc(A("mgf", parts=8), A("mgi", parts=8))
-    ts(A("mgr", 0, 128, parts=8), A("one", 0, 128, parts=8), A("mgf", parts=8), ALU.mult)
-    ts(A("mgr", 128, K, parts=8), A("one", 0, K - 128, parts=8), A("mgf", parts=8), ALU.mult)
-    for a, b in ((960, 1440), (1600, 2240), (2400, 3040), (3360, 3840)):
-        dma("Y", T.yx[:, a:b], A("Xb", a, b))["low"] = True
+    act(A("mgr", parts=8), A("cn", 0, K, parts=8), ACT.Identity, bias=A("mgf", parts=8), scale=0.0)
+
+    def told(t):
+        return (1 + t % (N - 1)) * V_ + (t % C) * K
+
+    def landing(t):
+        return A("X%d" % (t + 1), told(t), told(t) + K) if C <= t + 1 < RO else A("land", t * K, t * K + K)
+
+    def standing():
+        for t in range(C):
+            a, b = told(t) + K, told(t + 1) if t < C - 1 else W_
+            op = dma("Y", A("X4", a, b), T.base[:, a:b])
+            op["rd"].append(landing(0))
+            op["lat"] += 600.0 * t
+            chain("Y", op)
+        for a, b in ((960, 1440), (1600, 2240), (2400, 3040), (3360, 3840)):
+            chain("Y", dma("Y", T.yx[:, a:b], A("Xb", a, b)))
 
     last = {}
 
     def paired(t):
-        return min([l0 for l0, l1, e in FARV[t] if e in "ar"] + [K])
+        mine = [x for x in FARV[t] if x[2] in "arFW"] or [(K, K, "")]
+        return mine[0][0], mine[-1][1], mine[0][2]
 
-    def repeat(t):
-        l0, tag[0] = paired(t), "rep%d" % t
-        old = A("Bb", t * K + l0, t * K + K) if t < C else A("sb", (t - C) * K + l0, (t - C) * K + K)
-        for p in range(16 if l0 < K else 0):
-            out = A("rep", 1280 * t + p, 1280 * t + 16 * (K - l0), 16)
-            if REP[t] == "G": asel(out, old, [[0, K - l0]], 0, 0, ALU.is_ge)
-            else: tc(out, old)
+    def repeated(t, l0, l1):
+        r0 = 16 * (sum(paired(j)[1] - paired(j)[0] for j in range(t)) - paired(t)[0])
+        return A("rep", r0 + 16 * l0, r0 + 16 * l1)
+
+    def repeat(ts_):
+        t, u = ts_[0], ts_[-1]
+        a, b, tag[0] = (t % C) * K + paired(t)[0], (u % C) * K + paired(u)[1], "rep%d" % t
+        old, r0 = A("sb" if t >= C else "Bb" if t else "Xb", a, b), repeated(t, paired(t)[0], K)["lo"]
+        for a2, b2, e in CUTS.get(t, [(a, b, "G")]):
+            old, tag[0] = A(old["buf"] if a2 == a else "Bb", a2, b2), "rep%d" % (t if a2 == a else a2)
+            for p in range(16 if a < b else 0):
+                out = A("rep", r0 + 16 * (a2 - a) + p, r0 + 16 * (b2 - a), 16)
+                if e == "G": asel(out, old, [[0, b2 - a2]], 0, 0, ALU.is_ge)
+                else: tc(out, old)
 
     def far_gather(t):
         o = (t % C) * K
         for l0, l1, e in FARV[t]:
             tag[0] = "far%d%s" % (t, e)
-            out, src = A("far", 2560 * t + 16 * l0, 2560 * t + 16 * l1), IND(A("Xb"), A("S16", o + l0, o + l1))
-            if e == "S": act(out, src, ACT.Identity)
-            elif e == "V": tc(out, src)
+            out, src = A("far", 2560 * t + 16 * l0, 2560 * t + 16 * l1), IND(A("Xb" if t < C else "X%d" % t), A("S16", o + l0, o + l1))
+            if e in "SF": act(out, src, ACT.Identity)
+            elif e in "VW": tc(out, src)
             else:
-                r0 = 1280 * t + 16 * (l0 - paired(t))
-                tt(out, src, A("rep", r0, r0 + 16 * (l1 - l0)), ALU.subtract)
+                tt(out, src, repeated(t, l0, l1), ALU.subtract)
+
+    def folds(t, early):
+        for k in range(len(FOLDS)):
+            if FOLDS[k][3] != t - early or (early and t): continue
+            tag[0] = "fold%d" % k
+            far, most = folded(k, A)
+            old = repeated(*FOLDS[k][:3])
+
+            def fold(k=k, far=far, old=old):
+                rid, pid, _ = topo.addr(mate)
+                move = RemoteDMATransfer(dst_ids=[DstId(rid=rid, pnc=pid)], dma_engine_mask=topo.mask(core, mate), remote_sem=T.sem["fa%d" % k],
+                                         srcs=[far["ap"], old["ap"]], dsts=[far["ap"]], alu_op=2)
+                return g.remote_dma_fused([move], local_sem=T.sem.sent)
+            op = add("G", fold, (CALL + (1900 if k == 0 else 0), 0, 0, 0, 0), [far, old], [most], kind="r", lat=TRIP + 3.5 * far["n"])
+            op["semn"], op["out"], op["in"], op["back"] = "fb%d" % k, len(topo.engines(core, mate)), len(topo.engines(mate, core)), (mate, far, most)
+            op["gap"] = 2.0 * far["n"] + (GAP if k else -600.0)
+            chain("send", op)
 
     nch = [0]
 
@@ -288,17 +373,22 @@ def plan(T, g, topo, core, rank):
         return A("PDI", (t % 3) * K + l0, (t % 3) * K + l1) if t < C else A("PK", 2 * K + l0, 2 * K + l1)
 
     def distances(t, old):
-        lp, w = paired(t), 128 * (t >= C)
-        cut = [0, lp] if lp <= 102 else [0, lp // 2, lp]
-        segs = [(cut[j], cut[j + 1], "p") for j in range(len(cut) - 1)]
-        rs = [(lp, K, FARV[t][-1][2])] if lp < K else []
+        w = 128 * (t >= C)
+        a, b = (0, paired(t)[0]) if paired(t)[0] else (paired(t)[1], K)
+        cut = [a, b] if b - a <= 102 else [a, (a + b) // 2, b]
+        segs = [(cut[j], cut[j + 1], "p") for j in range(len(cut) - 1) if a < b]
+        rs = [paired(t)] if paired(t)[2] else []
         for l0, l1, e in (segs + rs if t < C else rs + segs):
             tag[0] = "dist%d%s" % (t, e)
             gid, f0, a0, n = (t, l0), 2560 * t + 16 * l0, 2560 * (t % 3) + 16 * l0, l1 - l0
             di = lapse(t, l0, l1)
             den = [(A("Dh", w, w + 128), A("cn", K, K + n)), (A("Dl", 128 * t, 128 * t + 128), A("cn", 0, n))]
             if t < C: den += [(A("P25"), A("sg", t * K + l0, t * K + l1))]
-            if e in "ar":
+            if e in "FW":
+                pairs = [(A("Zn", 15 - p, 143 - p), A("far", f0 + p, f0 + 16 * n, 16)) for p in range(16)] + [(A("Bn"), A(old[0], old[1] + l0, old[1] + l1))]
+                more = [(A("Z2", 15 - p, 143 - p), A("ab", a0 + p, a0 + 16 * n, 16)) for p in range(16)]
+                runs(terms(di, pairs + more + den), gid)
+            elif e in "ar":
                 pairs = []
                 if e == "r":
                     for m0, m1, e2 in FARV[t]:
@@ -330,7 +420,7 @@ def plan(T, g, topo, core, rank):
         act(A("Xk", n0, n0 + K), ps, ACT.Identity, bias=(KEY0 + n0) / 65536.0)
         ps = A("PK", K, 2 * K)
         mm(ps, [(CR(8), R1), (CR(9 + t), R1), (CR(7), LO)])
-        tt(A("Xk", n1, n1 + K), A("land", t * K, t * K + K), ps, ALU.add)
+        tt(A("Xk", n1, n1 + K), landing(t), ps, ALU.add)
 
     def sources(t):
         c = t % C
@@ -346,28 +436,33 @@ def plan(T, g, topo, core, rank):
             tt(G2, sa, G2, ALU.min)
         else:
             G2, G3, tag[0] = A("PS", 2 * K, 3 * K), A("PS", K, 2 * K), "src%d" % t
-            mm(G3, [(CR(0), LO), (CR(2 + c), R1)])
-            tt(A("x1"), xf, X1, ALU.subtract)
-            mm(G2, [(CR(6), R1), (A("P25"), A("x1"))])
+            tt(A("x1"), A("x1a"), A("PV", 0, K), ALU.min)
+            mm(G2, [(A("P25"), A("xx")), (A("N25"), A("x1")), (CR(0), LO), (CR(2 + c), R1)])
             tt(sa, di, A("Si", o, o + K), ALU.max)
-            tt(A("sa2"), sa, A("PE", 0, K), ALU.max)
-            tt(sa, A("sa2"), G3, ALU.min)
             tt(G2, sa, G2, ALU.min)
         act(A("c2", t * K, t * K + K), Rk, ACT.Identity, scale=65536.0)
-        tt(sz, A("c2", t * K, t * K + K), G2, ALU.max)
+        if t < C:
+            tt(sz, A("c2", t * K, t * K + K), G2, ALU.max)
+        else:
+            tt(A("sa2"), A("c2", t * K, t * K + K), G2, ALU.max)
+            mm(G3, [(CR(6), R1), (A("P25"), A("uu"))])
+            tt(G3, A("ef", o, o + K), G3, ALU.min)
+            tt(sz, A("sa2"), G3, ALU.max)
         ts(A("Si", o, o + K), sz, 4095, ALU.bitwise_and)
         if t + C < RO:
             tc(A("S16", o, o + K), A("Si", o, o + K))
         else:
-            tc(A("Sf", o, o + K), A("Si", o, o + K))
+            if t in TURN: act(A("Sf", o, o + K), IND(A("Si", o, o + K), A("L16")), ACT.Identity)
+            else: tc(A("Sf", o, o + K), A("Si", o, o + K))
             dma("Y", T.ys[:, o:o + K], A("Sf", o, o + K))
 
-    for t in range(C): repeat(t)
+    for ts_ in REPS:
+        if ts_[0] < C: repeat(ts_)
     for t in range(RO):
         c = t % C
         o, f, d, u, q = c * K, c ^ 1, 1 + t % (N - 1), (t % 2) * K, (t % 3) * K
         ys0, r0 = 1280 * (t % 2), 1280 * t
-        be, xf, ld = A("Bb", o, o + K), A("sb", t * K, t * K + K), A("land", t * K, t * K + K)
+        be, xf, ld = A("Bb", o, o + K), A("sb", t * K, t * K + K), landing(t)
         bP, E, Tf, mi, xx, uu = A("PV", 0, K), A("PE", 0, K), A("Tf", u, u + K), A("mi"), A("xx"), A("uu")
         prev, tag[0] = None, None
         for l0, l1 in YCH[t]:
@@ -381,17 +476,17 @@ def plan(T, g, topo, core, rank):
             tt(A("YV", 8 * l0, 8 * l1), IND(A("Xk"), A("O16", u + 80 + l0 // 2, u + 80 + l1 // 2)), A("YS", ys0 + 8 * l0, ys0 + 8 * l1), ALU.min)
             scan(A("R", r0 + 8 * l0, r0 + 8 * l1), A("D0c", 0, 8 * (l1 - l0)), A("YV", 8 * l0, 8 * l1))
         mm(bP, [(A("Ip"), be)])
-        if t >= C:
-            far_gather(t)
-            distances(t, ("sb", last[c] * K))
+        far_gather(t)
+        folds(t, True)
+        if t >= C: distances(t, ("sb", last[c] * K))
         tag[0] = None
         ts(mi, A("R", r0 + 7, r0 + 1280, 8), 255.502, ALU.add)
         if t < C:
             tt(xx, mi, bP, ALU.min)
         else:
+            tt(A("PV", 336, 336 + K), mi, bP, ALU.min)
             tt(A("x1a"), lapse(t), A("sb", last[c] * K, last[c] * K + K), ALU.max)
-            tt(X1, A("x1a"), bP, ALU.min)
-            tt(xx, mi, X1, ALU.min)
+            tt(xx, A("x1a"), A("PV", 336, 336 + K), ALU.min)
         pairs = [(A("Gt", parts=8), A("mgr", parts=8)), (A("Bp"), be)]
         if f in last:
             pairs += [(A("Bn"), A("Bb", f * K, f * K + K)), (A("Bp"), A("sb", last[f] * K, last[f] * K + K))]
@@ -404,8 +499,10 @@ def plan(T, g, topo, core, rank):
         def send(t=t, dst=T.cores[(rank + d) % N], xf=xf, ld=ld):
             rid, pid, _ = topo.addr(dst)
             return g.remote_dma(ld["ap"], xf["ap"], T.sem["arr%d" % t], T.sem.sent, pid, rid, topo.mask(core, dst))
-        op = add("G", send, (800 + (1300 if t == 0 else 0), 0, 0, 0, 0), [xf], [ld], kind="r")
-        op["t"] = t
+        op = add("G", send, (CALL + (1300 if t == 0 and not FOLDS else 0), 0, 0, 0, 0), [xf], [ld], kind="r")
+        op["semn"] = "arr%d" % t
+        chain("send", op)
+        folds(t, False)
         op["out"] = len(topo.engines(core, T.cores[(rank + d) % N]))
         op["in"] = len(topo.engines(T.cores[(rank - d) % N], core))
         tag[0] = "sel%d" % t
@@ -424,29 +521,34 @@ def plan(T, g, topo, core, rank):
             keys(t, xf, o, d * V_ + o)
             tag[0] = "cnt%d" % t
             act(A("sg", t * K, t * K + K), uu, ACT.Sign, bias=-255.5, accum=A("acc", t, t + 1))
-            ts(A("Ai", t, t + 1), A("acc", t, t + 1), 0.5, ALU.mult, A("Af", t, t + 1), ALU.add)
-            if t < RO - 2: ts(A("Af", t + 1, t + 2), A("Ai", t, t + 1), 80.0, ALU.add)
-            ts(A("Am", t, t + 1), A("Ai", t, t + 1), 31, ALU.bitwise_and)
-            ts(A("bias", t + 1, t + 2), A("Am", t, t + 1), A("thf", 0, 1), ALU.add)
-            ts(A("Dl", 128 * t + 128, 128 * t + 256), A("Ip"), A("bias", t + 1, t + 2), ALU.mult)
+            cnt = [A("cnt", 5 * t + j, 5 * t + j + 1) for j in range(6)]
+            act(cnt[1], A("acc", t, t + 1), ACT.Identity, bias=cnt[0], scale=0.5)
+            if t < RO - 2: act(cnt[5], cnt[1], ACT.Identity, bias=80.0)
+            act(cnt[2], cnt[1], ACT.Identity, bias=3.0 * 2 ** 27)
+            act(cnt[3], cnt[2], ACT.Identity, bias=3.0 * 2 ** 27, scale=-1.0)
+            ts(cnt[4], cnt[1], cnt[3], ALU.add, A("thf", 3, 4), ALU.add)
+            ts(A("Dl", 128 * t + 128, 128 * t + 256), A("Ip"), cnt[4], ALU.mult)
         else:
             for j in range(2):
                 dma("YS"[j], T.yl[:, 512 * j:512 * j + 512], A("Lf", 512 * j, 512 * j + 512))["lat"] += 512 * 512 / DBW
-        if t + C < RO: repeat(t + C)
-        if t < C: far_gather(t)
-        else: sources(t)
+        for ts_ in REPS:
+            if ts_[-1] == t + C: repeat(ts_)
+        if t >= C: sources(t)
         for t2 in range(C):
             if LAG[t2] == t: sources(t2)
         tag[0] = None
         if t + C >= RO: dma("Y", T.yx[:, o:o + K], xf)
         dma("Y", T.yx[:, d * V_ + o:d * V_ + o + K], ld)
-        if t < RO - 1:
-            if t < C - 1:
-                dma("Y", A("Xb", o, o + K), xf)
-                dma("Y", A("Xb", d * V_ + o, d * V_ + o + K), ld)
-            else:
-                tc(A("Xb", o, o + K), xf)
-                tc(A("Xb", d * V_ + o, d * V_ + o + K), ld)
+        if t < C - 1:
+            chain("Y", dma("Y", A("Xb", o, o + K), xf))
+            for win in ("Xb", "X4"): chain("Y", dma("Y", A(win, d * V_ + o, d * V_ + o + K), ld))
+        if t == 0: standing()
+        if t == C - 2: dma("Y", A("X4", 0, o + K), A("sb", 0, o + K))
+        if t == C - 1:
+            dma("Y", A("X4", o, o + K), xf)
+            dma("Y", A("X5", K, told(C)), A("X4", K, told(C)))
+            dma("Y", A("X5", told(C) + K, W_), A("X4", told(C) + K, W_))
+        if t == C: dma("Y", A("X5", o, o + K), xf)
         last[c] = t
     return ops
 
@@ -480,7 +582,7 @@ def tables(ops):
         for j in op["deps"]: a |= 1 << j
         anc.append(a)
     out = []
-    for cyc, ga, sc, pe, hop, own, rem in TIMES:
+    for cyc, ga, sc, pe, hop, own, rem in TIMES + [[sum(x) / len(x) for x in zip(*TIMES)]] * MEAN:
         cost = [c[0] + cyc * (c[1] + ga * c[2] + sc * c[3]) + pe * c[4] for c in [op["cost"] for op in ops]]
         lat = [op["lat"] + (rem if op["kind"] == "r" else 0.0) for op in ops]
         pre = []
@@ -488,34 +590,44 @@ def tables(ops):
             row = []
             for j in red[op["id"]]:
                 p = ops[j]
-                row.append((j, lat[j] + (own if p["eng"] == op["eng"] and p["kind"] == "c" else hop) if op["deps"][j] else 0.0))
+                row.append((j, lat[j] + (own if p["eng"] == op["eng"] and p["kind"] == "c" else hop) if op["deps"][j] else p.get("gap", 0.0)))
             pre.append(row)
-        out.append((cost, lat, pre, hop))
+        rest = list(lat)
+        for i in reversed(range(len(ops))):
+            for j, w in pre[i]: rest[j] = max(rest[j], w + cost[i] + rest[i])
+        out.append((cost, lat, pre, hop, rest))
     return out
 
 
-def play(ops, tab, seq):
-    cost, lat, pre, hop = tab
+def play(ops, tab, seq, base=None, same=0, most=1e18):
+    cost, lat, pre, hop, rest = tab
     n = len(cost)
-    t1, why = [0.0] * n + [-1e9], [None] * n
-    front = {e: n for e in "VSTGY"}
-    bank = {b: {} for b in SCRATCH if SCRATCH[b][0] == "psum"}
-    end = 0.0
-    for i in seq:
-        e, t, banks = ops[i]["key"]
-        y, j = None, front[e]
-        if t1[j] > t: t, y = t1[j], j
-        for b in banks:
-            held = bank[b]
-            for e2, j in held.items():
-                if e2 != e and t1[j] + hop > t: t, y = t1[j] + hop, j
-            held[e] = i
-        for j, w in pre[i]:
-            if t1[j] + w >= t: t, y = t1[j] + w, -1 - j
-        t += cost[i]
-        t1[i], why[i], front[e] = t, y, i
-        if t + lat[i] > end: end = t + lat[i]
-    return end, t1, why
+    if base:
+        marks = base[4][:same // 32 + 1]
+        t1, why = list(base[1]), list(base[2])
+    else:
+        marks = [({e: n for e in "VSTGY"}, {b: {} for b in SCRATCH if SCRATCH[b][0] == "psum"}, 0.0, None)]
+        t1, why = [0.0] * n + [-1e9], [None] * n
+    front, bank, end, final = marks[-1]
+    front, bank = dict(front), {b: dict(h) for b, h in bank.items()}
+    for a in range(32 * len(marks) - 32, n, 32):
+        for i in seq[a:a + 32]:
+            e, t, banks = ops[i]["key"]
+            y, j = None, front[e]
+            if t1[j] > t: t, y = t1[j], j
+            for b in banks:
+                held = bank[b]
+                for e2, j in held.items():
+                    if e2 != e and t1[j] + hop > t: t, y = t1[j] + hop, j
+                held[e] = i
+            for j, w in pre[i]:
+                if t1[j] + w >= t: t, y = t1[j] + w, -1 - j
+            t += cost[i]
+            if t + rest[i] > most: return 1e18, None
+            t1[i], why[i], front[e] = t, y, i
+            if t + lat[i] > end: end, final = t + lat[i], i
+        marks.append((dict(front), {b: dict(h) for b, h in bank.items()}, end, final))
+    return end, t1, why, final, marks
 
 
 def clash(ops, seq):
@@ -570,7 +682,7 @@ def order(ops):
             op["first"] = 9000.0 if op.get("low") else 0.0
             op["key"] = (op["eng"], op["first"], op["banks"])
         tabs = tables(ops)
-        cost, lat, pre, hop = tabs[0]
+        cost, lat, pre, hop, rest = tabs.pop() if MEAN else tabs[0]
         suc = [[] for op in ops]
         for i in range(n):
             for j, w in pre[i]: suc[j].append((i, w))
@@ -581,12 +693,15 @@ def order(ops):
                 for j, w in pre[i]: way[j] = max(way[j], cost[j] + w + way[i])
             return [-x for x in way]
 
-        def judge(seq, most=1e18):
-            ends = []
-            for tab in tabs:
-                ends.append(play(ops, tab, seq)[0])
-                if ends[0] > most: return 1e18, seq, ends
-            return (1e18 if clash(ops, seq) else sum(ends)), seq, ends
+        def judge(seq, m=0, most=1e18, base=None):
+            same = 0
+            while base and same < n and seq[same] == base[1][same]: same += 1
+            got = {m: play(ops, tabs[m], seq, base and base[3][m], same, most)}
+            if got[m][0] > most or clash(ops, seq): return 1e18, seq
+            for j in range(len(tabs)):
+                if j != m: got[j] = play(ops, tabs[j], seq, base and base[3][j], same)
+            ends = [got[j][0] for j in range(len(tabs))]
+            return sum(WEIGHT[j] * ends[j] + EARLY * sum(got[j][1][:n]) / n for j in range(len(ends))), seq, ends, got
 
         def pack(pr):
             t1 = place(ops, [op["first"] for op in ops], cost, pre, hop, sorted(range(n), key=lambda x: (pr[x], x)))
@@ -597,7 +712,7 @@ def order(ops):
             back = place(ops, lat, cost, suc, hop, sorted(range(n), key=lambda x: (-t1[x], -x)))
             return [-x for x in back]
 
-        due, z = dict(DUE), SEED
+        due, z = {a: b * (1.25 if MEAN else 1.0) for a, b in DUE.items()}, SEED
         tags = sorted(set(op["tag"] for op in ops if op["tag"]))
         best = judge(pack(urge(due))[1])
         for it in range(SHIFTS):
@@ -610,12 +725,11 @@ def order(ops):
             cur = judge(pack(urge(new))[1])
             if cur[0] <= best[0]: best, due = cur, new
         KEPT["due"], KEPT["log"] = due, [int(best[0] / 3)]
-        now = best
+        now, busy = best, [i for i in range(n) if ops[i]["eng"] in "VS"]
         for it in range(SWAPS):
             z = (z * 6364136223846793005 + 1442695040888963407) % (1 << 64)
-            seq, tab = now[1], tabs[(z >> 50) % len(tabs)]
-            end, t1, why = play(ops, tab, seq)
-            i = max(range(n), key=lambda a: t1[a] + tab[1][a])
+            m = (z >> 50) % len(tabs)
+            seq, (end, t1, why, i, marks) = now[1], now[3][m]
             pairs = []
             while why[i] is not None:
                 j = why[i]
@@ -623,6 +737,7 @@ def order(ops):
                 i = j if j >= 0 else -1 - j
             if not pairs: continue
             a, b = pairs[(z >> 20) % len(pairs)]
+            if (z >> 56) % 8 < FREE: a = b = busy[(z >> 21) % len(busy)]
             pr = [0.0] * n
             for pos in range(n): pr[seq[pos]] = float(pos)
             early, far = (z >> 10) & 1, (z >> 12) % REACH[(z >> 44) % len(REACH)]
@@ -638,14 +753,16 @@ def order(ops):
                     elif not early and pr[j] <= pr[x]:
                         pr[j] = pr[x] + 1e-4
                         todo.append(j)
-            how = (z >> 40) % 8
-            if how >= PACK: cur = judge(sorted(range(n), key=lambda x: (pr[x], x)), now[2][0] + 600.0)
-            else: cur = judge(pack(repack(pr) if how == 0 else pr)[1], now[2][0] + 600.0)
-            if cur[0] <= now[0] + SLACK * (1.0 - it / SWAPS):
-                t1 = play(ops, tabs[0], cur[1])[1]
-                spot = {cur[1][pos]: pos for pos in range(n)}
-                again = judge(sorted(range(n), key=lambda x: (t1[x] - cost[x], spot[x])))
-                now = again if again[0] <= cur[0] else cur
+            how = (z >> 40) % 32
+            slack = SLACK * (1.0 - it / SWAPS)
+            if how >= PACK: cur = judge(sorted(seq, key=lambda x: pr[x]), m, now[2][m] + slack, now)
+            else: cur = judge(pack(repack(pr) if how == 0 else pr)[1], m, now[2][m] + slack)
+            if cur[0] <= now[0] + slack:
+                if (z >> 24) % 4 == 0:
+                    t1, c1 = cur[3][m][1], tabs[m][0]
+                    again = judge(sorted(cur[1], key=lambda x: t1[x] - c1[x]))
+                    if again[0] <= cur[0]: cur = again
+                now = cur
                 if now[0] < best[0]: best = now
         KEPT["seq"], KEPT["ends"] = best[1], best[2]
     return [ops[i] for i in KEPT["seq"]]
@@ -691,7 +808,7 @@ def emit(seq, ops, g, T):
             nd += 1
             ends.append(op)
         else:
-            op["sem"], op["val"] = T.sem["arr%d" % op["t"]], op["in"]
+            op["sem"], op["val"] = T.sem[op["semn"]], op["in"]
             sent += op["out"]
     for op in seq:
         e = q[op["eng"]]
@@ -704,9 +821,20 @@ def emit(seq, ops, g, T):
         if not op["wr"]: q[op["eng"]].wait_ge(op["sem"], 16)
 
 
+def hand_back(g, core, owner, T, topo):
+    rid, pid, _ = topo.addr(owner)
+    for k in range(len(FOLDS)):
+        far, most = folded(k, lambda name, a, b: T[name][:, a:b])
+        g.wait_ge(T.sem["fa%d" % k], len(topo.engines(owner, core)))
+        g.remote_dma(most, far, T.sem["fb%d" % k], T.sem.sent, pid, rid, topo.mask(core, owner))
+    if FOLDS: g.wait_ge(T.sem.sent, len(FOLDS) * len(topo.engines(core, owner)))
+
+
 def rank_program(g, core, T, topo):
     rank = T.rank_of(core)
     if rank is None:
+        for owner in T.cores:
+            if neighbour(owner, T, topo) == core: hand_back(g, core, owner, T, topo)
         return
     ops = plan(T, g, topo, core, rank)
     depend(ops)

from concourse.bass import DstId, RemoteDMATransfer
from concourse.mybir import dt, AluOpType, AxisListType, ActivationFunctionType

K, C, NS, RO, N = 160, 4, 1024, 6, 6
V_, W_ = C * K, N * C * K
ALU = AluOpType
ACT = ActivationFunctionType
F32, BF, I32, U16 = "float32", "bfloat16", "int32", "uint16"

SCRATCH = {
    "Xb": ("sbuf", [128, W_], BF), "Xk": ("sbuf", [128, W_], F32), "Bb": ("sbuf", [128, V_], BF),
    "Li": ("sbuf", [128, NS], I32), "Lf": ("sbuf", [128, NS], F32),
    "Si": ("sbuf", [128, V_], I32), "S16": ("sbuf", [128, V_], U16), "Sf": ("sbuf", [128, V_], F32),
    "Pi": ("sbuf", [128, 40], I32), "Qi": ("sbuf", [128, 40], I32),
    "P16": ("sbuf", [128, 40], U16), "Q16": ("sbuf", [128, 40], U16),
    "thi": ("sbuf", [128, 1], I32), "mgi": ("sbuf", [128, 1], I32), "mgf": ("sbuf", [128, 1], F32),
    "thp": ("sbuf", [128, 2], I32), "Dh": ("sbuf", [128, 256], BF), "Dl": ("sbuf", [128, RO * 128], BF), "cn": ("sbuf", [128, 2 * K], BF),
    "thf": ("sbuf", [128, 4], F32), "mgr": ("sbuf", [128, K], F32),
    "YS": ("sbuf", [128, 2 * 1280], F32), "YV": ("sbuf", [128, 1280], F32), "R": ("sbuf", [128, RO * 1280], F32),
    "D0c": ("sbuf", [128, 1280], BF),
    "far": ("sbuf", [128, RO * 2560], BF), "ab": ("sbuf", [128, 3 * 2560], BF),
    "sb": ("sbuf", [128, RO * K], BF), "land": ("sbuf", [128, RO * K], BF),
    "Tf": ("sbuf", [128, 2 * K], F32), "O16": ("sbuf", [128, 2 * K], U16),
    "mi": ("sbuf", [128, K], I32), "xx": ("sbuf", [128, K], BF), "uu": ("sbuf", [128, K], BF),
    "x1a": ("sbuf", [128, K], BF), "x1": ("sbuf", [128, K], BF),
    "sg": ("sbuf", [128, RO * K], BF), "acc": ("sbuf", [128, 8], F32),
    "cnt": ("sbuf", [128, 6 * RO], F32), "Lj": ("sbuf", [128, 10], I32), "L16": ("sbuf", [128, 10], U16),
    "hi": ("sbuf", [128, K], I32), "hr": ("sbuf", [128, K], I32), "sel": ("sbuf", [128, K], F32),
    "dl": ("sbuf", [128, K], F32), "dv": ("sbuf", [128, K], F32),
    "sa": ("sbuf", [128, RO * K], F32), "sa2": ("sbuf", [128, K], F32), "sz": ("sbuf", [128, RO * K], I32),
    "one": ("sbuf", [128, 144], F32), "Iw": ("sbuf", [128, 144], F32), "W0": ("sbuf", [128, 144], F32), "W1": ("sbuf", [128, 144], F32),
    "Ip": ("sbuf", [128, 128], BF), "In": ("sbuf", [128, 128], BF),
    "P25": ("sbuf", [128, 128], BF), "N25": ("sbuf", [128, 128], BF), "Inf": ("sbuf", [128, 128], F32),
    "B1": ("sbuf", [128, 128], F32), "B2": ("sbuf", [128, 128], F32), "Bp": ("sbuf", [128, 128], BF), "Bn": ("sbuf", [128, 128], BF),
    "Z": ("sbuf", [128, 144], BF),
    "Gt": ("sbuf", [128, 128], F32), "ef": ("sbuf", [128, 2 * K], F32), "X4": ("sbuf", [128, W_], BF), "X5": ("sbuf", [128, W_], BF),
    "rlo": ("sbuf", [128, 512], BF), "rhi": ("sbuf", [128, 128], BF), "r1": ("sbuf", [128, 416], BF), "cr": ("sbuf", [128, 16 * 128], BF),
    "Z2": ("sbuf", [128, 144], BF), "Zn": ("sbuf", [128, 144], BF), "rep": ("sbuf", [128, 16 * 800], BF),
    "c2": ("sbuf", [128, RO * K], F32),
    "pi": ("sbuf", [128, 1], I32), "pm": ("sbuf", [128, 1], I32), "pc": ("sbuf", [128, 4], F32),
    "jm": ("sbuf", [128, 176], F32), "dg": ("sbuf", [128, 176], F32),
    "PD0": ("psum", [128, 512], F32), "PD1": ("psum", [128, 512], F32), "PDI": ("psum", [128, 512], F32), "PS": ("psum", [128, 512], F32),
    "PE": ("psum", [128, 512], F32), "PK": ("psum", [128, 512], F32), "PL": ("psum", [128, 512], F32), "PV": ("psum", [128, 512], F32),
}
NDMA = 56
SEMAPHORES = ["cV", "cS", "cT", "cG", "sent"] + ["arr%d" % t for t in range(RO)] + [w + str(k) for w in ("fa", "fb") for k in range(8)] + ["d%d" % i for i in range(NDMA)]

KEY0 = 61440 - (1 << 24)
FIX, DLAT, DBW, CALL, MARGIN = 60.0, 1400.0, 300.0, 1100.0, 1.25
TIMES = [(0.83, 1.56, 3.8, 0.42, 210.0, 160.0, 800.0), (1.18, 1.98, 4.6, 0.6, 220.0, 150.0, 900.0), (1.15, 1.55, 4.2, 0.7, 200.0, 120.0, 2500.0)]
YCH = [[(0, 24), (24, 52), (52, 104), (104, 160)]] * 4 + [[(0, 40), (40, 100), (100, 160)]] * 2
SELF = [24] * 4 + [0] * 2
FARV = [((0, 36, "S"), (36, 74, "S"), (74, 112, "S"), (112, 136, "V"), (136, 160, "F")),
        ((0, 48, "S"), (48, 96, "S"), (96, 144, "F"), (144, 160, "W")),
        ((0, 16, "W"), (16, 64, "F"), (64, 112, "S"), (112, 160, "S")),
        ((0, 32, "S"), (32, 64, "S"), (64, 112, "F"), (112, 160, "F")),
        ((0, 44, "S"), (44, 88, "S"), (88, 124, "r"), (124, 160, "r")),
        ((0, 36, "r"), (36, 72, "r"), (72, 116, "S"), (116, 160, "S"))]
FOLDS = [(0, 136, 160, -1), (1, 96, 160, 1), (2, 0, 64, 2), (3, 64, 160, 3)]
TURN = ()
ROWS, MEAN, FREE, GAP, TRIP, BUSY, EARLY = 8, 0, 0, -400.0, 2500.0, 0.0, 0.0
REPS = [(0,), (1, 2), (3,), (4, 5)]
CUTS = {}
LAG = [0, 1, 2, 4]
KEYQ = "SVSVSSDD"
BCH = [(0, 1024), (1024, 2048), (2048, 2560), (2560, 3072), (3072, 3488), (3488, 3840)]
LEFT = [50000.0, 42500.0, 35000.0, 28000.0, 21000.0, 11000.0, 1500.0, 0.0]
DUE = {"far%d%s" % (t, e): LEFT[t + 1] for t in range(C) for e in "SVrFW"}
DUE.update({"dist%d%s" % (t, e): LEFT[t + 2] for t in range(C) for e in "prFW"})
DUE.update({"src%d" % t: LEFT[t + 3] for t in range(C)})
DUE.update({"rep%d" % t: LEFT[min(t, C - 1)] for t in (0, 1, 3, 4)})
DUE.update({"far3" + e: 19000.0 for e in "SVFW"})
DUE.update({"dist2" + e: 19000.0 for e in "pFW"})
DUE.update({"dist3" + e: 10000.0 for e in "pFW"})
DUE["src2"] = 1500.0
REACH, WEIGHT = (1, 8, 30, 120), (1.2, 1.0, 1.0)
SHIFTS, PACK, SWAPS, SEED, SLACK, RUN = 800, 1, 15000, 2, 100.0, 256
KEPT = {}


def neighbour(core, T, topo):
    return [c for c in topo.cores_of(core) if c not in T.cores and topo.die(c) == topo.die(core)][0]


def folded(k, A):
    t, l0, l1, at = FOLDS[k]
    return A("far", 2560 * t + 16 * l0, 2560 * t + 16 * l1), A("ab", 2560 * (t % 3) + 16 * l0, 2560 * (t % 3) + 16 * l1)


def plan(T, g, topo, core, rank):
    ops, tag = [], [None]
    mate = neighbour(core, T, topo)
    size = {"float32": 4, "bfloat16": 2, "int32": 4, "uint16": 2}

    def A(name, a=None, b=None, step=1, parts=128, p0=0):
        n = SCRATCH[name][1][1]
        a = 0 if a is None else a
        b = n if b is None else b
        t = T[name]
        ap = t[p0:parts, a:b] if step == 1 else t[p0:parts, a:b:step]
        return {"ap": ap, "buf": name, "lo": a, "hi": b, "n": len(range(a, b, step)), "ps": SCRATCH[name][0] == "psum",
                "w": size[SCRATCH[name][2]], "x": []}

    def IND(win, off):
        return {"ap": win["ap"].indirect(off["ap"]), "buf": win["buf"], "lo": win["lo"], "hi": win["hi"], "n": 16 * off["n"],
                "ps": False, "w": win["w"], "x": [off], "ind": True}

    def add(eng, fn, cost, rd, wr, kind="c", lat=0.0):
        r, w = [], []
        for a in rd:
            if isinstance(a, dict):
                r.append(a); r.extend(a["x"])
        for a in wr:
            w.append(a); r.extend(a["x"])
        ops.append({"eng": eng, "fn": fn, "cost": cost, "rd": r, "wr": w, "kind": kind, "grp": None, "lat": lat, "id": len(ops), "after": None, "tag": tag[0]})
        return ops[-1]

    def val(s):
        return s["ap"] if isinstance(s, dict) else s

    def vcost(out, ins, two=False):
        n = out["n"]
        if out.get("ind"): return (0, FIX, 0, n, 0)
        if any(a.get("ind") for a in ins): return (0, FIX, n, 0, 0)
        if two: r = 1.0 if any(a["ps"] for a in ins) else 2.0
        else: r = 0.5 if all(a["w"] == 2 for a in ins + [out]) else 1.0
        return (0, 20 + max(64.0, n * r), 0, 0, 0)

    def tc(out, in_):
        return add("V", lambda: g.vector.tensor_copy(out["ap"], in_["ap"]), vcost(out, [in_]), [in_], [out])

    def tt(out, a, b, op):
        return add("V", lambda: g.vector.tensor_tensor(out["ap"], a["ap"], b["ap"], op), vcost(out, [a, b], True), [a, b], [out])

    def ts(out, a, s1, op0, s2=None, op1=None):
        if op1 is None: fn = lambda: g.vector.tensor_scalar(out["ap"], a["ap"], val(s1), None, op0)
        else: fn = lambda: g.vector.tensor_scalar(out["ap"], a["ap"], val(s1), val(s2), op0, op1)
        return add("V", fn, vcost(out, [a]), [a, s1, s2], [out])

    def ms(out, c):
        return add("V", lambda: g.vector.memset(out["ap"], c), (0, max(64.0, out["n"] * out["w"] / 4.0), 0, 0, 0), [], [out])

    def scan(out, d0, d1):
        return add("V", lambda: g.vector.tensor_tensor_scan(out["ap"], d0["ap"], d1["ap"], 0.0, ALU.add, ALU.min), (0, 20 + max(64, out["n"]), 0, 0, 0), [d0, d1], [out])

    def act(out, in_, func, bias=0.0, scale=1.0, accum=None):
        if accum is None: fn = lambda: g.scalar.activation(out["ap"], in_["ap"], func, bias=val(bias), scale=val(scale))
        else: fn = lambda: g.scalar.activation(out["ap"], in_["ap"], func, bias=val(bias), scale=scale, accum_out=accum["ap"])
        cost = (0, 78, out["n"], 0, 0) if in_.get("ind") else (0, 78 + out["n"], 0, 0, 0)
        return add("S", fn, cost, [in_, bias, scale], [out] + ([accum] if accum else []))

    def run(items, grp=None):
        def fn():
            for out, l, r, st, sp in items: ins = g.tensor.matmul(out["ap"], l["ap"], r["ap"], st, sp)
            return ins
        cyc = sum(max(64, r["n"]) * (4 if r["w"] == 4 else 1) for out, l, r, st, sp in items)
        op = add("T", fn, (0, 0, 0, 0, cyc), [a for it in items for a in it[1:3]], [it[0] for it in items])
        op["grp"], op["shut"] = grp, items[-1][4]
        return op

    def runs(items, grp=None):
        part = []
        for it in items:
            part.append(it)
            if sum(max(64, x[2]["n"]) for x in part) >= RUN and (grp or it[4]):
                run(part, grp)
                part = []
        if part: run(part, grp)

    def terms(out, pairs, st=True, sp=True):
        return [(out, pairs[i][0], pairs[i][1], st and i == 0, sp and i == len(pairs) - 1) for i in range(len(pairs))]

    def mm(out, pairs):
        return run(terms(out, pairs))

    def iota(out, pat, base, cm):
        if SCRATCH[out["buf"]][2] == I32: fn = lambda: g.iota(out["ap"], pat, base, cm)
        else: fn = lambda: g.iota(out["ap"], pat, base, cm, allow_small_or_imprecise_dtypes=True)
        return add("G", fn, (0, 157 + 2 * out["n"], 0, 0, 0), [], [out])

    def asel(out, in_, pat, base, cm, op):
        return add("G", lambda: g.affine_select(out["ap"], in_["ap"], pat, op, 0.0, base, cm), (0, MARGIN * (205 + 2 * out["n"]), 0, 0, 0), [in_], [out])

    def dma(q, out, in_):
        e = g.sync if q == "Y" else g.scalar
        sb = out if isinstance(out, dict) else in_
        nb = sb["n"] * sb["w"] * 128
        return add(q, lambda: e.dma_start(val(out), val(in_)), (60, 0, 0, 0, 0), [in_], [out] if isinstance(out, dict) else [], kind="d", lat=DLAT + nb / DBW)

    dma("Y", A("Pi"), T.grant[:])
    loads = [(A("Li"), T.favor[:])] + [(A("Xb", a, b), T.base[:, a:b]) for a, b in BCH]
    loads += [(A("Si", 0, K), T.src[:, 0:K]), (A("Bb"), T.base[:, 0:V_]), (A("Si", K, V_), T.src[:, K:V_])]
    before = 0.0
    for out, src in ((A("mgi", parts=8), T.mg[:]), (A("Qi"), T.part[:]), (A("thi"), T.th[:])):
        dma("S", out, src)
    prev = ops[0]
    for out, src in loads:
        op = dma("Y", out, src)
        op["after"] = prev
        prev = op
        op["lat"] += before
        before += out["n"] * out["w"] * 128 / DBW

    ms(A("one"), 1.0)
    asel(A("Iw"), A("one"), [[-1, 144]], 8, 1, ALU.is_equal)
    ms(A("rlo", parts=64), 0.0)
    iota(A("rlo", 0, K, parts=1), [[1, K]], 0, 0)
    iota(A("pi"), [[0, 1]], 0, 1)
    asel(A("B1"), A("one", 0, 128), [[-16, 8], [0, 16]], 0, 1, ALU.is_ge)
    asel(A("B2"), A("B1"), [[16, 8], [0, 16]], 15, -1, ALU.is_ge)
    iota(A("jm"), [[0, 11], [1, 16]], 0, 0)
    for c in range(RO - C): iota(A("ef", c * K, c * K + K), [[1, K]], 4096 + c * K, 0)
    for a in range(K, 512, K):
        b = min(a + K, 512)
        ms(A("rlo", a, b, parts=33, p0=32), float(a))
        tc(A("rlo", a, b, parts=1), A("rlo", 0, b - a, parts=1))
    ms(A("rhi", parts=64), 2.0 ** -16)
    ms(A("r1", parts=1), 1.0)
    crv = [1.0, -491520.0] + [4096.0 + c * K for c in range(C)] + [-2.0 ** 33, 2.0 ** -16, -255.0]
    crv += [((1 + t % (N - 1)) * V_ + (t % C) * K - 4096) / 65536.0 for t in range(RO - 1)] + [(a - 4096) / 65536.0 for a, b in BCH[-2:]]
    for j in range(len(crv)):
        if j < ROWS: act(A("cr", j * 128, (j + 1) * 128, parts=1), A("one", 0, 128, parts=1), ACT.Identity, scale=crv[j])
        else: ms(A("cr", j * 128, (j + 1) * 128, parts=1), crv[j])
    CR = lambda j: A("cr", j * 128, (j + 1) * 128, parts=1)
    Id = A("Iw", 8, 136)
    for nm, s in (("Ip", 1.0), ("In", -1.0), ("P25", 2.0 ** 25), ("N25", -2.0 ** 25), ("Inf", -1.0)):
        act(A(nm), Id, ACT.Identity, scale=s)
    ts(A("pm"), A("pi"), 15, ALU.bitwise_and)
    tc(A("pc", 0, 1), A("pm"))
    if TURN:
        iota(A("Lj"), [[16, 10]], 0, 0)
        ts(A("L16"), A("Lj"), A("pc", 0, 1), ALU.add)
    ts(A("pc", 1, 2), A("pm"), 8.0, ALU.is_lt)
    ts(A("pc", 2, 3), A("pm"), 8.0, ALU.is_ge)
    ts(A("pc", 3, 4), A("pm"), -1.0, ALU.mult, 2041.03125, ALU.add)
    ts(A("W0"), A("Iw"), A("pc", 1, 2), ALU.mult)
    ts(A("W1"), A("Iw"), A("pc", 2, 3), ALU.mult)
    for nm, s in (("Bp", 8192.0), ("Bn", -8192.0)):
        act(A(nm), A("B2"), ACT.Identity, scale=s)
    ms(A("Z"), 0.0)
    ts(A("Z", 15, 128, 16), A("B2", 0, 128, 16), 8192.0, ALU.mult)
    act(A("Z2"), A("Z"), ACT.Identity, scale=2.0)
    act(A("Zn"), A("Z"), ACT.Identity, scale=-1.0)
    mm(A("PS", 0, 128, parts=8), [(A("Iw", 8, 136, 16), A("B2"))])
    act(A("Gt", parts=8), A("PS", 0, 128, parts=8), ACT.Identity, scale=-8192.0)
    ts(A("dg"), A("jm"), A("pc", 0, 1), ALU.not_equal, 1e9, ALU.mult)
    nd0 = 8 * max(b - a for ch in YCH for a, b in ch)
    ms(A("D0c", 0, nd0), -0.0625)
    ms(A("D0c", 0, nd0, 8), 1024.0)
    ms(A("cnt", 0, 1), 80.0 - 15.5)
    LO = A("rlo", 0, K, parts=1)
    R1 = A("r1", 0, K, parts=1)

    tc(A("P16"), A("Pi"))

    def lists(t):
        c, u = t % C, (t % 2) * K
        off = A("P16", 10 * c, 10 * c + 10)
        if t == 0: tc(A("Tf", u, u + K), IND(A("Li"), off))
        else: act(A("Tf", u, u + K), IND(A("Lf"), off), ACT.Identity)
        ev, od = A("Tf", u, u + K, 2), A("Tf", u + 1, u + K, 2)
        low, high = A("PL", 352, 432), A("PV", 176, 256) if t else A("PL", 432, 512)
        mm(low, [(A("W0", 8, 136), ev), (A("W0", 0, 128), od)])
        mm(high, [(A("W1", 16, 144), ev), (A("W1", 8, 136), od)])
        tc(A("O16", u, u + 80), low)
        tc(A("O16", u + 80, u + K), high)

    banks = ["PD0", "PD1", "PDI", "PE", "PK", "PV", "PS", "PL"]
    cuts = list(range(0, BCH[-1][0], 512)) + list(BCH[-1])
    step = {}

    def chain(name, op):
        op["after"], step[name] = step.get(name), op

    for j in range(8):
        a, b = cuts[j], cuts[j + 1]
        ramp, ones = [(A("rhi", parts=33), A("rlo", 0, b - a, parts=33))], A("r1", 0, b - a, parts=1) if KEYQ[j] == "D" else None
        if ones: chain("T", mm(A(banks[j], 0, b - a), ramp + [(CR(8), ones), (CR(8 + j), ones)]))
        else: chain("T", run(terms(A(banks[j], 0, b - a), ramp, sp=False), ("key", j)))
    lists(0)
    for op in ops[-5:]: chain(op["eng"], op)
    for j in range(8):
        a, b = cuts[j], cuts[j + 1]
        ps = A(banks[j], 0, b - a)
        if KEYQ[j] == "D":
            chain("V", tt(A("Xk", a, b), A("Xb", a, b), ps, ALU.add))
            continue
        chain("T", run(terms(ps, [(A("Ip"), A("Xb", a, b))], st=False), ("key", j)))
        if KEYQ[j] == "S": chain("S", act(A("Xk", a, b), ps, ACT.Identity, bias=(KEY0 + a) / 65536.0))
        else: chain("V", ts(A("Xk", a, b), ps, (KEY0 + a) / 65536.0, ALU.add))
    tc(A("Q16"), A("Qi"))
    for j in range(2): tc(A("Lf", 512 * j, 512 * j + 512), A("Li", 512 * j, 512 * j + 512))
    for c in range(C): tc(A("S16", c * K, c * K + K), A("Si", c * K, c * K + K))
    ts(A("thp", 0, 1), A("thi"), 63, ALU.bitwise_and)
    ts(A("thp", 1, 2), A("thi"), 6, ALU.arith_shift_right)
    tc(A("thf", 0, 2), A("thp"))
    ts(A("thf", 2, 3), A("thp", 1, 2), -64.0, ALU.add)
    ts(A("thf", 3, 4), A("thp", 0, 1), 15.5, ALU.add)
    for w in range(2): ts(A("Dh", 128 * w, 128 * w + 128), A("Ip"), A("thf", 2 - w, 3 - w), ALU.mult)
    ts(A("Dl", 0, 128), A("Ip"), A("thf", 0, 1), ALU.mult)
    ms(A("cn", 0, K), -8192.0)
    ms(A("cn", K, 2 * K), -8192.0 * 64)
    tc(A("mgf", parts=8), A("mgi", parts=8))
    act(A("mgr", parts=8), A("cn", 0, K, parts=8), ACT.Identity, bias=A("mgf", parts=8), scale=0.0)

    def told(t):
        return (1 + t % (N - 1)) * V_ + (t % C) * K

    def landing(t):
        return A("X%d" % (t + 1), told(t), told(t) + K) if C <= t + 1 < RO else A("land", t * K, t * K + K)

    def standing():
        for t in range(C):
            a, b = told(t) + K, told(t + 1) if t < C - 1 else W_
            op = dma("Y", A("X4", a, b), T.base[:, a:b])
            op["rd"].append(landing(0))
            op["lat"] += 600.0 * t
            chain("Y", op)
        for a, b in ((960, 1440), (1600, 2240), (2400, 3040), (3360, 3840)):
            chain("Y", dma("Y", T.yx[:, a:b], A("Xb", a, b)))

    last = {}

    def paired(t):
        mine = [x for x in FARV[t] if x[2] in "arFW"] or [(K, K, "")]
        return mine[0][0], mine[-1][1], mine[0][2]

    def repeated(t, l0, l1):
        r0 = 16 * (sum(paired(j)[1] - paired(j)[0] for j in range(t)) - paired(t)[0])
        return A("rep", r0 + 16 * l0, r0 + 16 * l1)

    def repeat(ts_):
        t, u = ts_[0], ts_[-1]
        a, b, tag[0] = (t % C) * K + paired(t)[0], (u % C) * K + paired(u)[1], "rep%d" % t
        old, r0 = A("sb" if t >= C else "Bb" if t else "Xb", a, b), repeated(t, paired(t)[0], K)["lo"]
        for a2, b2, e in CUTS.get(t, [(a, b, "G")]):
            old, tag[0] = A(old["buf"] if a2 == a else "Bb", a2, b2), "rep%d" % (t if a2 == a else a2)
            for p in range(16 if a < b else 0):
                out = A("rep", r0 + 16 * (a2 - a) + p, r0 + 16 * (b2 - a), 16)
                if e == "G": asel(out, old, [[0, b2 - a2]], 0, 0, ALU.is_ge)
                else: tc(out, old)

    def far_gather(t):
        o = (t % C) * K
        for l0, l1, e in FARV[t]:
            tag[0] = "far%d%s" % (t, e)
            out, src = A("far", 2560 * t + 16 * l0, 2560 * t + 16 * l1), IND(A("Xb" if t < C else "X%d" % t), A("S16", o + l0, o + l1))
            if e in "SF": act(out, src, ACT.Identity)
            elif e in "VW": tc(out, src)
            else:
                tt(out, src, repeated(t, l0, l1), ALU.subtract)

    def folds(t, early):
        for k in range(len(FOLDS)):
            if FOLDS[k][3] != t - early or (early and t): continue
            tag[0] = "fold%d" % k
            far, most = folded(k, A)
            old = repeated(*FOLDS[k][:3])

            def fold(k=k, far=far, old=old):
                rid, pid, _ = topo.addr(mate)
                move = RemoteDMATransfer(dst_ids=[DstId(rid=rid, pnc=pid)], dma_engine_mask=topo.mask(core, mate), remote_sem=T.sem["fa%d" % k],
                                         srcs=[far["ap"], old["ap"]], dsts=[far["ap"]], alu_op=2)
                return g.remote_dma_fused([move], local_sem=T.sem.sent)
            op = add("G", fold, (CALL + (1900 if k == 0 else 0), 0, 0, 0, 0), [far, old], [most], kind="r", lat=TRIP + 3.5 * far["n"])
            op["semn"], op["out"], op["in"], op["back"] = "fb%d" % k, len(topo.engines(core, mate)), len(topo.engines(mate, core)), (mate, far, most)
            op["gap"] = 2.0 * far["n"] + (GAP if k else -600.0)
            chain("send", op)

    nch = [0]

    def lapse(t, l0=0, l1=K):
        return A("PDI", (t % 3) * K + l0, (t % 3) * K + l1) if t < C else A("PK", 2 * K + l0, 2 * K + l1)

    def distances(t, old):
        w = 128 * (t >= C)
        a, b = (0, paired(t)[0]) if paired(t)[0] else (paired(t)[1], K)
        cut = [a, b] if b - a <= 102 else [a, (a + b) // 2, b]
        segs = [(cut[j], cut[j + 1], "p") for j in range(len(cut) - 1) if a < b]
        rs = [paired(t)] if paired(t)[2] else []
        for l0, l1, e in (segs + rs if t < C else rs + segs):
            tag[0] = "dist%d%s" % (t, e)
            gid, f0, a0, n = (t, l0), 2560 * t + 16 * l0, 2560 * (t % 3) + 16 * l0, l1 - l0
            di = lapse(t, l0, l1)
            den = [(A("Dh", w, w + 128), A("cn", K, K + n)), (A("Dl", 128 * t, 128 * t + 128), A("cn", 0, n))]
            if t < C: den += [(A("P25"), A("sg", t * K + l0, t * K + l1))]
            if e in "FW":
                pairs = [(A("Zn", 15 - p, 143 - p), A("far", f0 + p, f0 + 16 * n, 16)) for p in range(16)] + [(A("Bn"), A(old[0], old[1] + l0, old[1] + l1))]
                more = [(A("Z2", 15 - p, 143 - p), A("ab", a0 + p, a0 + 16 * n, 16)) for p in range(16)]
                runs(terms(di, pairs + more + den), gid)
            elif e in "ar":
                pairs = []
                if e == "r":
                    for m0, m1, e2 in FARV[t]:
                        if e2 == "r": ts(A("ab", a0 + 16 * (m0 - l0), a0 + 16 * (m1 - l0)), A("far", f0 + 16 * (m0 - l0), f0 + 16 * (m1 - l0)), 0.0, ALU.max)
                    pairs = [(A("Zn", 15 - p, 143 - p), A("far", f0 + p, f0 + 16 * n, 16)) for p in range(16)]
                else:
                    act(A("ab", a0, a0 + 16 * n), A("far", f0, f0 + 16 * n), ACT.Abs)
                more = [(A("Z2" if e == "r" else "Z", 15 - p, 143 - p), A("ab", a0 + p, a0 + 16 * n, 16)) for p in range(16)]
                runs(terms(di, pairs + more + den if t < C else pairs + den + more), gid)
            else:
                nb = -(-16 // (512 // n))
                for j in range(nb):
                    p0, p1 = 16 * j // nb, 16 * (j + 1) // nb
                    bank = "PD%d" % (nch[0] % 2)
                    nch[0] += 1
                    items = []
                    for p in range(p0, p1):
                        items += terms(A(bank, n * (p - p0), n * (p - p0 + 1)),
                                       [(A("In"), A(old[0], old[1] + l0, old[1] + l1)), (A("Ip"), A("far", f0 + p, f0 + 16 * n, 16))])
                    runs(items)
                    act(A("ab", a0 + n * p0, a0 + n * p1), A(bank, 0, n * (p1 - p0)), ACT.Abs)
                    pairs = [(A("Z", 15 - p, 143 - p), A("ab", a0 + n * p, a0 + n * p + n)) for p in range(p0, p1)]
                    if t >= C: runs(terms(di, (den if p0 == 0 else []) + pairs, p0 == 0, p1 == 16), gid)
                    else: runs(terms(di, pairs + (den if p1 == 16 else []), p0 == 0, p1 == 16), gid)

    def keys(t, own, n0, n1):
        ps = A("PK", 0, K)
        mm(ps, [(CR(7), LO), (A("Ip"), own)])
        act(A("Xk", n0, n0 + K), ps, ACT.Identity, bias=(KEY0 + n0) / 65536.0)
        ps = A("PK", K, 2 * K)
        mm(ps, [(CR(8), R1), (CR(9 + t), R1), (CR(7), LO)])
        tt(A("Xk", n1, n1 + K), landing(t), ps, ALU.add)

    def sources(t):
        c = t % C
        o, q = c * K, (t % 3) * K
        be, xf, Rk = A("Bb", o, o + K), A("sb", t * K, t * K + K), A("R", 1280 * t + 7, 1280 * t + 1280, 8)
        sa, sz, di = A("sa", t * K, t * K + K), A("sz", t * K, t * K + K), lapse(t)
        if t < C:
            G2 = A("PS", 0, K)
            distances(t, ("Bb", o))
            tag[0] = "src%d" % t
            mm(G2, [(A("P25"), xf), (A("N25"), be), (CR(0), LO), (CR(2 + c), R1)])
            tt(sa, di, A("Si", o, o + K), ALU.max)
            tt(G2, sa, G2, ALU.min)
        else:
            G2, G3, tag[0] = A("PS", 2 * K, 3 * K), A("PS", K, 2 * K), "src%d" % t
            tt(A("x1"), A("x1a"), A("PV", 0, K), ALU.min)
            mm(G2, [(A("P25"), A("xx")), (A("N25"), A("x1")), (CR(0), LO), (CR(2 + c), R1)])
            tt(sa, di, A("Si", o, o + K), ALU.max)
            tt(G2, sa, G2, ALU.min)
        act(A("c2", t * K, t * K + K), Rk, ACT.Identity, scale=65536.0)
        if t < C:
            tt(sz, A("c2", t * K, t * K + K), G2, ALU.max)
        else:
            tt(A("sa2"), A("c2", t * K, t * K + K), G2, ALU.max)
            mm(G3, [(CR(6), R1), (A("P25"), A("uu"))])
            tt(G3, A("ef", o, o + K), G3, ALU.min)
            tt(sz, A("sa2"), G3, ALU.max)
        ts(A("Si", o, o + K), sz, 4095, ALU.bitwise_and)
        if t + C < RO:
            tc(A("S16", o, o + K), A("Si", o, o + K))
        else:
            if t in TURN: act(A("Sf", o, o + K), IND(A("Si", o, o + K), A("L16")), ACT.Identity)
            else: tc(A("Sf", o, o + K), A("Si", o, o + K))
            dma("Y", T.ys[:, o:o + K], A("Sf", o, o + K))

    for ts_ in REPS:
        if ts_[0] < C: repeat(ts_)
    for t in range(RO):
        c = t % C
        o, f, d, u, q = c * K, c ^ 1, 1 + t % (N - 1), (t % 2) * K, (t % 3) * K
        ys0, r0 = 1280 * (t % 2), 1280 * t
        be, xf, ld = A("Bb", o, o + K), A("sb", t * K, t * K + K), landing(t)
        bP, E, Tf, mi, xx, uu = A("PV", 0, K), A("PE", 0, K), A("Tf", u, u + K), A("mi"), A("xx"), A("uu")
        prev, tag[0] = None, None
        for l0, l1 in YCH[t]:
            low, src = A("YS", ys0 + 8 * l0, ys0 + 8 * l1), IND(A("Xk"), A("O16", u + l0 // 2, u + l1 // 2))
            if l1 <= SELF[t]:
                ts(low, src, -0.5, ALU.add)
            else:
                op = act(low, src, ACT.Identity, bias=-0.5)
                op["after"] = prev
                prev = op
            tt(A("YV", 8 * l0, 8 * l1), IND(A("Xk"), A("O16", u + 80 + l0 // 2, u + 80 + l1 // 2)), A("YS", ys0 + 8 * l0, ys0 + 8 * l1), ALU.min)
            scan(A("R", r0 + 8 * l0, r0 + 8 * l1), A("D0c", 0, 8 * (l1 - l0)), A("YV", 8 * l0, 8 * l1))
        mm(bP, [(A("Ip"), be)])
        far_gather(t)
        folds(t, True)
        if t >= C: distances(t, ("sb", last[c] * K))
        tag[0] = None
        ts(mi, A("R", r0 + 7, r0 + 1280, 8), 255.502, ALU.add)
        if t < C:
            tt(xx, mi, bP, ALU.min)
        else:
            tt(A("PV", 336, 336 + K), mi, bP, ALU.min)
            tt(A("x1a"), lapse(t), A("sb", last[c] * K, last[c] * K + K), ALU.max)
            tt(xx, A("x1a"), A("PV", 336, 336 + K), ALU.min)
        pairs = [(A("Gt", parts=8), A("mgr", parts=8)), (A("Bp"), be)]
        if f in last:
            pairs += [(A("Bn"), A("Bb", f * K, f * K + K)), (A("Bp"), A("sb", last[f] * K, last[f] * K + K))]
        run(terms(E, pairs[:1], sp=False), ("E", t))
        run(terms(E, pairs[1:], st=False, sp=False), ("E", t))
        run(terms(E, [(A("Bn"), xx)], st=False), ("E", t))
        tt(uu, E, xx, ALU.max)
        tt(xf, uu, bP, ALU.min)

        def send(t=t, dst=T.cores[(rank + d) % N], xf=xf, ld=ld):
            rid, pid, _ = topo.addr(dst)
            return g.remote_dma(ld["ap"], xf["ap"], T.sem["arr%d" % t], T.sem.sent, pid, rid, topo.mask(core, dst))
        op = add("G", send, (CALL + (1300 if t == 0 and not FOLDS else 0), 0, 0, 0, 0), [xf], [ld], kind="r")
        op["semn"] = "arr%d" % t
        chain("send", op)
        folds(t, False)
        op["out"] = len(topo.engines(core, T.cores[(rank + d) % N]))
        op["in"] = len(topo.engines(T.cores[(rank - d) % N], core))
        tag[0] = "sel%d" % t
        mm(A("PL", 0, K), [(A("B2"), A("YS", ys0, ys0 + 1280, 8))])
        ts(A("hi"), A("PL", 0, K), A("pc", 3, 4), ALU.add, 4096.0, ALU.mult)
        ts(A("hr"), A("hi"), 15 * 4096, ALU.bitwise_and)
        tt(A("sel"), IND(A("Lf"), A("Q16", 10 * c, 10 * c + 10)), A("hr"), ALU.max)
        run(terms(A("PL", K, 2 * K), [(CR(1), R1), (A("Inf"), Tf)], sp=False), ("L", t))
        run(terms(A("PL", K, 2 * K), [(A("B2"), A("sel"))], st=False), ("L", t))
        tag[0] = None
        tt(A("dl"), E, A("dg", t, K + t), ALU.is_gt)
        tt(A("dv"), A("PL", K, 2 * K), A("dl"), ALU.mult)
        tt(IND(A("Lf"), A("P16", 10 * c, 10 * c + 10)), Tf, A("dv"), ALU.add)
        if t < RO - 1:
            lists(t + 1)
            keys(t, xf, o, d * V_ + o)
            tag[0] = "cnt%d" % t
            act(A("sg", t * K, t * K + K), uu, ACT.Sign, bias=-255.5, accum=A("acc", t, t + 1))
            cnt = [A("cnt", 5 * t + j, 5 * t + j + 1) for j in range(6)]
            act(cnt[1], A("acc", t, t + 1), ACT.Identity, bias=cnt[0], scale=0.5)
            if t < RO - 2: act(cnt[5], cnt[1], ACT.Identity, bias=80.0)
            act(cnt[2], cnt[1], ACT.Identity, bias=3.0 * 2 ** 27)
            act(cnt[3], cnt[2], ACT.Identity, bias=3.0 * 2 ** 27, scale=-1.0)
            ts(cnt[4], cnt[1], cnt[3], ALU.add, A("thf", 3, 4), ALU.add)
            ts(A("Dl", 128 * t + 128, 128 * t + 256), A("Ip"), cnt[4], ALU.mult)
        else:
            for j in range(2):
                dma("YS"[j], T.yl[:, 512 * j:512 * j + 512], A("Lf", 512 * j, 512 * j + 512))["lat"] += 512 * 512 / DBW
        for ts_ in REPS:
            if ts_[-1] == t + C: repeat(ts_)
        if t >= C: sources(t)
        for t2 in range(C):
            if LAG[t2] == t: sources(t2)
        tag[0] = None
        if t + C >= RO: dma("Y", T.yx[:, o:o + K], xf)
        dma("Y", T.yx[:, d * V_ + o:d * V_ + o + K], ld)
        if t < C - 1:
            chain("Y", dma("Y", A("Xb", o, o + K), xf))
            for win in ("Xb", "X4"): chain("Y", dma("Y", A(win, d * V_ + o, d * V_ + o + K), ld))
        if t == 0: standing()
        if t == C - 2: dma("Y", A("X4", 0, o + K), A("sb", 0, o + K))
        if t == C - 1:
            dma("Y", A("X4", o, o + K), xf)
            dma("Y", A("X5", K, told(C)), A("X4", K, told(C)))
            dma("Y", A("X5", told(C) + K, W_), A("X4", told(C) + K, W_))
        if t == C: dma("Y", A("X5", o, o + K), xf)
        last[c] = t
    return ops


def depend(ops):
    seen, held = {}, {}
    for op in ops:
        deps = {op["after"]["id"]: False} if op["after"] else {}
        touch = [(a, False) for a in op["rd"]] + [(a, True) for a in op["wr"]]
        if op["eng"] == "T" and op["wr"][0]["buf"] in ("PDI", "PE", "PK", "PL"):
            if op["wr"][0]["buf"] in held: deps[held[op["wr"][0]["buf"]]] = False
            held[op["wr"][0]["buf"]] = op["id"]
        for acc, write in touch:
            for o2, a2, w2 in seen.get(acc["buf"], []):
                if not ((write or w2) and acc["lo"] < a2["hi"] and a2["lo"] < acc["hi"]): continue
                if acc["buf"] == "rep" and write and w2: continue
                soft = op["eng"] == "T" and o2["eng"] == "T" and acc["ps"]
                deps[o2["id"]] = deps.get(o2["id"], False) or not soft
        op["deps"] = deps
        op["banks"] = sorted(set(a["buf"] for a, w in touch if a["ps"]))
        for acc, write in touch:
            seen.setdefault(acc["buf"], []).append((op, acc, write))


def tables(ops):
    anc, red = [], []
    for op in ops:
        a = 0
        for j in op["deps"]: a |= anc[j]
        red.append([j for j in op["deps"] if not (a >> j) & 1])
        for j in op["deps"]: a |= 1 << j
        anc.append(a)
    out = []
    for cyc, ga, sc, pe, hop, own, rem in TIMES + [[sum(x) / len(x) for x in zip(*TIMES)]] * MEAN:
        cost = [c[0] + cyc * (c[1] + ga * c[2] + sc * c[3]) + pe * c[4] for c in [op["cost"] for op in ops]]
        lat = [op["lat"] + (rem if op["kind"] == "r" else 0.0) for op in ops]
        pre = []
        for op in ops:
            row = []
            for j in red[op["id"]]:
                p = ops[j]
                row.append((j, lat[j] + (own if p["eng"] == op["eng"] and p["kind"] == "c" else hop) if op["deps"][j] else p.get("gap", 0.0)))
            pre.append(row)
        rest = list(lat)
        for i in reversed(range(len(ops))):
            for j, w in pre[i]: rest[j] = max(rest[j], w + cost[i] + rest[i])
        out.append((cost, lat, pre, hop, rest))
    return out


def play(ops, tab, seq, base=None, same=0, most=1e18):
    cost, lat, pre, hop, rest = tab
    n = len(cost)
    if base:
        marks = base[4][:same // 32 + 1]
        t1, why = list(base[1]), list(base[2])
    else:
        marks = [({e: n for e in "VSTGY"}, {b: {} for b in SCRATCH if SCRATCH[b][0] == "psum"}, 0.0, None)]
        t1, why = [0.0] * n + [-1e9], [None] * n
    front, bank, end, final = marks[-1]
    front, bank = dict(front), {b: dict(h) for b, h in bank.items()}
    for a in range(32 * len(marks) - 32, n, 32):
        for i in seq[a:a + 32]:
            e, t, banks = ops[i]["key"]
            y, j = None, front[e]
            if t1[j] > t: t, y = t1[j], j
            for b in banks:
                held = bank[b]
                for e2, j in held.items():
                    if e2 != e and t1[j] + hop > t: t, y = t1[j] + hop, j
                held[e] = i
            for j, w in pre[i]:
                if t1[j] + w >= t: t, y = t1[j] + w, -1 - j
            t += cost[i]
            if t + rest[i] > most: return 1e18, None
            t1[i], why[i], front[e] = t, y, i
            if t + lat[i] > end: end, final = t + lat[i], i
        marks.append((dict(front), {b: dict(h) for b, h in bank.items()}, end, final))
    return end, t1, why, final, marks


def clash(ops, seq):
    lock = {}
    for i in seq:
        op = ops[i]
        if op["eng"] != "T": continue
        for b in op["banks"]:
            if lock.get(b) not in (None, op["grp"]): return True
            lock[b] = None if op["shut"] else op["grp"]
    return False


def place(ops, first, cost, edges, hop, rank):
    busy = {e: [] for e in "VSTGY"}
    bank = {b: [] for b in SCRATCH if SCRATCH[b][0] == "psum"}
    t1 = [0.0] * len(cost)
    for i in rank:
        t0, c, e, banks = first[i], cost[i], ops[i]["eng"], ops[i]["banks"]
        for j, w in edges[i]:
            if t1[j] + w > t0: t0 = t1[j] + w
        lst = busy[e]
        moved = True
        while moved:
            pos = n = len(lst)
            while pos and lst[pos - 1][1] > t0: pos -= 1
            while pos < n and t0 + c > lst[pos][0]:
                if lst[pos][1] > t0: t0 = lst[pos][1]
                pos += 1
            moved = False
            for b in banks:
                held = bank[b]
                k = len(held)
                while k and held[k - 1][0] > t0 - 1500.0:
                    k -= 1
                    s2, f2, e2 = held[k]
                    if e2 != e and t0 < f2 + hop and s2 < t0 + c + hop: t0, moved = f2 + hop, True
        lst.insert(pos, (t0, t0 + c))
        for b in banks:
            held = bank[b]
            k = len(held)
            while k and held[k - 1][0] > t0: k -= 1
            held.insert(k, (t0, t0 + c, e))
        t1[i] = t0 + c
    return t1


def order(ops):
    if "seq" not in KEPT:
        n = len(ops)
        for op in ops:
            op["first"] = 9000.0 if op.get("low") else 0.0
            op["key"] = (op["eng"], op["first"], op["banks"])
        tabs = tables(ops)
        cost, lat, pre, hop, rest = tabs.pop() if MEAN else tabs[0]
        suc = [[] for op in ops]
        for i in range(n):
            for j, w in pre[i]: suc[j].append((i, w))

        def urge(due):
            way = [cost[i] + max(lat[i], due.get(ops[i]["tag"], 0.0)) for i in range(n)]
            for i in reversed(range(n)):
                for j, w in pre[i]: way[j] = max(way[j], cost[j] + w + way[i])
            return [-x for x in way]

        def judge(seq, m=0, most=1e18, base=None):
            same = 0
            while base and same < n and seq[same] == base[1][same]: same += 1
            got = {m: play(ops, tabs[m], seq, base and base[3][m], same, most)}
            if got[m][0] > most or clash(ops, seq): return 1e18, seq
            for j in range(len(tabs)):
                if j != m: got[j] = play(ops, tabs[j], seq, base and base[3][j], same)
            ends = [got[j][0] for j in range(len(tabs))]
            return sum(WEIGHT[j] * ends[j] + EARLY * sum(got[j][1][:n]) / n for j in range(len(ends))), seq, ends, got

        def pack(pr):
            t1 = place(ops, [op["first"] for op in ops], cost, pre, hop, sorted(range(n), key=lambda x: (pr[x], x)))
            return t1, sorted(range(n), key=lambda x: (t1[x] - cost[x], x))

        def repack(pr):
            t1 = pack(pr)[0]
            back = place(ops, lat, cost, suc, hop, sorted(range(n), key=lambda x: (-t1[x], -x)))
            return [-x for x in back]

        due, z = {a: b * (1.25 if MEAN else 1.0) for a, b in DUE.items()}, SEED
        tags = sorted(set(op["tag"] for op in ops if op["tag"]))
        best = judge(pack(urge(due))[1])
        for it in range(SHIFTS):
            z = (z * 6364136223846793005 + 1442695040888963407) % (1 << 64)
            tg = tags[(z >> 33) % len(tags)]
            pr = urge(due)
            was = max(due.get(tg, 0.0), min(-pr[i] - cost[i] for i in range(n) if ops[i]["tag"] == tg))
            new = dict(due)
            new[tg] = was + ((z >> 13) % 2001 - 900) / 1000.0 * (500.0, 2000.0, 6000.0)[(z >> 28) % 3]
            cur = judge(pack(urge(new))[1])
            if cur[0] <= best[0]: best, due = cur, new
        KEPT["due"], KEPT["log"] = due, [int(best[0] / 3)]
        now, busy = best, [i for i in range(n) if ops[i]["eng"] in "VS"]
        for it in range(SWAPS):
            z = (z * 6364136223846793005 + 1442695040888963407) % (1 << 64)
            m = (z >> 50) % len(tabs)
            seq, (end, t1, why, i, marks) = now[1], now[3][m]
            pairs = []
            while why[i] is not None:
                j = why[i]
                if j >= 0 and t1[j] > 0: pairs.append((j, i))
                i = j if j >= 0 else -1 - j
            if not pairs: continue
            a, b = pairs[(z >> 20) % len(pairs)]
            if (z >> 56) % 8 < FREE: a = b = busy[(z >> 21) % len(busy)]
            pr = [0.0] * n
            for pos in range(n): pr[seq[pos]] = float(pos)
            early, far = (z >> 10) & 1, (z >> 12) % REACH[(z >> 44) % len(REACH)]
            x = b if early else a
            pr[x] = pr[a] - 0.5 - far if early else pr[b] + 0.5 + far
            todo = [x]
            while todo:
                x = todo.pop()
                for j, w in (pre[x] if early else suc[x]):
                    if early and pr[j] >= pr[x]:
                        pr[j] = pr[x] - 1e-4
                        todo.append(j)
                    elif not early and pr[j] <= pr[x]:
                        pr[j] = pr[x] + 1e-4
                        todo.append(j)
            how = (z >> 40) % 32
            slack = SLACK * (1.0 - it / SWAPS)
            if how >= PACK: cur = judge(sorted(seq, key=lambda x: pr[x]), m, now[2][m] + slack, now)
            else: cur = judge(pack(repack(pr) if how == 0 else pr)[1], m, now[2][m] + slack)
            if cur[0] <= now[0] + slack:
                if (z >> 24) % 4 == 0:
                    t1, c1 = cur[3][m][1], tabs[m][0]
                    again = judge(sorted(cur[1], key=lambda x: t1[x] - c1[x]))
                    if again[0] <= cur[0]: cur = again
                now = cur
                if now[0] < best[0]: best = now
        KEPT["seq"], KEPT["ends"] = best[1], best[2]
    return [ops[i] for i in KEPT["seq"]]


def emit(seq, ops, g, T):
    q = {"V": g.vector, "S": g.scalar, "T": g.tensor, "G": g, "Y": g.sync}
    rankq, bank = {}, {}
    for op in seq:
        op["sig"] = op["kind"] != "c"
        rankq[op["eng"]] = rankq.get(op["eng"], 0) + 1
        op["pos"] = rankq[op["eng"]]
        for b in op["banks"]:
            for e2, j in bank.get(b, {}).items():
                if e2 != op["eng"]: op["deps"][j] = True
            bank.setdefault(b, {})[op["eng"]] = op["id"]
    for op in seq:
        best = {}
        op["need"] = []
        for j, hard in op["deps"].items():
            p = ops[j]
            if not hard: continue
            if p["kind"] != "c": op["need"].append(p)
            elif p["eng"] not in best or best[p["eng"]]["pos"] < p["pos"]: best[p["eng"]] = p
        op["need"].extend(best.values())
    upto = {}
    for op in seq:
        keep = []
        for p in op["need"]:
            key = (op["eng"], p["eng"] if p["kind"] == "c" else p["id"])
            if upto.get(key, 0) >= p["pos"]: continue
            upto[key] = p["pos"]
            p["sig"] = True
            keep.append(p)
        op["need"] = keep
    cnt, nd, sent, ends = {}, 0, 0, []
    for op in seq:
        if op["kind"] == "c":
            if op["sig"]: cnt[op["eng"]] = cnt.get(op["eng"], 0) + 1
            op["sem"], op["val"] = T.sem["c" + op["eng"]], cnt.get(op["eng"], 0)
        elif op["kind"] == "d":
            op["sem"], op["val"] = T.sem["d%d" % nd], 16
            nd += 1
            ends.append(op)
        else:
            op["sem"], op["val"] = T.sem[op["semn"]], op["in"]
            sent += op["out"]
    for op in seq:
        e = q[op["eng"]]
        for p in op["need"]: e.wait_ge(p["sem"], p["val"])
        ins = op["fn"]()
        if op["kind"] == "d": ins.then_inc(op["sem"], 16)
        elif op["kind"] == "c" and op["sig"]: ins.then_inc(op["sem"], 1)
    g.wait_ge(T.sem.sent, sent)
    for op in ends:
        if not op["wr"]: q[op["eng"]].wait_ge(op["sem"], 16)


def hand_back(g, core, owner, T, topo):
    rid, pid, _ = topo.addr(owner)
    for k in range(len(FOLDS)):
        far, most = folded(k, lambda name, a, b: T[name][:, a:b])
        g.wait_ge(T.sem["fa%d" % k], len(topo.engines(owner, core)))
        g.remote_dma(most, far, T.sem["fb%d" % k], T.sem.sent, pid, rid, topo.mask(core, owner))
    if FOLDS: g.wait_ge(T.sem.sent, len(FOLDS) * len(topo.engines(core, owner)))


def rank_program(g, core, T, topo):
    rank = T.rank_of(core)
    if rank is None:
        for owner in T.cores:
            if neighbour(owner, T, topo) == core: hand_back(g, core, owner, T, topo)
        return
    ops = plan(T, g, topo, core, rank)
    depend(ops)
    emit(order(ops), ops, g, T)
